import numpy as np
import ml_dtypes


def mxq(x, axis, fmt="e4m3"):
    dtype, down = {"e4m3": (ml_dtypes.float8_e4m3fn, 7), "e5m2": (ml_dtypes.float8_e5m2, 14)}[fmt]
    v = np.moveaxis(np.asarray(x, np.float32).astype(ml_dtypes.bfloat16).astype(np.float64), axis, -1)
    blocks = v.reshape(v.shape[:-1] + (-1, 32))
    amax = np.abs(blocks).max(-1, keepdims=True)
    byte = np.maximum(np.where(amax > 0, np.frexp(amax)[1] - 1 + 127, 0) - down, 1)
    scale = np.exp2(byte - 127.0)
    codes = (blocks / scale).astype(np.float32).astype(dtype).astype(np.float64)
    return np.moveaxis((codes * scale).reshape(v.shape), -1, axis)


WIDE = False


def mx_kscale(k):
    if not WIDE:
        return np.ones(k)
    levels = np.array([10, -10, 5, -5, 0])
    if k % 512:
        return np.exp2(np.random.permutation(np.resize(levels, k // 32))).repeat(32)
    a = np.empty((k // 512, 16))
    for p in range(k // 512):
        a[p, :8] = np.random.permutation(np.resize(levels, 8))
        for g in range(8):
            far = levels[np.abs(levels - a[p, g]) >= 10]
            a[p, g + 8] = far[np.random.randint(len(far))]
    return np.exp2(a.ravel()).repeat(32)


def f64(x):
    return np.asarray(x).astype(np.float64)


def striped(idx):
    return np.tile(idx.reshape(-1, 16).T, (8, 1)).astype(np.uint16)


def unstriped(offs):
    return offs[:16].T.reshape(-1).astype(np.int64)


E2M1 = np.array([0.0, 0.5, 1.0, 1.5, 2.0, 3.0, 4.0, 6.0, -0.0, -0.5, -1.0, -1.5, -2.0, -3.0, -4.0, -6.0])


def pack_weight(w, fmt):
    k, n = w.shape
    w = f64(np.asarray(w, np.float32).astype(ml_dtypes.bfloat16)).reshape(k // 32, 32, n)
    amax = np.abs(w).max(1)
    if fmt == "e4m3":
        byte = np.frexp(amax)[1] - 1 + 127 - 7
    else:
        mant, ex = np.frexp(amax / 6.0)
        byte = np.where(mant > 0.5, ex, ex - 1) + 127
    byte = np.clip(np.where(amax > 0, byte, 1), 1, 254)
    scaled = (w * np.exp2(127.0 - byte)[:, None, :]).reshape(k, n).astype(np.float32)
    by_word = np.ascontiguousarray(scaled.reshape(k // 512, 128, 4, n).transpose(0, 1, 3, 2))
    if fmt == "e4m3":
        words = by_word.astype(ml_dtypes.float8_e4m3fn).view(np.uint8)
    else:
        c = by_word.astype(ml_dtypes.float4_e2m1fn).view(np.uint8) & 0xF
        words = (c[..., 0::2] | (c[..., 1::2] << 4)).reshape(k // 512, 128, 2 * n)
    return np.ascontiguousarray(words), np.ascontiguousarray(byte.astype(np.uint8).reshape(k // 512, 16, n))


def unpack_weight(words, scales, fmt):
    g, _, n = scales.shape
    words = np.ascontiguousarray(words).reshape(g, 128, n, -1)
    if fmt == "e4m3":
        vals = words.view(ml_dtypes.float8_e4m3fn).astype(np.float64)
    else:
        nib = np.empty((g, 128, n, 4), np.uint8)
        nib[..., 0::2] = words & 0xF
        nib[..., 1::2] = words >> 4
        vals = E2M1[nib]
    vals = vals * np.repeat(np.exp2(scales.astype(np.float64) - 127.0), 8, axis=1)[..., None]
    return vals.transpose(0, 1, 3, 2).reshape(g * 512, n)


def gelu(v):
    return 0.5 * v * (1.0 + np.tanh(np.sqrt(2.0 / np.pi) * (v + 0.044715 * v**3)))


def pack_table4(v):
    words, scales = pack_weight(v, "e2m1")
    g, t = words.shape[0] // 2, v.shape[1]
    words = words.reshape(g, 2, 128, t, 2).transpose(0, 2, 3, 1, 4)
    return np.concatenate([words.reshape(g, -1), scales.reshape(g, -1)], axis=1)


def unpack_table4(tab):
    g, t = tab.shape[0], tab.shape[1] // 544
    words = tab[:, :512 * t].reshape(g, 128, t, 2, 2).transpose(0, 3, 1, 2, 4).reshape(2 * g, 128, 2 * t)
    return unpack_weight(words, tab[:, 512 * t:].reshape(2 * g, 16, t), "e2m1")


K, T, S, H, N = 1024, 2048, 1024, 1024, 256

def setup_inputs():
    n = np.random.standard_normal
    s = mx_kscale(K)[:, None]
    u = mx_kscale(H)[:, None]
    tab = pack_table4(n((K, T)) * s)
    offs = striped(np.random.permutation(T)[:S])
    we = (n((K, H)) / np.sqrt(K) / s * u.T).astype(np.float32)
    wi_words, wi_scales = pack_weight(n((K, H)) / np.sqrt(K) / s, "e2m1")
    wo_words, wo_scales = pack_weight(n((H, N)) / np.sqrt(H) / u, "e4m3")
    bo = (0.5 * n(N)).astype(np.float32)
    return {"tab": tab, "offs": offs, "we": we,
            "wi_words": wi_words, "wi_scales": wi_scales,
            "wo_words": wo_words, "wo_scales": wo_scales, "bo": bo}

def reference(tab, offs, we, wi_words, wi_scales, wo_words, wo_scales, bo):
    v = unpack_table4(tab)[:, unstriped(offs)]
    weq = mxq(f64(we), 0, "e4m3")
    wi = unpack_weight(wi_words, wi_scales, "e2m1")
    wo = unpack_weight(wo_words, wo_scales, "e4m3")
    e = weq.T @ v
    i = wi.T @ v
    h = e / (1.0 + np.abs(i))
    hq = mxq(h, 0, "e4m3")
    y = wo.T @ hq
    return y + f64(bo)[:, None]

@@ -1,0 +1,327 @@
+from contextlib import ExitStack
+
+import concourse.mybir as mybir
+
+K, T, S, H, N = 1024, 2048, 1024, 1024, 256
+FLOPS = 2 * K * H * S * 2 + 2 * H * N * S
+
+F32 = mybir.dt.float32
+BF16 = mybir.dt.bfloat16
+I32 = mybir.dt.int32
+U32 = mybir.dt.uint32
+U16 = mybir.dt.uint16
+U8 = mybir.dt.uint8
+FP8X4 = mybir.dt.float8_e4m3fn_x4
+FP4X4 = mybir.dt.float4_e2m1fn_x4
+ACT = mybir.ActivationFunctionType
+MULT = mybir.AluOpType.mult
+
+P = 128
+JW = 256
+NJ = S // JW
+SLICES = [(0, 256), (256, 256), (512, 512)]
+SCALAR_SQUARES = (0, 1, 2, 3, 4, 7)
+
+
+def tile_list_saccade_divisive_inhibition_kernel(
+    tc, tab, offs, we, wi_words, wi_scales, wo_words, wo_scales, bo, out
+):
+    nc = tc.nc
+    with ExitStack() as ctx:
+        keep = ctx.enter_context(tc.tile_pool(name="keep", bufs=1))
+        work = ctx.enter_context(tc.tile_pool(name="work", bufs=2))
+        psum_i = ctx.enter_context(tc.psum_pool(name="psum_i", bufs=3))
+        psum_e = ctx.enter_context(tc.psum_pool(name="psum_e", bufs=3))
+        psum_y = ctx.enter_context(tc.psum_pool(name="psum_y", bufs=2))
+
+        offsets = keep.tile([P, S // 16], U16, name="offsets")
+        tab_words = keep.tile([P, T], I32, name="tab_words", align_bytes=64)
+        tab_planes = keep.tile([P, 2 * T], U8, name="tab_planes", tag="shared_a", align_bytes=64)
+        wi_area = keep.tile([P, 5 * H], U8, name="wi_area", align_bytes=64)
+        wi_planes_raw = wi_area[:, 1536:3584]
+        warm = keep.tile([P, 1], F32, name="warm", tag="shared_c")
+        warm_out = keep.tile([P, 1], F32, name="warm_out", tag="shared_d", align_bytes=64)
+        wi_raw = {}
+        we_raw = {}
+
+        def load_wi(b, tag):
+            raw = keep.tile([P, 2, 256], I32, name="wi_raw%d" % b, tag=tag, align_bytes=64)
+            nc.sync.dma_start(
+                raw[:], wi_words[:, :, 1024 * b : 1024 * (b + 1)].rearrange("a p x -> p a x").bitcast(I32)
+            )
+            wi_raw[b] = raw
+
+        def load_plane(engine, plane, rows, quad):
+            engine.dma_start(
+                plane[32 * quad : 32 * quad + 4, :].bitcast(I32).rearrange("p (a x) -> p a x", a=2),
+                rows[4 * quad : 4 * quad + 4, :, :],
+            )
+
+        nc.vector.memset(tab_planes[:].bitcast(I32), 0)
+        nc.gpsimd.memset(wi_planes_raw.bitcast(I32), 0)
+        nc.vector.memset(warm[:], 1.0)
+
+        nc.sync.dma_start(offsets[:], offs)
+        nc.sync.dma_start(tab_words[:], tab[0, 0 : 512 * T].rearrange("(p x) -> p x", p=P).bitcast(I32))
+        load_wi(0, "shared_e")
+        tab_rows = tab[0, 512 * T : 544 * T].rearrange("(a q t) -> q a t", a=2, q=16).bitcast(I32)
+        for quad in range(4):
+            load_plane(nc.scalar if quad < 2 else nc.sync, tab_planes, tab_rows, quad)
+        wi_rows = wi_scales.rearrange("a q c -> q a c").bitcast(I32)
+        for quad in range(4):
+            load_plane(nc.sync if quad < 2 else nc.gpsimd, wi_planes_raw, wi_rows, quad)
+        nc.scalar.activation(warm_out[:], warm[:], ACT.Abs_reciprocal_sqrt)
+
+        we_all = keep.tile([P, 4 * 2048], F32, name="we_all", tag="shared_c")
+
+        def load_we(b, a):
+            raw = we_all[:, 2048 * (2 * b + a) : 2048 * (2 * b + a + 1)].rearrange("p (i c) -> p i c", i=4)
+            nc.sync.dma_start(
+                raw, we[512 * a : 512 * (a + 1), 512 * b : 512 * (b + 1)].rearrange("(p i) c -> p i c", i=4)
+            )
+            we_raw[b, a] = raw
+
+        load_wi(1, "shared_d")
+        load_we(0, 0)
+        load_we(0, 1)
+        load_we(1, 0)
+        load_we(1, 1)
+        late = {}
+
+        def load_read_out():
+            wo_codes = work.tile([P, 2, N], I32, name="wo_codes", tag="we_bf", align_bytes=64)
+            wo_planes = work.tile([P, 2 * N], U8, name="wo_planes", tag="we_bf", align_bytes=64)
+            bias = keep.tile([P, 2], F32, name="bias", tag="shared_c")
+            nc.sync.dma_start(wo_codes[:], wo_words.rearrange("a p c i -> p a (c i)").bitcast(I32))
+            nc.vector.memset(wo_planes[:].bitcast(I32), 0)
+            wo_rows = wo_scales.rearrange("a q c -> q a c").bitcast(I32)
+            for quad in range(4):
+                load_plane(nc.sync, wo_planes, wo_rows, quad)
+            with nc.allow_non_contiguous_dma(reason="one bias value a partition"):
+                nc.sync.dma_start(bias[:], bo.rearrange("(c p) -> p c", p=P))
+            late["codes"] = wo_codes
+            late["planes"] = wo_planes
+            late["bias"] = bias
+
+        v_codes = {}
+        v_planes = {}
+        pairs = {}
+        held = {}
+
+        def gather_scales(s):
+            j0, n = SLICES[s]
+            if s == 0:
+                held["first"] = keep.tile([P, 2 * n], U8, name="v_planes_first", align_bytes=64)
+            if s == 1:
+                held["rest"] = keep.tile([P, 2 * (S - j0)], U8, name="v_planes_rest", tag="shared_d", align_bytes=64)
+            for a in range(2):
+                o = n * a if s == 0 else 2 * (j0 - JW) + n * a
+                plane = held["first" if s == 0 else "rest"][:, o : o + n]
+                nc.vector.tensor_copy(plane, tab_planes[:, T * a : T * (a + 1)].indirect(offsets[:, j0 // 16 : (j0 + n) // 16]))
+                v_planes[s, a] = plane
+
+        def gather_words(s):
+            j0, n = SLICES[s]
+            both = keep.tile([P, n], U32, name="v_pairs%d" % s, tag="shared_e" if s else "v_pairs0", align_bytes=64)
+            nc.vector.tensor_copy(both[:], tab_words[:].bitcast(U32).indirect(offsets[:, j0 // 16 : (j0 + n) // 16]))
+            pairs[s] = both
+
+        def part_words(s):
+            n = SLICES[s][1]
+            codes = keep.tile([P, 2, 2 * n], U8, name="v_codes%d" % s, align_bytes=64)
+            nc.vector.tensor_copy(
+                codes[:].bitcast(U16), pairs[s][:].bitcast(U16).rearrange("p (j a) -> p a j", a=2)
+            )
+            v_codes[s] = codes
+
+        def v_operand(a, j0, n):
+            s = max(x for x in range(len(SLICES)) if SLICES[x][0] <= j0)
+            o = j0 - SLICES[s][0]
+            return v_codes[s][:, a, 2 * o : 2 * (o + n)].bitcast(FP4X4), v_planes[s, a][:, o : o + n]
+
+        wi_codes = {}
+        wi_planes = {}
+
+        def order_wi_scales(b):
+            plane = keep.tile([P, 2, 512], U8, name="wi_plane%d" % b, align_bytes=64)
+            nc.vector.tensor_copy(
+                plane[:].rearrange("p a (t m) -> p a t m", t=4),
+                wi_planes_raw.rearrange("p (a b m t) -> p b a t m", a=2, b=2, t=4)[:, b, :, :, :],
+            )
+            wi_planes[b] = plane
+
+        def order_wi_words(b):
+            codes = wi_area[:, 3072 * b : 3072 * b + 2048]
+            nc.vector.tensor_copy(
+                codes.bitcast(U16).rearrange("p (a t m) -> p a t m", a=2, t=4),
+                wi_raw[b][:].bitcast(U16).rearrange("p a (m t) -> p a t m", t=4),
+            )
+            wi_codes[b] = codes
+
+        we_bf = {}
+        we_codes = {}
+        we_planes = {}
+
+        def round_we(b, a):
+            grouped = work.tile([P, 2048], BF16, name="we_bf", tag="we_bf", align_bytes=64)
+            nc.vector.tensor_copy(
+                grouped[:].rearrange("p (t m i) -> p m i t", t=4, i=4),
+                we_raw[b, a].rearrange("p i (m t) -> p m i t", t=4),
+            )
+            we_bf[b, a] = grouped
+
+        def quantize_we(b, a):
+            codes = keep.tile([P, 512], U32, name="we_codes%d%d" % (b, a), align_bytes=64)
+            plane = keep.tile([P, 512], U8, name="we_plane%d%d" % (b, a), align_bytes=64)
+            nc.vector.quantize_mx(codes[:].bitcast(FP8X4), plane[:], we_bf[b, a][:])
+            we_codes[b, a] = codes
+            we_planes[b, a] = plane
+
+        gain = {}
+
+        def inhibit(u):
+            jh, b = divmod(u, 2)
+            mag = work.tile([P, 2, 2 * JW], F32, name="mag")
+            for tp in range(2):
+                bank = psum_i.tile([P, 2, JW], F32, name="bank_i")
+                for t2 in range(2):
+                    t = 2 * tp + t2
+                    for a in range(2):
+                        rhs, rhs_scale = v_operand(a, JW * jh, JW)
+                        nc.tensor.matmul_mx(
+                            out=bank[:, t2, :],
+                            lhsT=wi_codes[b][:, 1024 * a + 256 * t : 1024 * a + 256 * (t + 1)].bitcast(FP4X4),
+                            lhsT_scale=wi_planes[b][:, a, 128 * t : 128 * (t + 1)],
+                            rhs=rhs,
+                            rhs_scale=rhs_scale,
+                            start=(a == 0),
+                            stop=(a == 1),
+                        )
+                nc.scalar.activation(
+                    mag[:, tp, :].rearrange("p (j t) -> p j t", t=2), bank[:].rearrange("p t j -> p j t"), ACT.Abs
+                )
+            root = keep.tile([P, 4 * JW], F32, name="root%d" % u)
+            nc.scalar.activation(root[:], mag[:].rearrange("p a x -> p (a x)"), ACT.Abs_reciprocal_sqrt, bias=1.0)
+            gain[u] = root
+
+        def square(u):
+            sq = keep.tile([P, 4 * JW], F32, name="gain%d" % u)
+            if u in SCALAR_SQUARES:
+                nc.scalar.activation(sq[:], gain[u][:], ACT.Square)
+            else:
+                nc.vector.tensor_tensor(sq[:], gain[u][:], gain[u][:], MULT)
+            gain[u] = sq
+
+        h_bf = {}
+        h_codes = {}
+        h_planes = {}
+
+        def excite(u):
+            jh, b = divmod(u, 2)
+            h = work.tile([P, 4 * JW], BF16, name="h_bf", bufs=3, align_bytes=64)
+            g = gain[u][:].rearrange("p (tp j t) -> p j tp t", tp=2, t=2)
+            for jc in range(JW // 128):
+                bank = psum_e.tile([P, 4, 128], F32, name="bank_e")
+                for t in range(4):
+                    for a in range(2):
+                        rhs, rhs_scale = v_operand(a, JW * jh + 128 * jc, 128)
+                        nc.tensor.matmul_mx(
+                            out=bank[:, t, :],
+                            lhsT=we_codes[b, a][:, 128 * t : 128 * (t + 1)].bitcast(FP8X4),
+                            lhsT_scale=we_planes[b, a][:, 128 * t : 128 * (t + 1)],
+                            rhs=rhs,
+                            rhs_scale=rhs_scale,
+                            start=(a == 0),
+                            stop=(a == 1),
+                        )
+                nc.vector.tensor_tensor(
+                    h[:, 512 * jc : 512 * (jc + 1)].rearrange("p (j tp t) -> p j tp t", tp=2, t=2),
+                    bank[:].rearrange("p (tp t) j -> p j tp t", tp=2),
+                    g[:, 128 * jc : 128 * (jc + 1), :, :],
+                    MULT,
+                )
+            h_bf[u] = h
+
+        def quantize_h(u):
+            codes = keep.tile([P, JW], U32, name="h_codes%d" % u, align_bytes=64)
+            plane = keep.tile([P, JW], U8, name="h_plane%d" % u, align_bytes=64)
+            nc.vector.quantize_mx(codes[:].bitcast(FP8X4), plane[:], h_bf[u][:])
+            h_codes[u] = codes
+            h_planes[u] = plane
+
+        def read_out(jh):
+            bank = psum_y.tile([P, 2, JW], F32, name="bank_y")
+            result = work.tile([P, 2, JW], F32, name="result")
+            for c in range(2):
+                for b in range(2):
+                    nc.tensor.matmul_mx(
+                        out=bank[:, c, :],
+                        lhsT=late["codes"][:, b, 128 * c : 128 * (c + 1)].bitcast(FP8X4),
+                        lhsT_scale=late["planes"][:, N * b + 128 * c : N * b + 128 * (c + 1)],
+                        rhs=h_codes[2 * jh + b][:].bitcast(FP8X4),
+                        rhs_scale=h_planes[2 * jh + b][:],
+                        start=(b == 0),
+                        stop=(b == 1),
+                    )
+            for c in range(2):
+                nc.scalar.activation(result[:, c, :], bank[:, c, :], ACT.Identity, bias=late["bias"][:, c : c + 1])
+            nc.sync.dma_start(out[:, JW * jh : JW * (jh + 1)].rearrange("(c p) j -> p c j", p=P), result[:])
+
+        gather_scales(0)
+        gather_words(0)
+        order_wi_scales(0)
+        part_words(0)
+        order_wi_words(0)
+        inhibit(0)
+        square(0)
+        order_wi_scales(1)
+        order_wi_words(1)
+        inhibit(1)
+        square(1)
+        gather_words(1)
+        gather_scales(1)
+        part_words(1)
+        inhibit(2)
+        square(2)
+        gather_words(2)
+        gather_scales(2)
+        part_words(2)
+        round_we(0, 0)
+        round_we(0, 1)
+        quantize_we(0, 0)
+        quantize_we(0, 1)
+        inhibit(3)
+        square(3)
+        round_we(1, 0)
+        round_we(1, 1)
+        quantize_we(1, 0)
+        quantize_we(1, 1)
+        load_read_out()
+        excite(0)
+        inhibit(4)
+        excite(1)
+        quantize_h(0)
+        square(4)
+        excite(2)
+        quantize_h(1)
+        read_out(0)
+        inhibit(5)
+        excite(3)
+        quantize_h(2)
+        excite(4)
+        quantize_h(3)
+        read_out(1)
+        square(5)
+        inhibit(6)
+        quantize_h(4)
+        excite(5)
+        inhibit(7)
+        square(6)
+        quantize_h(5)
+        read_out(2)
+        square(7)
+        excite(6)
+        excite(7)
+        quantize_h(6)
+        quantize_h(7)
+        read_out(3)

@@ -30,9 +30,8 @@ def tile_list_saccade_divisive_inhibition_kernel(
     with ExitStack() as ctx:
         keep = ctx.enter_context(tc.tile_pool(name="keep", bufs=1))
         work = ctx.enter_context(tc.tile_pool(name="work", bufs=2))
-        psum_i = ctx.enter_context(tc.psum_pool(name="psum_i", bufs=3))
-        psum_e = ctx.enter_context(tc.psum_pool(name="psum_e", bufs=3))
-        psum_y = ctx.enter_context(tc.psum_pool(name="psum_y", bufs=2))
+        psum_i = ctx.enter_context(tc.psum_pool(name="psum_i", bufs=4))
+        psum_e = ctx.enter_context(tc.psum_pool(name="psum_e", bufs=4))
 
         offsets = keep.tile([P, S // 16], U16, name="offsets")
         tab_words = keep.tile([P, T], I32, name="tab_words", align_bytes=64)
@@ -165,8 +164,8 @@ def tile_list_saccade_divisive_inhibition_kernel(
         def round_we(b, a):
             grouped = work.tile([P, 2048], BF16, name="we_bf", tag="we_bf", align_bytes=64)
             nc.vector.tensor_copy(
-                grouped[:].rearrange("p (t m i) -> p m i t", t=4, i=4),
-                we_raw[b, a].rearrange("p i (m t) -> p m i t", t=4),
+                grouped[:].rearrange("p (t m i) -> p m t i", t=4, i=4),
+                we_raw[b, a].rearrange("p i (m t) -> p m t i", t=4),
             )
             we_bf[b, a] = grouped
 
@@ -181,9 +180,9 @@ def tile_list_saccade_divisive_inhibition_kernel(
 
         def inhibit(u):
             jh, b = divmod(u, 2)
-            mag = work.tile([P, 2, 2 * JW], F32, name="mag")
+            mag = keep.tile([P, 2, 2 * JW], F32, name="mag%d" % u)
             for tp in range(2):
-                bank = psum_i.tile([P, 2, JW], F32, name="bank_i")
+                bank = psum_i.tile([P, 2, JW], F32, name="bank_i", tag="bank_i")
                 for t2 in range(2):
                     t = 2 * tp + t2
                     for a in range(2):
@@ -200,11 +199,12 @@ def tile_list_saccade_divisive_inhibition_kernel(
                 nc.scalar.activation(
                     mag[:, tp, :].rearrange("p (j t) -> p j t", t=2), bank[:].rearrange("p t j -> p j t"), ACT.Abs
                 )
-            root = keep.tile([P, 4 * JW], F32, name="root%d" % u)
-            nc.scalar.activation(root[:], mag[:].rearrange("p a x -> p (a x)"), ACT.Abs_reciprocal_sqrt, bias=1.0)
-            gain[u] = root
+            gain[u] = mag
 
-        def square(u):
+        def make_gain(u):
+            root = work.tile([P, 4 * JW], F32, name="root", bufs=3)
+            nc.scalar.activation(root[:], gain[u][:].rearrange("p a x -> p (a x)"), ACT.Abs_reciprocal_sqrt, bias=1.0)
+            gain[u] = root
             sq = keep.tile([P, 4 * JW], F32, name="gain%d" % u)
             if u in SCALAR_SQUARES:
                 nc.scalar.activation(sq[:], gain[u][:], ACT.Square)
@@ -250,12 +250,12 @@ def tile_list_saccade_divisive_inhibition_kernel(
             h_planes[u] = plane
 
         def read_out(jh):
-            bank = psum_y.tile([P, 2, JW], F32, name="bank_y")
-            result = work.tile([P, 2, JW], F32, name="result")
             for c in range(2):
+                bank = psum_i.tile([P, JW], F32, name="bank_y", tag="bank_i")
+                result = work.tile([P, JW], F32, name="result", bufs=4)
                 for b in range(2):
                     nc.tensor.matmul_mx(
-                        out=bank[:, c, :],
+                        out=bank[:],
                         lhsT=late["codes"][:, b, 128 * c : 128 * (c + 1)].bitcast(FP8X4),
                         lhsT_scale=late["planes"][:, N * b + 128 * c : N * b + 128 * (c + 1)],
                         rhs=h_codes[2 * jh + b][:].bitcast(FP8X4),
@@ -263,9 +263,11 @@ def tile_list_saccade_divisive_inhibition_kernel(
                         start=(b == 0),
                         stop=(b == 1),
                     )
-            for c in range(2):
-                nc.scalar.activation(result[:, c, :], bank[:, c, :], ACT.Identity, bias=late["bias"][:, c : c + 1])
-            nc.sync.dma_start(out[:, JW * jh : JW * (jh + 1)].rearrange("(c p) j -> p c j", p=P), result[:])
+                if jh == NJ - 1 and c == 1:
+                    nc.vector.tensor_scalar_add(result[:], bank[:], late["bias"][:, c : c + 1])
+                else:
+                    nc.scalar.activation(result[:], bank[:], ACT.Identity, bias=late["bias"][:, c : c + 1])
+                nc.sync.dma_start(out[P * c : P * (c + 1), JW * jh : JW * (jh + 1)], result[:])
 
         gather_scales(0)
         gather_words(0)
@@ -273,53 +275,53 @@ def tile_list_saccade_divisive_inhibition_kernel(
         part_words(0)
         order_wi_words(0)
         inhibit(0)
-        square(0)
         order_wi_scales(1)
         order_wi_words(1)
         inhibit(1)
-        square(1)
+        make_gain(0)
         gather_words(1)
         gather_scales(1)
         part_words(1)
         inhibit(2)
-        square(2)
+        inhibit(3)
+        make_gain(2)
         gather_words(2)
         gather_scales(2)
         part_words(2)
         round_we(0, 0)
         round_we(0, 1)
         quantize_we(0, 0)
+        inhibit(4)
+        inhibit(5)
         quantize_we(0, 1)
-        inhibit(3)
-        square(3)
+        make_gain(1)
         round_we(1, 0)
+        excite(0)
+        inhibit(6)
         round_we(1, 1)
         quantize_we(1, 0)
+        make_gain(3)
+        excite(2)
         quantize_we(1, 1)
         load_read_out()
-        excite(0)
-        inhibit(4)
-        excite(1)
+        inhibit(7)
         quantize_h(0)
-        square(4)
-        excite(2)
+        make_gain(4)
+        excite(1)
+        quantize_h(2)
+        excite(3)
         quantize_h(1)
         read_out(0)
-        inhibit(5)
-        excite(3)
-        quantize_h(2)
+        make_gain(5)
         excite(4)
         quantize_h(3)
         read_out(1)
-        square(5)
-        inhibit(6)
+        make_gain(6)
         quantize_h(4)
         excite(5)
-        inhibit(7)
-        square(6)
+        make_gain(7)
         quantize_h(5)
         read_out(2)
-        square(7)
         excite(6)
         excite(7)
         quantize_h(6)

@@ -20,7 +20,7 @@ P = 128
 JW = 256
 NJ = S // JW
 SLICES = [(0, 256), (256, 256), (512, 512)]
-SCALAR_SQUARES = (0, 1, 2, 3, 4, 7)
+SCALAR_SQUARES = (5, 7)
 
 
 def tile_list_saccade_divisive_inhibition_kernel(
@@ -74,22 +74,25 @@ def tile_list_saccade_divisive_inhibition_kernel(
         we_all = keep.tile([P, 4 * 2048], F32, name="we_all", tag="shared_c")
 
         def load_we(b, a):
-            raw = we_all[:, 2048 * (2 * b + a) : 2048 * (2 * b + a + 1)].rearrange("p (i c) -> p i c", i=4)
-            nc.sync.dma_start(
-                raw, we[512 * a : 512 * (a + 1), 512 * b : 512 * (b + 1)].rearrange("(p i) c -> p i c", i=4)
-            )
-            we_raw[b, a] = raw
+            parts = 2 if (b, a) == (0, 0) else 1
+            w = 512 // parts
+            for part in range(parts):
+                o = 2048 * (2 * b + a) + 4 * w * part
+                raw = we_all[:, o : o + 4 * w].rearrange("p (i c) -> p i c", i=4)
+                c0 = 512 * b + w * part
+                nc.sync.dma_start(raw, we[512 * a : 512 * (a + 1), c0 : c0 + w].rearrange("(p i) c -> p i c", i=4))
+                we_raw[b, a, part] = raw
 
-        load_wi(1, "shared_d")
         load_we(0, 0)
+        load_wi(1, "shared_d")
         load_we(0, 1)
         load_we(1, 0)
         load_we(1, 1)
         late = {}
 
         def load_read_out():
-            wo_codes = work.tile([P, 2, N], I32, name="wo_codes", tag="we_bf", align_bytes=64)
-            wo_planes = work.tile([P, 2 * N], U8, name="wo_planes", tag="we_bf", align_bytes=64)
+            wo_codes = work.tile([P, 2, N], I32, name="wo_codes", tag="we_bf", bufs=4, align_bytes=64)
+            wo_planes = work.tile([P, 2 * N], U8, name="wo_planes", tag="we_bf", bufs=4, align_bytes=64)
             bias = keep.tile([P, 2], F32, name="bias", tag="shared_c")
             nc.sync.dma_start(wo_codes[:], wo_words.rearrange("a p c i -> p a (c i)").bitcast(I32))
             nc.vector.memset(wo_planes[:].bitcast(I32), 0)
@@ -162,11 +165,16 @@ def tile_list_saccade_divisive_inhibition_kernel(
         we_planes = {}
 
         def round_we(b, a):
-            grouped = work.tile([P, 2048], BF16, name="we_bf", tag="we_bf", align_bytes=64)
-            nc.vector.tensor_copy(
-                grouped[:].rearrange("p (t m i) -> p m t i", t=4, i=4),
-                we_raw[b, a].rearrange("p i (m t) -> p m t i", t=4),
-            )
+            grouped = work.tile([P, 2048], BF16, name="we_bf", tag="we_bf", bufs=4, align_bytes=64)
+            parts = 2 if (b, a) == (0, 0) else 1
+            for part in range(parts):
+                m = 128 // parts
+                dst = grouped[:].rearrange("p (t m i) -> p m t i", t=4, i=4)[:, m * part : m * (part + 1), :, :]
+                src = we_raw[b, a, part].rearrange("p i (m t) -> p m t i", t=4)
+                if b == 0:
+                    nc.scalar.copy(dst, src)
+                else:
+                    nc.vector.tensor_copy(dst, src)
             we_bf[b, a] = grouped
 
         def quantize_we(b, a):
@@ -203,13 +211,20 @@ def tile_list_saccade_divisive_inhibition_kernel(
 
         def make_gain(u):
             root = work.tile([P, 4 * JW], F32, name="root", bufs=3)
-            nc.scalar.activation(root[:], gain[u][:].rearrange("p a x -> p (a x)"), ACT.Abs_reciprocal_sqrt, bias=1.0)
+            nc.scalar.activation(
+                root[:].rearrange("p (j tp t) -> p j tp t", tp=2, t=2),
+                gain[u][:].rearrange("p tp (j t) -> p j tp t", t=2),
+                ACT.Abs_reciprocal_sqrt,
+                bias=1.0,
+            )
             gain[u] = root
             sq = keep.tile([P, 4 * JW], F32, name="gain%d" % u)
             if u in SCALAR_SQUARES:
                 nc.scalar.activation(sq[:], gain[u][:], ACT.Square)
             else:
-                nc.vector.tensor_tensor(sq[:], gain[u][:], gain[u][:], MULT)
+                for half in range(2):
+                    cols = slice(512 * half, 512 * (half + 1))
+                    nc.gpsimd.tensor_tensor(sq[:, cols], root[:, cols], root[:, cols], MULT)
             gain[u] = sq
 
         h_bf = {}
@@ -219,7 +234,6 @@ def tile_list_saccade_divisive_inhibition_kernel(
         def excite(u):
             jh, b = divmod(u, 2)
             h = work.tile([P, 4 * JW], BF16, name="h_bf", bufs=3, align_bytes=64)
-            g = gain[u][:].rearrange("p (tp j t) -> p j tp t", tp=2, t=2)
             for jc in range(JW // 128):
                 bank = psum_e.tile([P, 4, 128], F32, name="bank_e")
                 for t in range(4):
@@ -235,9 +249,9 @@ def tile_list_saccade_divisive_inhibition_kernel(
                             stop=(a == 1),
                         )
                 nc.vector.tensor_tensor(
-                    h[:, 512 * jc : 512 * (jc + 1)].rearrange("p (j tp t) -> p j tp t", tp=2, t=2),
-                    bank[:].rearrange("p (tp t) j -> p j tp t", tp=2),
-                    g[:, 128 * jc : 128 * (jc + 1), :, :],
+                    h[:, 512 * jc : 512 * (jc + 1)].rearrange("p (j t) -> p j t", t=4),
+                    bank[:].rearrange("p t j -> p j t"),
+                    gain[u][:, 512 * jc : 512 * (jc + 1)].rearrange("p (j t) -> p j t", t=4),
                     MULT,
                 )
             h_bf[u] = h
@@ -263,7 +277,7 @@ def tile_list_saccade_divisive_inhibition_kernel(
                         start=(b == 0),
                         stop=(b == 1),
                     )
-                if jh == NJ - 1 and c == 1:
+                if c == 1:
                     nc.vector.tensor_scalar_add(result[:], bank[:], late["bias"][:, c : c + 1])
                 else:
                     nc.scalar.activation(result[:], bank[:], ACT.Identity, bias=late["bias"][:, c : c + 1])
@@ -274,6 +288,7 @@ def tile_list_saccade_divisive_inhibition_kernel(
         order_wi_scales(0)
         part_words(0)
         order_wi_words(0)
+        round_we(0, 0)
         inhibit(0)
         order_wi_scales(1)
         order_wi_words(1)
@@ -284,46 +299,45 @@ def tile_list_saccade_divisive_inhibition_kernel(
         part_words(1)
         inhibit(2)
         inhibit(3)
+        round_we(0, 1)
         make_gain(2)
         gather_words(2)
         gather_scales(2)
         part_words(2)
-        round_we(0, 0)
-        round_we(0, 1)
         quantize_we(0, 0)
-        inhibit(4)
-        inhibit(5)
-        quantize_we(0, 1)
-        make_gain(1)
         round_we(1, 0)
-        excite(0)
-        inhibit(6)
+        quantize_we(0, 1)
         round_we(1, 1)
+        inhibit(4)
+        make_gain(1)
+        excite(0)
+        inhibit(5)
         quantize_we(1, 0)
-        make_gain(3)
-        excite(2)
         quantize_we(1, 1)
         load_read_out()
-        inhibit(7)
+        make_gain(3)
+        excite(2)
         quantize_h(0)
         make_gain(4)
         excite(1)
         quantize_h(2)
+        inhibit(6)
+        make_gain(5)
         excite(3)
         quantize_h(1)
         read_out(0)
-        make_gain(5)
+        inhibit(7)
+        make_gain(6)
         excite(4)
         quantize_h(3)
         read_out(1)
-        make_gain(6)
+        make_gain(7)
         quantize_h(4)
         excite(5)
-        make_gain(7)
+        excite(6)
         quantize_h(5)
         read_out(2)
-        excite(6)
-        excite(7)
         quantize_h(6)
+        excite(7)
         quantize_h(7)
         read_out(3)

@@ -19,8 +19,8 @@ MULT = mybir.AluOpType.mult
 P = 128
 JW = 256
 NJ = S // JW
-SLICES = [(0, 256), (256, 256), (512, 512)]
-SCALAR_SQUARES = (5, 7)
+SLICES = [(0, 256), (256, 768)]
+VECTOR_SQUARES = ((1, 0), (3, 0), (4, 0), (5, 0), (6, 0), (7, 0))
 
 
 def tile_list_saccade_divisive_inhibition_kernel(
@@ -35,7 +35,8 @@ def tile_list_saccade_divisive_inhibition_kernel(
 
         offsets = keep.tile([P, S // 16], U16, name="offsets")
         tab_words = keep.tile([P, T], I32, name="tab_words", align_bytes=64)
-        tab_planes = keep.tile([P, 2 * T], U8, name="tab_planes", tag="shared_a", align_bytes=64)
+        tab_planes = keep.tile([P, T], U8, name="tab_planes", tag="shared_a", align_bytes=64)
+        second_plane = keep.tile([P, S], U8, name="v_plane_second", align_bytes=64)
         wi_area = keep.tile([P, 5 * H], U8, name="wi_area", align_bytes=64)
         wi_planes_raw = wi_area[:, 1536:3584]
         warm = keep.tile([P, 1], F32, name="warm", tag="shared_c")
@@ -56,38 +57,39 @@ def tile_list_saccade_divisive_inhibition_kernel(
                 rows[4 * quad : 4 * quad + 4, :, :],
             )
 
-        nc.vector.memset(tab_planes[:].bitcast(I32), 0)
-        nc.gpsimd.memset(wi_planes_raw.bitcast(I32), 0)
+        nc.gpsimd.memset(tab_planes[:].bitcast(I32), 0)
+        nc.vector.memset(wi_planes_raw.bitcast(I32), 0)
         nc.vector.memset(warm[:], 1.0)
+        nc.vector.memset(second_plane[96:P, :].bitcast(I32), 0)
 
         nc.sync.dma_start(offsets[:], offs)
         nc.sync.dma_start(tab_words[:], tab[0, 0 : 512 * T].rearrange("(p x) -> p x", p=P).bitcast(I32))
         load_wi(0, "shared_e")
-        tab_rows = tab[0, 512 * T : 544 * T].rearrange("(a q t) -> q a t", a=2, q=16).bitcast(I32)
+        tab_rows = tab[0, 512 * T : 544 * T].rearrange("(a q t) -> a q t", a=2, q=16).bitcast(I32)
         for quad in range(4):
-            load_plane(nc.scalar if quad < 2 else nc.sync, tab_planes, tab_rows, quad)
+            nc.scalar.dma_start(
+                tab_planes[32 * quad : 32 * quad + 8, :].bitcast(I32), tab_rows[:, 4 * quad : 4 * quad + 4, :]
+            )
         wi_rows = wi_scales.rearrange("a q c -> q a c").bitcast(I32)
         for quad in range(4):
             load_plane(nc.sync if quad < 2 else nc.gpsimd, wi_planes_raw, wi_rows, quad)
         nc.scalar.activation(warm_out[:], warm[:], ACT.Abs_reciprocal_sqrt)
 
-        we_all = keep.tile([P, 4 * 2048], F32, name="we_all", tag="shared_c")
+        we_first = keep.tile([P, 2048], F32, name="we_first", tag="shared_c")
+        staged = {}
 
         def load_we(b, a):
             parts = 2 if (b, a) == (0, 0) else 1
             w = 512 // parts
             for part in range(parts):
-                o = 2048 * (2 * b + a) + 4 * w * part
-                raw = we_all[:, o : o + 4 * w].rearrange("p (i c) -> p i c", i=4)
+                o = 4 * w * part if parts == 2 else 2048 * (2 * b + a - 1)
+                raw = (we_first if parts == 2 else staged["rest"])[:, o : o + 4 * w].rearrange("p (i c) -> p i c", i=4)
                 c0 = 512 * b + w * part
                 nc.sync.dma_start(raw, we[512 * a : 512 * (a + 1), c0 : c0 + w].rearrange("(p i) c -> p i c", i=4))
                 we_raw[b, a, part] = raw
 
         load_we(0, 0)
         load_wi(1, "shared_d")
-        load_we(0, 1)
-        load_we(1, 0)
-        load_we(1, 1)
         late = {}
 
         def load_read_out():
@@ -108,19 +110,13 @@ def tile_list_saccade_divisive_inhibition_kernel(
         v_codes = {}
         v_planes = {}
         pairs = {}
-        held = {}
 
-        def gather_scales(s):
-            j0, n = SLICES[s]
-            if s == 0:
-                held["first"] = keep.tile([P, 2 * n], U8, name="v_planes_first", align_bytes=64)
-            if s == 1:
-                held["rest"] = keep.tile([P, 2 * (S - j0)], U8, name="v_planes_rest", tag="shared_d", align_bytes=64)
-            for a in range(2):
-                o = n * a if s == 0 else 2 * (j0 - JW) + n * a
-                plane = held["first" if s == 0 else "rest"][:, o : o + n]
-                nc.vector.tensor_copy(plane, tab_planes[:, T * a : T * (a + 1)].indirect(offsets[:, j0 // 16 : (j0 + n) // 16]))
-                v_planes[s, a] = plane
+        def gather_scales():
+            packed = keep.tile([P, S], U8, name="v_planes_packed", align_bytes=64)
+            nc.vector.tensor_copy(packed[:], tab_planes[:].indirect(offsets[:]))
+            nc.sync.dma_start(second_plane[0 : P - 4, :].bitcast(I32), packed[4:P, :].bitcast(I32))
+            v_planes[0] = packed
+            v_planes[1] = second_plane
 
         def gather_words(s):
             j0, n = SLICES[s]
@@ -139,7 +135,7 @@ def tile_list_saccade_divisive_inhibition_kernel(
         def v_operand(a, j0, n):
             s = max(x for x in range(len(SLICES)) if SLICES[x][0] <= j0)
             o = j0 - SLICES[s][0]
-            return v_codes[s][:, a, 2 * o : 2 * (o + n)].bitcast(FP4X4), v_planes[s, a][:, o : o + n]
+            return v_codes[s][:, a, 2 * o : 2 * (o + n)].bitcast(FP4X4), v_planes[a][:, j0 : j0 + n]
 
         wi_codes = {}
         wi_planes = {}
@@ -171,7 +167,7 @@ def tile_list_saccade_divisive_inhibition_kernel(
                 m = 128 // parts
                 dst = grouped[:].rearrange("p (t m i) -> p m t i", t=4, i=4)[:, m * part : m * (part + 1), :, :]
                 src = we_raw[b, a, part].rearrange("p i (m t) -> p m t i", t=4)
-                if b == 0:
+                if parts == 2:
                     nc.scalar.copy(dst, src)
                 else:
                     nc.vector.tensor_copy(dst, src)
@@ -211,20 +207,20 @@ def tile_list_saccade_divisive_inhibition_kernel(
 
         def make_gain(u):
             root = work.tile([P, 4 * JW], F32, name="root", bufs=3)
-            nc.scalar.activation(
-                root[:].rearrange("p (j tp t) -> p j tp t", tp=2, t=2),
-                gain[u][:].rearrange("p tp (j t) -> p j tp t", t=2),
-                ACT.Abs_reciprocal_sqrt,
-                bias=1.0,
-            )
-            gain[u] = root
             sq = keep.tile([P, 4 * JW], F32, name="gain%d" % u)
-            if u in SCALAR_SQUARES:
-                nc.scalar.activation(sq[:], gain[u][:], ACT.Square)
-            else:
-                for half in range(2):
-                    cols = slice(512 * half, 512 * (half + 1))
-                    nc.gpsimd.tensor_tensor(sq[:, cols], root[:, cols], root[:, cols], MULT)
+            for jc in range(2):
+                nc.scalar.activation(
+                    root[:, 512 * jc : 512 * (jc + 1)].rearrange("p (j tp t) -> p j tp t", tp=2, t=2),
+                    gain[u][:, :, 256 * jc : 256 * (jc + 1)].rearrange("p tp (j t) -> p j tp t", t=2),
+                    ACT.Abs_reciprocal_sqrt,
+                    bias=1.0,
+                )
+            for jc in range(2):
+                cols = slice(512 * jc, 512 * (jc + 1))
+                if (u, jc) in VECTOR_SQUARES:
+                    nc.vector.tensor_tensor(sq[:, cols], root[:, cols], root[:, cols], MULT)
+                else:
+                    nc.scalar.activation(sq[:, cols], root[:, cols], ACT.Square)
             gain[u] = sq
 
         h_bf = {}
@@ -283,7 +279,11 @@ def tile_list_saccade_divisive_inhibition_kernel(
                     nc.scalar.activation(result[:], bank[:], ACT.Identity, bias=late["bias"][:, c : c + 1])
                 nc.sync.dma_start(out[P * c : P * (c + 1), JW * jh : JW * (jh + 1)], result[:])
 
-        gather_scales(0)
+        gather_scales()
+        staged["rest"] = keep.tile([P, 3 * 2048], F32, name="we_rest", tag="shared_a", align_bytes=64)
+        load_we(0, 1)
+        load_we(1, 0)
+        load_we(1, 1)
         gather_words(0)
         order_wi_scales(0)
         part_words(0)
@@ -295,49 +295,45 @@ def tile_list_saccade_divisive_inhibition_kernel(
         inhibit(1)
         make_gain(0)
         gather_words(1)
-        gather_scales(1)
         part_words(1)
+        round_we(0, 1)
+        quantize_we(0, 0)
         inhibit(2)
         inhibit(3)
-        round_we(0, 1)
-        make_gain(2)
-        gather_words(2)
-        gather_scales(2)
-        part_words(2)
-        quantize_we(0, 0)
         round_we(1, 0)
         quantize_we(0, 1)
+        make_gain(2)
+        excite(0)
         round_we(1, 1)
+        quantize_we(1, 0)
         inhibit(4)
         make_gain(1)
-        excite(0)
-        inhibit(5)
-        quantize_we(1, 0)
+        quantize_h(0)
         quantize_we(1, 1)
         load_read_out()
-        make_gain(3)
         excite(2)
-        quantize_h(0)
-        make_gain(4)
+        inhibit(5)
+        make_gain(3)
         excite(1)
         quantize_h(2)
         inhibit(6)
-        make_gain(5)
+        make_gain(4)
         excite(3)
         quantize_h(1)
         read_out(0)
         inhibit(7)
-        make_gain(6)
+        make_gain(5)
         excite(4)
         quantize_h(3)
         read_out(1)
-        make_gain(7)
-        quantize_h(4)
+        make_gain(6)
         excite(5)
+        quantize_h(4)
+        make_gain(7)
         excite(6)
         quantize_h(5)
         read_out(2)
-        quantize_h(6)
         excite(7)
+        quantize_h(6)
         quantize_h(7)
         read_out(3)

@@ -20,7 +20,7 @@ P = 128
 JW = 256
 NJ = S // JW
 SLICES = [(0, 256), (256, 768)]
-VECTOR_SQUARES = ((1, 0), (3, 0), (4, 0), (5, 0), (6, 0), (7, 0))
+VECTOR_SQUARES = (3, 4, 5)
 
 
 def tile_list_saccade_divisive_inhibition_kernel(
@@ -29,27 +29,26 @@ def tile_list_saccade_divisive_inhibition_kernel(
     nc = tc.nc
     with ExitStack() as ctx:
         keep = ctx.enter_context(tc.tile_pool(name="keep", bufs=1))
+        stage = ctx.enter_context(tc.tile_pool(name="stage", bufs=1))
         work = ctx.enter_context(tc.tile_pool(name="work", bufs=2))
         psum_i = ctx.enter_context(tc.psum_pool(name="psum_i", bufs=4))
         psum_e = ctx.enter_context(tc.psum_pool(name="psum_e", bufs=4))
 
         offsets = keep.tile([P, S // 16], U16, name="offsets")
-        tab_words = keep.tile([P, T], I32, name="tab_words", align_bytes=64)
-        tab_planes = keep.tile([P, T], U8, name="tab_planes", tag="shared_a", align_bytes=64)
+        tab_planes = stage.tile([P, T], U8, name="tab_planes", offset=15360, align_bytes=64)
         second_plane = keep.tile([P, S], U8, name="v_plane_second", align_bytes=64)
-        wi_area = keep.tile([P, 5 * H], U8, name="wi_area", align_bytes=64)
-        wi_planes_raw = wi_area[:, 1536:3584]
-        warm = keep.tile([P, 1], F32, name="warm", tag="shared_c")
+        wi_planes_raw = keep.tile([P, 2 * H], U8, name="wi_planes_raw", align_bytes=64)
+        warm = keep.tile([P, 1], F32, name="warm", tag="shared_c", align_bytes=64)
         warm_out = keep.tile([P, 1], F32, name="warm_out", tag="shared_d", align_bytes=64)
         wi_raw = {}
         we_raw = {}
 
-        def load_wi(b, tag):
-            raw = keep.tile([P, 2, 256], I32, name="wi_raw%d" % b, tag=tag, align_bytes=64)
+        def load_wi(b, area):
+            raw = area.bitcast(I32).rearrange("p (a x) -> p a x", a=2)
             nc.sync.dma_start(
-                raw[:], wi_words[:, :, 1024 * b : 1024 * (b + 1)].rearrange("a p x -> p a x").bitcast(I32)
+                raw, wi_words[:, :, 1024 * b : 1024 * (b + 1)].rearrange("a p x -> p a x").bitcast(I32)
             )
-            wi_raw[b] = raw
+            wi_raw[b] = area
 
         def load_plane(engine, plane, rows, quad):
             engine.dma_start(
@@ -58,49 +57,44 @@ def tile_list_saccade_divisive_inhibition_kernel(
             )
 
         nc.gpsimd.memset(tab_planes[:].bitcast(I32), 0)
-        nc.vector.memset(wi_planes_raw.bitcast(I32), 0)
-        nc.vector.memset(warm[:], 1.0)
-        nc.vector.memset(second_plane[96:P, :].bitcast(I32), 0)
+        nc.vector.memset(wi_planes_raw[:].bitcast(I32), 0)
+        nc.vector.memset(warm[:], 0.0)
+        nc.vector.memset(second_plane[:].bitcast(I32), 0)
 
         nc.sync.dma_start(offsets[:], offs)
-        nc.sync.dma_start(tab_words[:], tab[0, 0 : 512 * T].rearrange("(p x) -> p x", p=P).bitcast(I32))
-        load_wi(0, "shared_e")
+        wi_first = keep.tile([P, 2048], U8, name="wi_first", tag="shared_e", align_bytes=64)
+        load_wi(0, wi_first[:])
         tab_rows = tab[0, 512 * T : 544 * T].rearrange("(a q t) -> a q t", a=2, q=16).bitcast(I32)
         for quad in range(4):
-            nc.scalar.dma_start(
+            nc.sync.dma_start(
                 tab_planes[32 * quad : 32 * quad + 8, :].bitcast(I32), tab_rows[:, 4 * quad : 4 * quad + 4, :]
             )
         wi_rows = wi_scales.rearrange("a q c -> q a c").bitcast(I32)
         for quad in range(4):
-            load_plane(nc.sync if quad < 2 else nc.gpsimd, wi_planes_raw, wi_rows, quad)
-        nc.scalar.activation(warm_out[:], warm[:], ACT.Abs_reciprocal_sqrt)
+            load_plane(nc.sync, wi_planes_raw[:], wi_rows, quad)
+        nc.scalar.activation(warm_out[:], warm[:], ACT.Abs_reciprocal_sqrt, bias=1.0)
 
-        we_first = keep.tile([P, 2048], F32, name="we_first", tag="shared_c")
-        staged = {}
+        tab_words = keep.tile([P, T], I32, name="tab_words", tag="shared_c", align_bytes=64)
 
-        def load_we(b, a):
-            parts = 2 if (b, a) == (0, 0) else 1
-            w = 512 // parts
-            for part in range(parts):
-                o = 4 * w * part if parts == 2 else 2048 * (2 * b + a - 1)
-                raw = (we_first if parts == 2 else staged["rest"])[:, o : o + 4 * w].rearrange("p (i c) -> p i c", i=4)
-                c0 = 512 * b + w * part
-                nc.sync.dma_start(raw, we[512 * a : 512 * (a + 1), c0 : c0 + w].rearrange("(p i) c -> p i c", i=4))
-                we_raw[b, a, part] = raw
+        def load_we(b, a, area):
+            raw = area.bitcast(F32).rearrange("p (i c) -> p i c", i=4)
+            nc.sync.dma_start(
+                raw, we[512 * a : 512 * (a + 1), 512 * b : 512 * (b + 1)].rearrange("(p i) c -> p i c", i=4)
+            )
+            we_raw[b, a] = raw
 
-        load_we(0, 0)
-        load_wi(1, "shared_d")
+        nc.sync.dma_start(tab_words[:], tab[0, 0 : 512 * T].rearrange("(p x) -> p x", p=P).bitcast(I32))
         late = {}
 
         def load_read_out():
             wo_codes = work.tile([P, 2, N], I32, name="wo_codes", tag="we_bf", bufs=4, align_bytes=64)
             wo_planes = work.tile([P, 2 * N], U8, name="wo_planes", tag="we_bf", bufs=4, align_bytes=64)
-            bias = keep.tile([P, 2], F32, name="bias", tag="shared_c")
+            bias = keep.tile([P, 2], F32, name="bias", tag="shared_d", align_bytes=64)
             nc.sync.dma_start(wo_codes[:], wo_words.rearrange("a p c i -> p a (c i)").bitcast(I32))
             nc.vector.memset(wo_planes[:].bitcast(I32), 0)
             wo_rows = wo_scales.rearrange("a q c -> q a c").bitcast(I32)
             for quad in range(4):
-                load_plane(nc.sync, wo_planes, wo_rows, quad)
+                load_plane(nc.sync, wo_planes[:], wo_rows, quad)
             with nc.allow_non_contiguous_dma(reason="one bias value a partition"):
                 nc.sync.dma_start(bias[:], bo.rearrange("(c p) -> p c", p=P))
             late["codes"] = wo_codes
@@ -114,13 +108,18 @@ def tile_list_saccade_divisive_inhibition_kernel(
         def gather_scales():
             packed = keep.tile([P, S], U8, name="v_planes_packed", align_bytes=64)
             nc.vector.tensor_copy(packed[:], tab_planes[:].indirect(offsets[:]))
-            nc.sync.dma_start(second_plane[0 : P - 4, :].bitcast(I32), packed[4:P, :].bitcast(I32))
+            for quad in range(4):
+                engine = nc.sync if quad % 2 == 0 else nc.scalar
+                engine.dma_start(
+                    second_plane[32 * quad : 32 * quad + 4, :].bitcast(I32),
+                    packed[32 * quad + 4 : 32 * quad + 8, :].bitcast(I32),
+                )
             v_planes[0] = packed
             v_planes[1] = second_plane
 
         def gather_words(s):
             j0, n = SLICES[s]
-            both = keep.tile([P, n], U32, name="v_pairs%d" % s, tag="shared_e" if s else "v_pairs0", align_bytes=64)
+            both = keep.tile([P, n], U32, name="v_pairs%d" % s, tag="v_pairs", align_bytes=64)
             nc.vector.tensor_copy(both[:], tab_words[:].bitcast(U32).indirect(offsets[:, j0 // 16 : (j0 + n) // 16]))
             pairs[s] = both
 
@@ -144,15 +143,15 @@ def tile_list_saccade_divisive_inhibition_kernel(
             plane = keep.tile([P, 2, 512], U8, name="wi_plane%d" % b, align_bytes=64)
             nc.vector.tensor_copy(
                 plane[:].rearrange("p a (t m) -> p a t m", t=4),
-                wi_planes_raw.rearrange("p (a b m t) -> p b a t m", a=2, b=2, t=4)[:, b, :, :, :],
+                wi_planes_raw[:].rearrange("p (a b m t) -> p b a t m", a=2, b=2, t=4)[:, b, :, :, :],
             )
             wi_planes[b] = plane
 
         def order_wi_words(b):
-            codes = wi_area[:, 3072 * b : 3072 * b + 2048]
+            codes = keep.tile([P, 2048], U8, name="wi_codes%d" % b, align_bytes=64)
             nc.vector.tensor_copy(
-                codes.bitcast(U16).rearrange("p (a t m) -> p a t m", a=2, t=4),
-                wi_raw[b][:].bitcast(U16).rearrange("p a (m t) -> p a t m", t=4),
+                codes[:].bitcast(U16).rearrange("p (a t m) -> p a t m", a=2, t=4),
+                wi_raw[b].bitcast(U16).rearrange("p (a m t) -> p a t m", a=2, t=4),
             )
             wi_codes[b] = codes
 
@@ -162,15 +161,10 @@ def tile_list_saccade_divisive_inhibition_kernel(
 
         def round_we(b, a):
             grouped = work.tile([P, 2048], BF16, name="we_bf", tag="we_bf", bufs=4, align_bytes=64)
-            parts = 2 if (b, a) == (0, 0) else 1
-            for part in range(parts):
-                m = 128 // parts
-                dst = grouped[:].rearrange("p (t m i) -> p m t i", t=4, i=4)[:, m * part : m * (part + 1), :, :]
-                src = we_raw[b, a, part].rearrange("p i (m t) -> p m t i", t=4)
-                if parts == 2:
-                    nc.scalar.copy(dst, src)
-                else:
-                    nc.vector.tensor_copy(dst, src)
+            nc.vector.tensor_copy(
+                grouped[:].rearrange("p (t m i) -> p m t i", t=4, i=4),
+                we_raw[b, a].rearrange("p i (m t) -> p m t i", t=4),
+            )
             we_bf[b, a] = grouped
 
         def quantize_we(b, a):
@@ -180,10 +174,12 @@ def tile_list_saccade_divisive_inhibition_kernel(
             we_codes[b, a] = codes
             we_planes[b, a] = plane
 
+        mags = {}
+        roots = {}
         gain = {}
 
         def inhibit(u):
-            jh, b = divmod(u, 2)
+            b, jh = divmod(u, NJ)
             mag = keep.tile([P, 2, 2 * JW], F32, name="mag%d" % u)
             for tp in range(2):
                 bank = psum_i.tile([P, 2, JW], F32, name="bank_i", tag="bank_i")
@@ -203,24 +199,24 @@ def tile_list_saccade_divisive_inhibition_kernel(
                 nc.scalar.activation(
                     mag[:, tp, :].rearrange("p (j t) -> p j t", t=2), bank[:].rearrange("p t j -> p j t"), ACT.Abs
                 )
-            gain[u] = mag
+            mags[u] = mag
+
+        def make_root(u):
+            root = work.tile([P, 4 * JW], F32, name="root", bufs=3)
+            nc.scalar.activation(
+                root[:].rearrange("p (j tp t) -> p j tp t", tp=2, t=2),
+                mags[u][:].rearrange("p tp (j t) -> p j tp t", t=2),
+                ACT.Abs_reciprocal_sqrt,
+                bias=1.0,
+            )
+            roots[u] = root
 
         def make_gain(u):
-            root = work.tile([P, 4 * JW], F32, name="root", bufs=3)
             sq = keep.tile([P, 4 * JW], F32, name="gain%d" % u)
-            for jc in range(2):
-                nc.scalar.activation(
-                    root[:, 512 * jc : 512 * (jc + 1)].rearrange("p (j tp t) -> p j tp t", tp=2, t=2),
-                    gain[u][:, :, 256 * jc : 256 * (jc + 1)].rearrange("p tp (j t) -> p j tp t", t=2),
-                    ACT.Abs_reciprocal_sqrt,
-                    bias=1.0,
-                )
-            for jc in range(2):
-                cols = slice(512 * jc, 512 * (jc + 1))
-                if (u, jc) in VECTOR_SQUARES:
-                    nc.vector.tensor_tensor(sq[:, cols], root[:, cols], root[:, cols], MULT)
-                else:
-                    nc.scalar.activation(sq[:, cols], root[:, cols], ACT.Square)
+            if u in VECTOR_SQUARES:
+                nc.vector.tensor_tensor(sq[:], roots[u][:], roots[u][:], MULT)
+            else:
+                nc.scalar.activation(sq[:], roots[u][:], ACT.Square)
             gain[u] = sq
 
         h_bf = {}
@@ -228,7 +224,7 @@ def tile_list_saccade_divisive_inhibition_kernel(
         h_planes = {}
 
         def excite(u):
-            jh, b = divmod(u, 2)
+            b, jh = divmod(u, NJ)
             h = work.tile([P, 4 * JW], BF16, name="h_bf", bufs=3, align_bytes=64)
             for jc in range(JW // 128):
                 bank = psum_e.tile([P, 4, 128], F32, name="bank_e")
@@ -262,78 +258,71 @@ def tile_list_saccade_divisive_inhibition_kernel(
         def read_out(jh):
             for c in range(2):
                 bank = psum_i.tile([P, JW], F32, name="bank_y", tag="bank_i")
-                result = work.tile([P, JW], F32, name="result", bufs=4)
+                result = work.tile([P, JW], F32, name="result", bufs=8)
                 for b in range(2):
                     nc.tensor.matmul_mx(
                         out=bank[:],
                         lhsT=late["codes"][:, b, 128 * c : 128 * (c + 1)].bitcast(FP8X4),
                         lhsT_scale=late["planes"][:, N * b + 128 * c : N * b + 128 * (c + 1)],
-                        rhs=h_codes[2 * jh + b][:].bitcast(FP8X4),
-                        rhs_scale=h_planes[2 * jh + b][:],
+                        rhs=h_codes[NJ * b + jh][:].bitcast(FP8X4),
+                        rhs_scale=h_planes[NJ * b + jh][:],
                         start=(b == 0),
                         stop=(b == 1),
                     )
-                if c == 1:
+                if c == 1 and jh == NJ - 1:
                     nc.vector.tensor_scalar_add(result[:], bank[:], late["bias"][:, c : c + 1])
                 else:
                     nc.scalar.activation(result[:], bank[:], ACT.Identity, bias=late["bias"][:, c : c + 1])
                 nc.sync.dma_start(out[P * c : P * (c + 1), JW * jh : JW * (jh + 1)], result[:])
 
         gather_scales()
-        staged["rest"] = keep.tile([P, 3 * 2048], F32, name="we_rest", tag="shared_a", align_bytes=64)
-        load_we(0, 1)
-        load_we(1, 0)
-        load_we(1, 1)
-        gather_words(0)
-        order_wi_scales(0)
-        part_words(0)
+        early = stage.tile([P, 16384], U8, name="early", offset=0, align_bytes=64)
+        wi_second = stage.tile([P, 2048], U8, name="wi_second", offset=16384, align_bytes=64)
+        load_we(0, 0, early[:, 0:8192])
+        load_we(0, 1, early[:, 8192:16384])
+        load_wi(1, wi_second[:])
         order_wi_words(0)
-        round_we(0, 0)
+        later = keep.tile([P, 16384], U8, name="later", tag="shared_e", align_bytes=64)
+        load_we(1, 0, later[:, 0:8192])
+        load_we(1, 1, later[:, 8192:16384])
+        order_wi_scales(0)
+        gather_words(0)
+        part_words(0)
         inhibit(0)
-        order_wi_scales(1)
-        order_wi_words(1)
-        inhibit(1)
-        make_gain(0)
         gather_words(1)
         part_words(1)
+        make_root(0)
+        make_gain(0)
+        inhibit(1)
+        round_we(0, 0)
         round_we(0, 1)
         quantize_we(0, 0)
+        quantize_we(0, 1)
+        order_wi_scales(1)
+        make_root(1)
+        make_gain(1)
         inhibit(2)
+        excite(0)
+        order_wi_words(1)
+        quantize_h(0)
         inhibit(3)
         round_we(1, 0)
-        quantize_we(0, 1)
-        make_gain(2)
-        excite(0)
-        round_we(1, 1)
+        excite(1)
         quantize_we(1, 0)
-        inhibit(4)
-        make_gain(1)
-        quantize_h(0)
+        make_root(2)
+        make_gain(2)
+        round_we(1, 1)
+        quantize_h(1)
         quantize_we(1, 1)
         load_read_out()
-        excite(2)
-        inhibit(5)
-        make_gain(3)
-        excite(1)
-        quantize_h(2)
-        inhibit(6)
-        make_gain(4)
-        excite(3)
-        quantize_h(1)
-        read_out(0)
-        inhibit(7)
-        make_gain(5)
-        excite(4)
-        quantize_h(3)
-        read_out(1)
-        make_gain(6)
-        excite(5)
-        quantize_h(4)
-        make_gain(7)
-        excite(6)
-        quantize_h(5)
-        read_out(2)
-        excite(7)
-        quantize_h(6)
-        quantize_h(7)
-        read_out(3)
+        for u in range(2, 2 * NJ):
+            if u + 2 < 2 * NJ:
+                inhibit(u + 2)
+            if u + 1 < 2 * NJ:
+                make_root(u + 1)
+            excite(u)
+            if u + 1 < 2 * NJ:
+                make_gain(u + 1)
+            quantize_h(u)
+            if u >= NJ:
+                read_out(u - NJ)

@@ -196,16 +196,14 @@ def tile_list_saccade_divisive_inhibition_kernel(
                             start=(a == 0),
                             stop=(a == 1),
                         )
-                nc.scalar.activation(
-                    mag[:, tp, :].rearrange("p (j t) -> p j t", t=2), bank[:].rearrange("p t j -> p j t"), ACT.Abs
-                )
+                nc.scalar.activation(mag[:, tp, :], bank[:].rearrange("p t j -> p (t j)"), ACT.Abs)
             mags[u] = mag
 
         def make_root(u):
             root = work.tile([P, 4 * JW], F32, name="root", bufs=3)
             nc.scalar.activation(
-                root[:].rearrange("p (j tp t) -> p j tp t", tp=2, t=2),
-                mags[u][:].rearrange("p tp (j t) -> p j tp t", t=2),
+                root[:].rearrange("p (j t x) -> p j t x", t=4, x=2),
+                mags[u][:].rearrange("p tp (t j x) -> p j (tp t) x", t=2, x=2),
                 ACT.Abs_reciprocal_sqrt,
                 bias=1.0,
             )
@@ -241,9 +239,9 @@ def tile_list_saccade_divisive_inhibition_kernel(
                             stop=(a == 1),
                         )
                 nc.vector.tensor_tensor(
-                    h[:, 512 * jc : 512 * (jc + 1)].rearrange("p (j t) -> p j t", t=4),
-                    bank[:].rearrange("p t j -> p j t"),
-                    gain[u][:, 512 * jc : 512 * (jc + 1)].rearrange("p (j t) -> p j t", t=4),
+                    h[:, 512 * jc : 512 * (jc + 1)].rearrange("p (j x t) -> p j t x", t=4, x=2),
+                    bank[:].rearrange("p t (j x) -> p j t x", x=2),
+                    gain[u][:, 512 * jc : 512 * (jc + 1)].rearrange("p (j t x) -> p j t x", t=4, x=2),
                     MULT,
                 )
             h_bf[u] = h
@@ -294,30 +292,31 @@ def tile_list_saccade_divisive_inhibition_kernel(
         make_root(0)
         make_gain(0)
         inhibit(1)
+        inhibit(2)
         round_we(0, 0)
         round_we(0, 1)
         quantize_we(0, 0)
         quantize_we(0, 1)
+        inhibit(3)
         order_wi_scales(1)
+        order_wi_words(1)
         make_root(1)
         make_gain(1)
-        inhibit(2)
         excite(0)
-        order_wi_words(1)
-        quantize_h(0)
-        inhibit(3)
+        inhibit(4)
         round_we(1, 0)
-        excite(1)
+        quantize_h(0)
+        round_we(1, 1)
         quantize_we(1, 0)
         make_root(2)
         make_gain(2)
-        round_we(1, 1)
-        quantize_h(1)
+        excite(1)
         quantize_we(1, 1)
         load_read_out()
+        quantize_h(1)
         for u in range(2, 2 * NJ):
-            if u + 2 < 2 * NJ:
-                inhibit(u + 2)
+            if u + 3 < 2 * NJ:
+                inhibit(u + 3)
             if u + 1 < 2 * NJ:
                 make_root(u + 1)
             excite(u)

@@ -20,7 +20,7 @@ P = 128
 JW = 256
 NJ = S // JW
 SLICES = [(0, 256), (256, 768)]
-VECTOR_SQUARES = (3, 4, 5)
+VECTOR_SQUARES = (2, 3, 4)
 
 
 def tile_list_saccade_divisive_inhibition_kernel(
@@ -56,19 +56,17 @@ def tile_list_saccade_divisive_inhibition_kernel(
                 rows[4 * quad : 4 * quad + 4, :, :],
             )
 
-        nc.gpsimd.memset(tab_planes[:].bitcast(I32), 0)
-        nc.vector.memset(wi_planes_raw[:].bitcast(I32), 0)
+        nc.vector.memset(tab_planes[:].bitcast(I32), 0)
         nc.vector.memset(warm[:], 0.0)
+        nc.gpsimd.memset(wi_planes_raw[:].bitcast(I32), 0)
         nc.vector.memset(second_plane[:].bitcast(I32), 0)
 
         nc.sync.dma_start(offsets[:], offs)
         wi_first = keep.tile([P, 2048], U8, name="wi_first", tag="shared_e", align_bytes=64)
         load_wi(0, wi_first[:])
-        tab_rows = tab[0, 512 * T : 544 * T].rearrange("(a q t) -> a q t", a=2, q=16).bitcast(I32)
-        for quad in range(4):
-            nc.sync.dma_start(
-                tab_planes[32 * quad : 32 * quad + 8, :].bitcast(I32), tab_rows[:, 4 * quad : 4 * quad + 4, :]
-            )
+        tab_rows = tab[0, 512 * T : 544 * T].rearrange("(a q r t) -> r q a t", a=2, q=4, r=4).bitcast(I32)
+        for row in range(4):
+            nc.sync.dma_start(tab_planes[row:P:16, :].bitcast(I32), tab_rows[row])
         wi_rows = wi_scales.rearrange("a q c -> q a c").bitcast(I32)
         for quad in range(4):
             load_plane(nc.sync, wi_planes_raw[:], wi_rows, quad)
@@ -111,8 +109,8 @@ def tile_list_saccade_divisive_inhibition_kernel(
             for quad in range(4):
                 engine = nc.sync if quad % 2 == 0 else nc.scalar
                 engine.dma_start(
-                    second_plane[32 * quad : 32 * quad + 4, :].bitcast(I32),
-                    packed[32 * quad + 4 : 32 * quad + 8, :].bitcast(I32),
+                    second_plane[quad:P:32, :].bitcast(I32),
+                    packed[16 + quad : P : 32, :].bitcast(I32),
                 )
             v_planes[0] = packed
             v_planes[1] = second_plane
@@ -196,26 +194,34 @@ def tile_list_saccade_divisive_inhibition_kernel(
                             start=(a == 0),
                             stop=(a == 1),
                         )
-                nc.scalar.activation(mag[:, tp, :], bank[:].rearrange("p t j -> p (t j)"), ACT.Abs)
+                nc.scalar.activation(
+                    mag[:, tp, :].rearrange("p (j t x) -> p j t x", t=2, x=2),
+                    bank[:].rearrange("p t (j x) -> p j t x", x=2),
+                    ACT.Abs,
+                )
             mags[u] = mag
 
-        def make_root(u):
-            root = work.tile([P, 4 * JW], F32, name="root", bufs=3)
+        def halves(u):
+            return [(0, JW)] if u + 1 < 2 * NJ else [(0, JW // 2), (JW // 2, JW // 2)]
+
+        def make_root(u, j0, n):
+            if j0 == 0:
+                roots[u] = work.tile([P, 4 * JW], F32, name="root", bufs=3)
             nc.scalar.activation(
-                root[:].rearrange("p (j t x) -> p j t x", t=4, x=2),
-                mags[u][:].rearrange("p tp (t j x) -> p j (tp t) x", t=2, x=2),
+                roots[u][:, 4 * j0 : 4 * (j0 + n)].rearrange("p (j tp y) -> p j tp y", tp=2, y=4),
+                mags[u][:].rearrange("p tp (j y) -> p j tp y", y=4)[:, j0 // 2 : (j0 + n) // 2, :, :],
                 ACT.Abs_reciprocal_sqrt,
                 bias=1.0,
             )
-            roots[u] = root
 
-        def make_gain(u):
-            sq = keep.tile([P, 4 * JW], F32, name="gain%d" % u)
+        def make_gain(u, j0, n):
+            if j0 == 0:
+                gain[u] = keep.tile([P, 4 * JW], F32, name="gain%d" % u)
+            cols = slice(4 * j0, 4 * (j0 + n))
             if u in VECTOR_SQUARES:
-                nc.vector.tensor_tensor(sq[:], roots[u][:], roots[u][:], MULT)
+                nc.vector.tensor_tensor(gain[u][:, cols], roots[u][:, cols], roots[u][:, cols], MULT)
             else:
-                nc.scalar.activation(sq[:], roots[u][:], ACT.Square)
-            gain[u] = sq
+                nc.scalar.activation(gain[u][:, cols], roots[u][:, cols], ACT.Square)
 
         h_bf = {}
         h_codes = {}
@@ -246,32 +252,35 @@ def tile_list_saccade_divisive_inhibition_kernel(
                 )
             h_bf[u] = h
 
-        def quantize_h(u):
-            codes = keep.tile([P, JW], U32, name="h_codes%d" % u, align_bytes=64)
-            plane = keep.tile([P, JW], U8, name="h_plane%d" % u, align_bytes=64)
-            nc.vector.quantize_mx(codes[:].bitcast(FP8X4), plane[:], h_bf[u][:])
-            h_codes[u] = codes
-            h_planes[u] = plane
+        def quantize_h(u, j0, n):
+            codes = keep.tile([P, n], U32, name="h_codes%d_%d" % (u, j0), align_bytes=64)
+            plane = keep.tile([P, n], U8, name="h_plane%d_%d" % (u, j0), align_bytes=64)
+            nc.vector.quantize_mx(codes[:].bitcast(FP8X4), plane[:], h_bf[u][:, 4 * j0 : 4 * (j0 + n)])
+            h_codes[u, j0] = codes
+            h_planes[u, j0] = plane
 
-        def read_out(jh):
+        def read_out(jh, j0, n):
+            result = work.tile([P, 2, n], F32, name="result", bufs=5)
             for c in range(2):
-                bank = psum_i.tile([P, JW], F32, name="bank_y", tag="bank_i")
-                result = work.tile([P, JW], F32, name="result", bufs=8)
+                bank = psum_i.tile([P, n], F32, name="bank_y", tag="bank_i")
                 for b in range(2):
+                    o = j0 if b == 0 else 0
+                    key = (NJ * b + jh, j0 - o)
                     nc.tensor.matmul_mx(
                         out=bank[:],
                         lhsT=late["codes"][:, b, 128 * c : 128 * (c + 1)].bitcast(FP8X4),
                         lhsT_scale=late["planes"][:, N * b + 128 * c : N * b + 128 * (c + 1)],
-                        rhs=h_codes[NJ * b + jh][:].bitcast(FP8X4),
-                        rhs_scale=h_planes[NJ * b + jh][:],
+                        rhs=h_codes[key][:, o : o + n].bitcast(FP8X4),
+                        rhs_scale=h_planes[key][:, o : o + n],
                         start=(b == 0),
                         stop=(b == 1),
                     )
                 if c == 1 and jh == NJ - 1:
-                    nc.vector.tensor_scalar_add(result[:], bank[:], late["bias"][:, c : c + 1])
+                    nc.vector.tensor_scalar_add(result[:, c, :], bank[:], late["bias"][:, c : c + 1])
                 else:
-                    nc.scalar.activation(result[:], bank[:], ACT.Identity, bias=late["bias"][:, c : c + 1])
-                nc.sync.dma_start(out[P * c : P * (c + 1), JW * jh : JW * (jh + 1)], result[:])
+                    nc.scalar.activation(result[:, c, :], bank[:], ACT.Identity, bias=late["bias"][:, c : c + 1])
+            c0 = JW * jh + j0
+            nc.sync.dma_start(out[:, c0 : c0 + n].rearrange("(c p) j -> p c j", p=P), result[:])
 
         gather_scales()
         early = stage.tile([P, 16384], U8, name="early", offset=0, align_bytes=64)
@@ -289,8 +298,8 @@ def tile_list_saccade_divisive_inhibition_kernel(
         inhibit(0)
         gather_words(1)
         part_words(1)
-        make_root(0)
-        make_gain(0)
+        make_root(0, 0, JW)
+        make_gain(0, 0, JW)
         inhibit(1)
         inhibit(2)
         round_we(0, 0)
@@ -300,28 +309,30 @@ def tile_list_saccade_divisive_inhibition_kernel(
         inhibit(3)
         order_wi_scales(1)
         order_wi_words(1)
-        make_root(1)
-        make_gain(1)
+        make_root(1, 0, JW)
+        make_gain(1, 0, JW)
         excite(0)
         inhibit(4)
         round_we(1, 0)
-        quantize_h(0)
+        quantize_h(0, 0, JW)
         round_we(1, 1)
         quantize_we(1, 0)
-        make_root(2)
-        make_gain(2)
+        make_root(2, 0, JW)
         excite(1)
         quantize_we(1, 1)
         load_read_out()
-        quantize_h(1)
+        make_gain(2, 0, JW)
+        quantize_h(1, 0, JW)
         for u in range(2, 2 * NJ):
             if u + 3 < 2 * NJ:
                 inhibit(u + 3)
-            if u + 1 < 2 * NJ:
-                make_root(u + 1)
             excite(u)
             if u + 1 < 2 * NJ:
-                make_gain(u + 1)
-            quantize_h(u)
+                for j0, n in halves(u + 1):
+                    make_root(u + 1, j0, n)
+                    make_gain(u + 1, j0, n)
+            for j0, n in halves(u):
+                quantize_h(u, j0, n)
             if u >= NJ:
-                read_out(u - NJ)
+                for j0, n in halves(u):
+                    read_out(u - NJ, j0, n)

@@ -17,10 +17,14 @@ ACT = mybir.ActivationFunctionType
 MULT = mybir.AluOpType.mult
 
 P = 128
-JW = 256
-NJ = S // JW
-SLICES = [(0, 256), (256, 768)]
+PASS = 512
+BLOCK = 256
+BLOCKS = S // BLOCK
+PIECES = 2 * BLOCKS
+RUNS = ((0, BLOCK), (BLOCK, S - BLOCK))
 VECTOR_SQUARES = (2, 3, 4)
+LEAD = 3
+QUARTER = 4 * 4 * PASS
 
 
 def tile_list_saccade_divisive_inhibition_kernel(
@@ -35,118 +39,110 @@ def tile_list_saccade_divisive_inhibition_kernel(
         psum_e = ctx.enter_context(tc.psum_pool(name="psum_e", bufs=4))
 
         offsets = keep.tile([P, S // 16], U16, name="offsets")
-        tab_planes = stage.tile([P, T], U8, name="tab_planes", offset=15360, align_bytes=64)
-        second_plane = keep.tile([P, S], U8, name="v_plane_second", align_bytes=64)
+        tab_planes = stage.tile([P, T], U8, name="tab_planes", offset=2 * QUARTER - T // 2, align_bytes=64)
+        second_plane = keep.tile([P, S], U8, name="second_plane", align_bytes=64)
         wi_planes_raw = keep.tile([P, 2 * H], U8, name="wi_planes_raw", align_bytes=64)
-        warm = keep.tile([P, 1], F32, name="warm", tag="shared_c", align_bytes=64)
-        warm_out = keep.tile([P, 1], F32, name="warm_out", tag="shared_d", align_bytes=64)
+        warm = keep.tile([P, 1], F32, name="warm", tag="tab_words", align_bytes=64)
+        warm_out = keep.tile([P, 1], F32, name="warm_out")
         wi_raw = {}
         we_raw = {}
 
         def load_wi(b, area):
-            raw = area.bitcast(I32).rearrange("p (a x) -> p a x", a=2)
             nc.sync.dma_start(
-                raw, wi_words[:, :, 1024 * b : 1024 * (b + 1)].rearrange("a p x -> p a x").bitcast(I32)
+                area.bitcast(I32).rearrange("p (a x) -> p a x", a=2),
+                wi_words[:, :, 2 * PASS * b : 2 * PASS * (b + 1)].rearrange("a p x -> p a x").bitcast(I32),
             )
             wi_raw[b] = area
 
-        def load_plane(engine, plane, rows, quad):
-            engine.dma_start(
-                plane[32 * quad : 32 * quad + 4, :].bitcast(I32).rearrange("p (a x) -> p a x", a=2),
-                rows[4 * quad : 4 * quad + 4, :, :],
-            )
+        def load_planes(planes, scales):
+            rows = scales.rearrange("a s c -> s a c").bitcast(I32)
+            for quad in range(4):
+                nc.sync.dma_start(
+                    planes[32 * quad : 32 * quad + 4, :].bitcast(I32).rearrange("p (a x) -> p a x", a=2),
+                    rows[4 * quad : 4 * quad + 4, :, :],
+                )
 
-        nc.vector.memset(tab_planes[:].bitcast(I32), 0)
+        def load_we(b, a, area, c0=0, width=PASS):
+            raw = area.bitcast(F32).rearrange("p (q c) -> p q c", q=4)
+            first = PASS * b + c0
+            nc.sync.dma_start(
+                raw, we[PASS * a : PASS * (a + 1), first : first + width].rearrange("(p q) c -> p q c", q=4)
+            )
+            we_raw.setdefault((b, a), []).append((c0 // 4, width // 4, raw))
+
+        nc.vector.memset(tab_planes[:, 0 : T // 2].bitcast(I32), 0)
+        nc.gpsimd.memset(tab_planes[:, T // 2 : T].bitcast(I32), 0)
         nc.vector.memset(warm[:], 0.0)
         nc.gpsimd.memset(wi_planes_raw[:].bitcast(I32), 0)
         nc.vector.memset(second_plane[:].bitcast(I32), 0)
 
-        nc.sync.dma_start(offsets[:], offs)
-        wi_first = keep.tile([P, 2048], U8, name="wi_first", tag="shared_e", align_bytes=64)
+        wi_first = keep.tile([P, 4 * PASS], U8, name="wi_first", tag="we_second", align_bytes=64)
         load_wi(0, wi_first[:])
-        tab_rows = tab[0, 512 * T : 544 * T].rearrange("(a q r t) -> r q a t", a=2, q=4, r=4).bitcast(I32)
+        nc.sync.dma_start(offsets[:], offs)
+        tab_rows = tab[0, PASS * T : (PASS + 32) * T].rearrange("(a Q r x) -> r Q a x", a=2, Q=4, r=4).bitcast(I32)
         for row in range(4):
             nc.sync.dma_start(tab_planes[row:P:16, :].bitcast(I32), tab_rows[row])
-        wi_rows = wi_scales.rearrange("a q c -> q a c").bitcast(I32)
-        for quad in range(4):
-            load_plane(nc.sync, wi_planes_raw[:], wi_rows, quad)
+        load_planes(wi_planes_raw[:], wi_scales)
         nc.scalar.activation(warm_out[:], warm[:], ACT.Abs_reciprocal_sqrt, bias=1.0)
 
-        tab_words = keep.tile([P, T], I32, name="tab_words", tag="shared_c", align_bytes=64)
+        tab_words = keep.tile([P, T], I32, name="tab_words", tag="tab_words", align_bytes=64)
+        nc.sync.dma_start(tab_words[:], tab[0, 0 : PASS * T].rearrange("(p x) -> p x", p=P).bitcast(I32))
 
-        def load_we(b, a, area):
-            raw = area.bitcast(F32).rearrange("p (i c) -> p i c", i=4)
-            nc.sync.dma_start(
-                raw, we[512 * a : 512 * (a + 1), 512 * b : 512 * (b + 1)].rearrange("(p i) c -> p i c", i=4)
-            )
-            we_raw[b, a] = raw
-
-        nc.sync.dma_start(tab_words[:], tab[0, 0 : 512 * T].rearrange("(p x) -> p x", p=P).bitcast(I32))
-        late = {}
+        wo = {}
 
         def load_read_out():
-            wo_codes = work.tile([P, 2, N], I32, name="wo_codes", tag="we_bf", bufs=4, align_bytes=64)
-            wo_planes = work.tile([P, 2 * N], U8, name="wo_planes", tag="we_bf", bufs=4, align_bytes=64)
-            bias = keep.tile([P, 2], F32, name="bias", tag="shared_d", align_bytes=64)
-            nc.sync.dma_start(wo_codes[:], wo_words.rearrange("a p c i -> p a (c i)").bitcast(I32))
-            nc.vector.memset(wo_planes[:].bitcast(I32), 0)
-            wo_rows = wo_scales.rearrange("a q c -> q a c").bitcast(I32)
-            for quad in range(4):
-                load_plane(nc.sync, wo_planes[:], wo_rows, quad)
+            codes = work.tile([P, 2, N], I32, name="wo_codes", tag="we_bf", bufs=4, align_bytes=64)
+            planes = work.tile([P, 2 * N], U8, name="wo_planes", tag="we_bf", bufs=4, align_bytes=64)
+            bias = keep.tile([P, 2], F32, name="bias", tag="v_pairs", align_bytes=64)
+            nc.sync.dma_start(codes[:], wo_words.rearrange("a p c q -> p a (c q)").bitcast(I32))
+            nc.vector.memset(planes[:].bitcast(I32), 0)
+            load_planes(planes[:], wo_scales)
             with nc.allow_non_contiguous_dma(reason="one bias value a partition"):
                 nc.sync.dma_start(bias[:], bo.rearrange("(c p) -> p c", p=P))
-            late["codes"] = wo_codes
-            late["planes"] = wo_planes
-            late["bias"] = bias
+            wo["codes"] = codes
+            wo["planes"] = planes
+            wo["bias"] = bias
 
         v_codes = {}
         v_planes = {}
-        pairs = {}
 
         def gather_scales():
-            packed = keep.tile([P, S], U8, name="v_planes_packed", align_bytes=64)
-            nc.vector.tensor_copy(packed[:], tab_planes[:].indirect(offsets[:]))
-            for quad in range(4):
-                engine = nc.sync if quad % 2 == 0 else nc.scalar
+            gathered = keep.tile([P, S], U8, name="v_planes", align_bytes=64)
+            nc.vector.tensor_copy(gathered[:], tab_planes[:].indirect(offsets[:]))
+            for row in range(4):
+                engine = nc.sync if row % 2 == 0 else nc.scalar
                 engine.dma_start(
-                    second_plane[quad:P:32, :].bitcast(I32),
-                    packed[16 + quad : P : 32, :].bitcast(I32),
+                    second_plane[row:P:32, :].bitcast(I32), gathered[16 + row : P : 32, :].bitcast(I32)
                 )
-            v_planes[0] = packed
+            v_planes[0] = gathered
             v_planes[1] = second_plane
 
-        def gather_words(s):
-            j0, n = SLICES[s]
-            both = keep.tile([P, n], U32, name="v_pairs%d" % s, tag="v_pairs", align_bytes=64)
-            nc.vector.tensor_copy(both[:], tab_words[:].bitcast(U32).indirect(offsets[:, j0 // 16 : (j0 + n) // 16]))
-            pairs[s] = both
-
-        def part_words(s):
-            n = SLICES[s][1]
-            codes = keep.tile([P, 2, 2 * n], U8, name="v_codes%d" % s, align_bytes=64)
-            nc.vector.tensor_copy(
-                codes[:].bitcast(U16), pairs[s][:].bitcast(U16).rearrange("p (j a) -> p a j", a=2)
-            )
-            v_codes[s] = codes
+        def gather_words(run):
+            j0, n = RUNS[run]
+            pairs = keep.tile([P, n], U32, name="v_pairs%d" % run, tag="v_pairs", align_bytes=64)
+            nc.vector.tensor_copy(pairs[:], tab_words[:].bitcast(U32).indirect(offsets[:, j0 // 16 : (j0 + n) // 16]))
+            codes = keep.tile([P, 2, 2 * n], U8, name="v_codes%d" % run, align_bytes=64)
+            nc.vector.tensor_copy(codes[:].bitcast(U16), pairs[:].bitcast(U16).rearrange("p (j a) -> p a j", a=2))
+            v_codes[run] = codes
 
         def v_operand(a, j0, n):
-            s = max(x for x in range(len(SLICES)) if SLICES[x][0] <= j0)
-            o = j0 - SLICES[s][0]
-            return v_codes[s][:, a, 2 * o : 2 * (o + n)].bitcast(FP4X4), v_planes[a][:, j0 : j0 + n]
+            run = 0 if j0 < BLOCK else 1
+            o = j0 - RUNS[run][0]
+            return v_codes[run][:, a, 2 * o : 2 * (o + n)].bitcast(FP4X4), v_planes[a][:, j0 : j0 + n]
 
         wi_codes = {}
         wi_planes = {}
 
         def order_wi_scales(b):
-            plane = keep.tile([P, 2, 512], U8, name="wi_plane%d" % b, align_bytes=64)
+            planes = keep.tile([P, 2, PASS], U8, name="wi_planes%d" % b, align_bytes=64)
             nc.vector.tensor_copy(
-                plane[:].rearrange("p a (t m) -> p a t m", t=4),
+                planes[:].rearrange("p a (t m) -> p a t m", t=4),
                 wi_planes_raw[:].rearrange("p (a b m t) -> p b a t m", a=2, b=2, t=4)[:, b, :, :, :],
             )
-            wi_planes[b] = plane
+            wi_planes[b] = planes
 
         def order_wi_words(b):
-            codes = keep.tile([P, 2048], U8, name="wi_codes%d" % b, align_bytes=64)
+            codes = keep.tile([P, 4 * PASS], U8, name="wi_codes%d" % b, align_bytes=64)
             nc.vector.tensor_copy(
                 codes[:].bitcast(U16).rearrange("p (a t m) -> p a t m", a=2, t=4),
                 wi_raw[b].bitcast(U16).rearrange("p (a m t) -> p a t m", a=2, t=4),
@@ -158,96 +154,99 @@ def tile_list_saccade_divisive_inhibition_kernel(
         we_planes = {}
 
         def round_we(b, a):
-            grouped = work.tile([P, 2048], BF16, name="we_bf", tag="we_bf", bufs=4, align_bytes=64)
-            nc.vector.tensor_copy(
-                grouped[:].rearrange("p (t m i) -> p m t i", t=4, i=4),
-                we_raw[b, a].rearrange("p i (m t) -> p m t i", t=4),
-            )
+            grouped = work.tile([P, 4 * PASS], BF16, name="we_bf", tag="we_bf", bufs=4, align_bytes=64)
+            for m0, count, raw in we_raw[b, a]:
+                nc.vector.tensor_copy(
+                    grouped[:].rearrange("p (t m q) -> p m t q", t=4, q=4)[:, m0 : m0 + count, :, :],
+                    raw.rearrange("p q (m t) -> p m t q", t=4),
+                )
             we_bf[b, a] = grouped
 
         def quantize_we(b, a):
-            codes = keep.tile([P, 512], U32, name="we_codes%d%d" % (b, a), align_bytes=64)
-            plane = keep.tile([P, 512], U8, name="we_plane%d%d" % (b, a), align_bytes=64)
+            codes = keep.tile([P, PASS], U32, name="we_codes%d%d" % (b, a), align_bytes=64)
+            plane = keep.tile([P, PASS], U8, name="we_plane%d%d" % (b, a), align_bytes=64)
             nc.vector.quantize_mx(codes[:].bitcast(FP8X4), plane[:], we_bf[b, a][:])
             we_codes[b, a] = codes
             we_planes[b, a] = plane
 
         mags = {}
         roots = {}
-        gain = {}
+        gains = {}
 
         def inhibit(u):
-            b, jh = divmod(u, NJ)
-            mag = keep.tile([P, 2, 2 * JW], F32, name="mag%d" % u)
+            b, block = divmod(u, BLOCKS)
+            mag = keep.tile([P, 2, 2 * BLOCK], F32, name="mag%d" % u)
             for tp in range(2):
-                bank = psum_i.tile([P, 2, JW], F32, name="bank_i", tag="bank_i")
-                for t2 in range(2):
-                    t = 2 * tp + t2
+                bank = psum_i.tile([P, 2, BLOCK], F32, name="bank_i", tag="bank_i")
+                for s in range(2):
+                    t = 2 * tp + s
                     for a in range(2):
-                        rhs, rhs_scale = v_operand(a, JW * jh, JW)
+                        rhs, rhs_scale = v_operand(a, BLOCK * block, BLOCK)
+                        first = 2 * (PASS * a + P * t)
                         nc.tensor.matmul_mx(
-                            out=bank[:, t2, :],
-                            lhsT=wi_codes[b][:, 1024 * a + 256 * t : 1024 * a + 256 * (t + 1)].bitcast(FP4X4),
-                            lhsT_scale=wi_planes[b][:, a, 128 * t : 128 * (t + 1)],
+                            out=bank[:, s, :],
+                            lhsT=wi_codes[b][:, first : first + 2 * P].bitcast(FP4X4),
+                            lhsT_scale=wi_planes[b][:, a, P * t : P * (t + 1)],
                             rhs=rhs,
                             rhs_scale=rhs_scale,
                             start=(a == 0),
                             stop=(a == 1),
                         )
                 nc.scalar.activation(
-                    mag[:, tp, :].rearrange("p (j t x) -> p j t x", t=2, x=2),
-                    bank[:].rearrange("p t (j x) -> p j t x", x=2),
+                    mag[:, tp, :].rearrange("p (g s x) -> p g s x", s=2, x=2),
+                    bank[:].rearrange("p s (g x) -> p g s x", x=2),
                     ACT.Abs,
                 )
             mags[u] = mag
 
-        def halves(u):
-            return [(0, JW)] if u + 1 < 2 * NJ else [(0, JW // 2), (JW // 2, JW // 2)]
+        def parts(u):
+            return [(0, BLOCK)] if u + 1 < PIECES else [(0, BLOCK // 2), (BLOCK // 2, BLOCK // 2)]
 
         def make_root(u, j0, n):
             if j0 == 0:
-                roots[u] = work.tile([P, 4 * JW], F32, name="root", bufs=3)
+                roots[u] = work.tile([P, 4 * BLOCK], F32, name="root", bufs=3)
             nc.scalar.activation(
-                roots[u][:, 4 * j0 : 4 * (j0 + n)].rearrange("p (j tp y) -> p j tp y", tp=2, y=4),
-                mags[u][:].rearrange("p tp (j y) -> p j tp y", y=4)[:, j0 // 2 : (j0 + n) // 2, :, :],
+                roots[u][:, 4 * j0 : 4 * (j0 + n)].rearrange("p (g tp y) -> p g tp y", tp=2, y=4),
+                mags[u][:].rearrange("p tp (g y) -> p g tp y", y=4)[:, j0 // 2 : (j0 + n) // 2, :, :],
                 ACT.Abs_reciprocal_sqrt,
                 bias=1.0,
             )
 
         def make_gain(u, j0, n):
             if j0 == 0:
-                gain[u] = keep.tile([P, 4 * JW], F32, name="gain%d" % u)
+                gains[u] = keep.tile([P, 4 * BLOCK], F32, name="gain%d" % u)
             cols = slice(4 * j0, 4 * (j0 + n))
             if u in VECTOR_SQUARES:
-                nc.vector.tensor_tensor(gain[u][:, cols], roots[u][:, cols], roots[u][:, cols], MULT)
+                nc.vector.tensor_tensor(gains[u][:, cols], roots[u][:, cols], roots[u][:, cols], MULT)
             else:
-                nc.scalar.activation(gain[u][:, cols], roots[u][:, cols], ACT.Square)
+                nc.scalar.activation(gains[u][:, cols], roots[u][:, cols], ACT.Square)
 
         h_bf = {}
         h_codes = {}
         h_planes = {}
 
         def excite(u):
-            b, jh = divmod(u, NJ)
-            h = work.tile([P, 4 * JW], BF16, name="h_bf", bufs=3, align_bytes=64)
-            for jc in range(JW // 128):
-                bank = psum_e.tile([P, 4, 128], F32, name="bank_e")
+            b, block = divmod(u, BLOCKS)
+            h = work.tile([P, 4 * BLOCK], BF16, name="h_bf", bufs=3, align_bytes=64)
+            for j0 in range(0, BLOCK, P):
+                bank = psum_e.tile([P, 4, P], F32, name="bank_e", tag="bank_e")
                 for t in range(4):
                     for a in range(2):
-                        rhs, rhs_scale = v_operand(a, JW * jh + 128 * jc, 128)
+                        rhs, rhs_scale = v_operand(a, BLOCK * block + j0, P)
                         nc.tensor.matmul_mx(
                             out=bank[:, t, :],
-                            lhsT=we_codes[b, a][:, 128 * t : 128 * (t + 1)].bitcast(FP8X4),
-                            lhsT_scale=we_planes[b, a][:, 128 * t : 128 * (t + 1)],
+                            lhsT=we_codes[b, a][:, P * t : P * (t + 1)].bitcast(FP8X4),
+                            lhsT_scale=we_planes[b, a][:, P * t : P * (t + 1)],
                             rhs=rhs,
                             rhs_scale=rhs_scale,
                             start=(a == 0),
                             stop=(a == 1),
                         )
+                cols = slice(4 * j0, 4 * (j0 + P))
                 nc.vector.tensor_tensor(
-                    h[:, 512 * jc : 512 * (jc + 1)].rearrange("p (j x t) -> p j t x", t=4, x=2),
-                    bank[:].rearrange("p t (j x) -> p j t x", x=2),
-                    gain[u][:, 512 * jc : 512 * (jc + 1)].rearrange("p (j t x) -> p j t x", t=4, x=2),
+                    h[:, cols].rearrange("p (g x t) -> p g t x", t=4, x=2),
+                    bank[:].rearrange("p t (g x) -> p g t x", x=2),
+                    gains[u][:, cols].rearrange("p (g t x) -> p g t x", t=4, x=2),
                     MULT,
                 )
             h_bf[u] = h
@@ -259,80 +258,86 @@ def tile_list_saccade_divisive_inhibition_kernel(
             h_codes[u, j0] = codes
             h_planes[u, j0] = plane
 
-        def read_out(jh, j0, n):
-            result = work.tile([P, 2, n], F32, name="result", bufs=5)
+        def read_out(block, j0, n):
+            last = block == BLOCKS - 1
+            result = work.tile([P, 2, n], F32, name="result", bufs=BLOCKS + 1)
             for c in range(2):
-                bank = psum_i.tile([P, n], F32, name="bank_y", tag="bank_i")
+                if last:
+                    bank = psum_e.tile([P, n], F32, name="bank_last", tag="bank_e")
+                else:
+                    bank = psum_i.tile([P, n], F32, name="bank_y", tag="bank_i")
                 for b in range(2):
                     o = j0 if b == 0 else 0
-                    key = (NJ * b + jh, j0 - o)
+                    key = (BLOCKS * b + block, j0 - o)
                     nc.tensor.matmul_mx(
                         out=bank[:],
-                        lhsT=late["codes"][:, b, 128 * c : 128 * (c + 1)].bitcast(FP8X4),
-                        lhsT_scale=late["planes"][:, N * b + 128 * c : N * b + 128 * (c + 1)],
+                        lhsT=wo["codes"][:, b, P * c : P * (c + 1)].bitcast(FP8X4),
+                        lhsT_scale=wo["planes"][:, N * b + P * c : N * b + P * (c + 1)],
                         rhs=h_codes[key][:, o : o + n].bitcast(FP8X4),
                         rhs_scale=h_planes[key][:, o : o + n],
                         start=(b == 0),
                         stop=(b == 1),
                     )
-                if c == 1 and jh == NJ - 1:
-                    nc.vector.tensor_scalar_add(result[:, c, :], bank[:], late["bias"][:, c : c + 1])
+                if last and c == 1:
+                    nc.vector.tensor_scalar_add(result[:, c, :], bank[:], wo["bias"][:, c : c + 1])
                 else:
-                    nc.scalar.activation(result[:, c, :], bank[:], ACT.Identity, bias=late["bias"][:, c : c + 1])
-            c0 = JW * jh + j0
-            nc.sync.dma_start(out[:, c0 : c0 + n].rearrange("(c p) j -> p c j", p=P), result[:])
+                    nc.scalar.activation(result[:, c, :], bank[:], ACT.Identity, bias=wo["bias"][:, c : c + 1])
+            first = BLOCK * block + j0
+            nc.sync.dma_start(out[:, first : first + n].rearrange("(c p) j -> p c j", p=P), result[:])
 
         gather_scales()
-        early = stage.tile([P, 16384], U8, name="early", offset=0, align_bytes=64)
-        wi_second = stage.tile([P, 2048], U8, name="wi_second", offset=16384, align_bytes=64)
-        load_we(0, 0, early[:, 0:8192])
-        load_we(0, 1, early[:, 8192:16384])
+        we_first = stage.tile([P, 2 * QUARTER], U8, name="we_first", offset=0, align_bytes=64)
+        wi_second = stage.tile([P, 4 * PASS], U8, name="wi_second", offset=2 * QUARTER, align_bytes=64)
+        load_we(0, 0, we_first[:, 0:QUARTER])
+        load_we(0, 1, we_first[:, QUARTER : 3 * QUARTER // 2], 0, PASS // 2)
+        load_we(0, 1, we_first[:, 3 * QUARTER // 2 : 2 * QUARTER], PASS // 2, PASS // 2)
         load_wi(1, wi_second[:])
         order_wi_words(0)
-        later = keep.tile([P, 16384], U8, name="later", tag="shared_e", align_bytes=64)
-        load_we(1, 0, later[:, 0:8192])
-        load_we(1, 1, later[:, 8192:16384])
+        we_second = keep.tile([P, 2 * QUARTER], U8, name="we_second", tag="we_second", align_bytes=64)
+        for a in range(2):
+            load_we(1, a, we_second[:, QUARTER * a : QUARTER * (a + 1)])
+
         order_wi_scales(0)
         gather_words(0)
-        part_words(0)
         inhibit(0)
         gather_words(1)
-        part_words(1)
-        make_root(0, 0, JW)
-        make_gain(0, 0, JW)
-        inhibit(1)
-        inhibit(2)
-        round_we(0, 0)
-        round_we(0, 1)
-        quantize_we(0, 0)
-        quantize_we(0, 1)
-        inhibit(3)
+        make_root(0, 0, BLOCK)
+        make_gain(0, 0, BLOCK)
+        for u in range(1, LEAD):
+            inhibit(u)
+        for a in range(2):
+            round_we(0, a)
+        for a in range(2):
+            quantize_we(0, a)
+        inhibit(LEAD)
         order_wi_scales(1)
         order_wi_words(1)
-        make_root(1, 0, JW)
-        make_gain(1, 0, JW)
+        make_root(1, 0, BLOCK)
+        make_gain(1, 0, BLOCK)
+
         excite(0)
-        inhibit(4)
+        inhibit(LEAD + 1)
         round_we(1, 0)
-        quantize_h(0, 0, JW)
+        quantize_h(0, 0, BLOCK)
         round_we(1, 1)
         quantize_we(1, 0)
-        make_root(2, 0, JW)
+        make_root(2, 0, BLOCK)
         excite(1)
         quantize_we(1, 1)
         load_read_out()
-        make_gain(2, 0, JW)
-        quantize_h(1, 0, JW)
-        for u in range(2, 2 * NJ):
-            if u + 3 < 2 * NJ:
-                inhibit(u + 3)
+        make_gain(2, 0, BLOCK)
+        quantize_h(1, 0, BLOCK)
+
+        for u in range(2, PIECES):
+            if u + LEAD < PIECES:
+                inhibit(u + LEAD)
             excite(u)
-            if u + 1 < 2 * NJ:
-                for j0, n in halves(u + 1):
+            if u + 1 < PIECES:
+                for j0, n in parts(u + 1):
                     make_root(u + 1, j0, n)
                     make_gain(u + 1, j0, n)
-            for j0, n in halves(u):
+            for j0, n in parts(u):
                 quantize_h(u, j0, n)
-            if u >= NJ:
-                for j0, n in halves(u):
-                    read_out(u - NJ, j0, n)
+            if u >= BLOCKS:
+                for j0, n in parts(u):
+                    read_out(u - BLOCKS, j0, n)

@@ -24,6 +24,7 @@ PIECES = 2 * BLOCKS
 RUNS = ((0, BLOCK), (BLOCK, S - BLOCK))
 VECTOR_SQUARES = (2, 3, 4)
 LEAD = 3
+WARM_PASSES = 4
 QUARTER = 4 * 4 * PASS
 
 
@@ -39,10 +40,11 @@ def tile_list_saccade_divisive_inhibition_kernel(
         psum_e = ctx.enter_context(tc.psum_pool(name="psum_e", bufs=4))
 
         offsets = keep.tile([P, S // 16], U16, name="offsets")
-        tab_planes = stage.tile([P, T], U8, name="tab_planes", offset=2 * QUARTER - T // 2, align_bytes=64)
-        second_plane = keep.tile([P, S], U8, name="second_plane", align_bytes=64)
-        wi_planes_raw = keep.tile([P, 2 * H], U8, name="wi_planes_raw", align_bytes=64)
-        warm = keep.tile([P, 1], F32, name="warm", tag="tab_words", align_bytes=64)
+        tab_rows = stage.tile([P, T], U8, name="tab_rows", offset=2 * QUARTER - T // 2, align_bytes=64)
+        wi_rows = stage.tile([P, PASS], U8, name="wi_rows", offset=0, align_bytes=64)
+        v_planes = keep.tile([P, 2 * S], U8, name="v_planes", align_bytes=64)
+        wi_planes = keep.tile([P, 4 * PASS], U8, name="wi_planes", align_bytes=64)
+        warm = keep.tile([P, 1], F32, name="warm")
         warm_out = keep.tile([P, 1], F32, name="warm_out")
         wi_raw = {}
         we_raw = {}
@@ -70,23 +72,33 @@ def tile_list_saccade_divisive_inhibition_kernel(
             )
             we_raw.setdefault((b, a), []).append((c0 // 4, width // 4, raw))
 
-        nc.vector.memset(tab_planes[:, 0 : T // 2].bitcast(I32), 0)
-        nc.gpsimd.memset(tab_planes[:, T // 2 : T].bitcast(I32), 0)
-        nc.vector.memset(warm[:], 0.0)
-        nc.gpsimd.memset(wi_planes_raw[:].bitcast(I32), 0)
-        nc.vector.memset(second_plane[:].bitcast(I32), 0)
-
-        wi_first = keep.tile([P, 4 * PASS], U8, name="wi_first", tag="we_second", align_bytes=64)
-        load_wi(0, wi_first[:])
+        nc.sync.dma_start(
+            wi_rows[0:64, :].bitcast(I32), wi_scales.rearrange("a n (b c) -> (n b) a c", b=2).bitcast(I32)
+        )
+        nc.sync.dma_start(
+            tab_rows[0:32, :].bitcast(I32),
+            tab[0, PASS * T : (PASS + 32) * T].rearrange("(a n x) -> n a x", a=2, n=16).bitcast(I32),
+        )
         nc.sync.dma_start(offsets[:], offs)
-        tab_rows = tab[0, PASS * T : (PASS + 32) * T].rearrange("(a Q r x) -> r Q a x", a=2, Q=4, r=4).bitcast(I32)
-        for row in range(4):
-            nc.sync.dma_start(tab_planes[row:P:16, :].bitcast(I32), tab_rows[row])
-        load_planes(wi_planes_raw[:], wi_scales)
+        tab_words = keep.tile([P, T], I32, name="tab_words", align_bytes=64)
+        nc.sync.dma_start(tab_words[:], tab[0, 0 : PASS * T].rearrange("(p x) -> p x", p=P).bitcast(I32))
+        wi_first = keep.tile([P, 4 * PASS], U8, name="wi_first", tag="wi_words", align_bytes=64)
+        load_wi(0, wi_first[:])
+
+        nc.vector.memset(warm[:], 0.0)
+        nc.vector.memset(wi_rows[64:P, :].bitcast(I32), 0)
+        nc.vector.memset(tab_rows[32:64, :].bitcast(I32), 0)
+        nc.vector.memset(tab_rows[64:P, :].bitcast(I32), 0)
+        nc.gpsimd.memset(wi_planes[:].bitcast(I32), 0)
+        nc.gpsimd.memset(v_planes[:].bitcast(I32), 0)
         nc.scalar.activation(warm_out[:], warm[:], ACT.Abs_reciprocal_sqrt, bias=1.0)
 
-        tab_words = keep.tile([P, T], I32, name="tab_words", tag="tab_words", align_bytes=64)
-        nc.sync.dma_start(tab_words[:], tab[0, 0 : PASS * T].rearrange("(p x) -> p x", p=P).bitcast(I32))
+        def move_rows(planes, rows, count, engines):
+            for quad in range(4):
+                engines[quad % len(engines)].dma_start(
+                    planes[32 * quad : 32 * quad + 4, :].bitcast(I32).rearrange("p (a x) -> p a x", a=count),
+                    rows[4 * count * quad : 4 * count * (quad + 1), :].bitcast(I32),
+                )
 
         wo = {}
 
@@ -104,18 +116,11 @@ def tile_list_saccade_divisive_inhibition_kernel(
             wo["bias"] = bias
 
         v_codes = {}
-        v_planes = {}
 
         def gather_scales():
-            gathered = keep.tile([P, S], U8, name="v_planes", align_bytes=64)
-            nc.vector.tensor_copy(gathered[:], tab_planes[:].indirect(offsets[:]))
-            for row in range(4):
-                engine = nc.sync if row % 2 == 0 else nc.scalar
-                engine.dma_start(
-                    second_plane[row:P:32, :].bitcast(I32), gathered[16 + row : P : 32, :].bitcast(I32)
-                )
-            v_planes[0] = gathered
-            v_planes[1] = second_plane
+            gathered = keep.tile([P, S], U8, name="v_rows", tag="we_second", align_bytes=64)
+            nc.vector.tensor_copy(gathered[:], tab_rows[:].indirect(offsets[:]))
+            move_rows(v_planes, gathered, 2, (nc.sync,))
 
         def gather_words(run):
             j0, n = RUNS[run]
@@ -128,18 +133,16 @@ def tile_list_saccade_divisive_inhibition_kernel(
         def v_operand(a, j0, n):
             run = 0 if j0 < BLOCK else 1
             o = j0 - RUNS[run][0]
-            return v_codes[run][:, a, 2 * o : 2 * (o + n)].bitcast(FP4X4), v_planes[a][:, j0 : j0 + n]
+            return v_codes[run][:, a, 2 * o : 2 * (o + n)].bitcast(FP4X4), v_planes[:, S * a + j0 : S * a + j0 + n]
 
         wi_codes = {}
-        wi_planes = {}
 
-        def order_wi_scales(b):
-            planes = keep.tile([P, 2, PASS], U8, name="wi_planes%d" % b, align_bytes=64)
+        def order_wi_scales():
+            ordered = keep.tile([P, PASS], U8, name="wi_ordered", align_bytes=64)
             nc.vector.tensor_copy(
-                planes[:].rearrange("p a (t m) -> p a t m", t=4),
-                wi_planes_raw[:].rearrange("p (a b m t) -> p b a t m", a=2, b=2, t=4)[:, b, :, :, :],
+                ordered[:].rearrange("p (t m) -> p t m", t=4), wi_rows[:].rearrange("p (m t) -> p t m", t=4)
             )
-            wi_planes[b] = planes
+            move_rows(wi_planes, ordered, 4, (nc.sync,))
 
         def order_wi_words(b):
             codes = keep.tile([P, 4 * PASS], U8, name="wi_codes%d" % b, align_bytes=64)
@@ -153,14 +156,14 @@ def tile_list_saccade_divisive_inhibition_kernel(
         we_codes = {}
         we_planes = {}
 
-        def round_we(b, a):
-            grouped = work.tile([P, 4 * PASS], BF16, name="we_bf", tag="we_bf", bufs=4, align_bytes=64)
-            for m0, count, raw in we_raw[b, a]:
-                nc.vector.tensor_copy(
-                    grouped[:].rearrange("p (t m q) -> p m t q", t=4, q=4)[:, m0 : m0 + count, :, :],
-                    raw.rearrange("p q (m t) -> p m t q", t=4),
-                )
-            we_bf[b, a] = grouped
+        def round_we(b, a, part=0, copy=nc.vector.tensor_copy):
+            if (b, a) not in we_bf:
+                we_bf[b, a] = work.tile([P, 4 * PASS], BF16, name="we_bf", tag="we_bf", bufs=4, align_bytes=64)
+            m0, count, raw = we_raw[b, a][part]
+            copy(
+                we_bf[b, a][:].rearrange("p (t m q) -> p m t q", t=4, q=4)[:, m0 : m0 + count, :, :],
+                raw.rearrange("p q (m t) -> p m t q", t=4),
+            )
 
         def quantize_we(b, a):
             codes = keep.tile([P, PASS], U32, name="we_codes%d%d" % (b, a), align_bytes=64)
@@ -186,7 +189,7 @@ def tile_list_saccade_divisive_inhibition_kernel(
                         nc.tensor.matmul_mx(
                             out=bank[:, s, :],
                             lhsT=wi_codes[b][:, first : first + 2 * P].bitcast(FP4X4),
-                            lhsT_scale=wi_planes[b][:, a, P * t : P * (t + 1)],
+                            lhsT_scale=wi_planes[:, PASS * (2 * b + a) + P * t : PASS * (2 * b + a) + P * (t + 1)],
                             rhs=rhs,
                             rhs_scale=rhs_scale,
                             start=(a == 0),
@@ -285,19 +288,34 @@ def tile_list_saccade_divisive_inhibition_kernel(
             first = BLOCK * block + j0
             nc.sync.dma_start(out[:, first : first + n].rearrange("(c p) j -> p c j", p=P), result[:])
 
+        order_wi_scales()
+        we_early = stage.tile([P, QUARTER // 2], U8, name="we_early", offset=0, align_bytes=64)
+        load_we(0, 0, we_early[:], 0, PASS // 2)
         gather_scales()
-        we_first = stage.tile([P, 2 * QUARTER], U8, name="we_first", offset=0, align_bytes=64)
-        wi_second = stage.tile([P, 4 * PASS], U8, name="wi_second", offset=2 * QUARTER, align_bytes=64)
-        load_we(0, 0, we_first[:, 0:QUARTER])
-        load_we(0, 1, we_first[:, QUARTER : 3 * QUARTER // 2], 0, PASS // 2)
-        load_we(0, 1, we_first[:, 3 * QUARTER // 2 : 2 * QUARTER], PASS // 2, PASS // 2)
-        load_wi(1, wi_second[:])
+        we_first = stage.tile([P, 3 * QUARTER // 2], U8, name="we_first", offset=QUARTER // 2, align_bytes=64)
+        we_bf[0, 0] = stage.tile([P, 4 * PASS], BF16, name="we_bf_first", offset=2 * QUARTER, align_bytes=64)
+        round_we(0, 0, 0, nc.scalar.copy)
+        load_we(0, 0, we_first[:, 0 : QUARTER // 2], PASS // 2, PASS // 2)
+        load_we(0, 1, we_first[:, QUARTER // 2 : QUARTER], 0, PASS // 2)
+        load_we(0, 1, we_first[:, QUARTER : 3 * QUARTER // 2], PASS // 2, PASS // 2)
+        warm_bank = psum_e.tile([P, PASS], F32, name="warm_bank", tag="bank_e")
+        for step in range(WARM_PASSES):
+            nc.tensor.matmul_mx(
+                out=warm_bank[:],
+                lhsT=wi_first[:, 0 : 2 * P].bitcast(FP4X4),
+                lhsT_scale=wi_planes[:, 0:P],
+                rhs=wi_first[:, 0 : 2 * PASS].bitcast(FP4X4),
+                rhs_scale=wi_planes[:, 0:PASS],
+                start=True,
+                stop=True,
+            )
         order_wi_words(0)
+        wi_second = keep.tile([P, 4 * PASS], U8, name="wi_second", tag="wi_words", align_bytes=64)
+        load_wi(1, wi_second[:])
         we_second = keep.tile([P, 2 * QUARTER], U8, name="we_second", tag="we_second", align_bytes=64)
         for a in range(2):
             load_we(1, a, we_second[:, QUARTER * a : QUARTER * (a + 1)])
 
-        order_wi_scales(0)
         gather_words(0)
         inhibit(0)
         gather_words(1)
@@ -305,13 +323,13 @@ def tile_list_saccade_divisive_inhibition_kernel(
         make_gain(0, 0, BLOCK)
         for u in range(1, LEAD):
             inhibit(u)
-        for a in range(2):
-            round_we(0, a)
-        for a in range(2):
-            quantize_we(0, a)
-        inhibit(LEAD)
-        order_wi_scales(1)
+        round_we(0, 0, 1)
+        round_we(0, 1, 0)
+        quantize_we(0, 0)
+        round_we(0, 1, 1)
         order_wi_words(1)
+        quantize_we(0, 1)
+        inhibit(LEAD)
         make_root(1, 0, BLOCK)
         make_gain(1, 0, BLOCK)
 

@@ -40,8 +40,8 @@ def tile_list_saccade_divisive_inhibition_kernel(
         psum_e = ctx.enter_context(tc.psum_pool(name="psum_e", bufs=4))
 
         offsets = keep.tile([P, S // 16], U16, name="offsets")
-        tab_rows = stage.tile([P, T], U8, name="tab_rows", offset=2 * QUARTER - T // 2, align_bytes=64)
-        wi_rows = stage.tile([P, PASS], U8, name="wi_rows", offset=0, align_bytes=64)
+        tab_rows = stage.tile([P, T], U8, name="tab_rows", offset=4 * PASS + 2 * QUARTER - T // 2, align_bytes=64)
+        wi_rows = stage.tile([P, PASS], U8, name="wi_rows", offset=4 * PASS - PASS // 2, align_bytes=64)
         v_planes = keep.tile([P, 2 * S], U8, name="v_planes", align_bytes=64)
         wi_planes = keep.tile([P, 4 * PASS], U8, name="wi_planes", align_bytes=64)
         warm = keep.tile([P, 1], F32, name="warm")
@@ -82,7 +82,7 @@ def tile_list_saccade_divisive_inhibition_kernel(
         nc.sync.dma_start(offsets[:], offs)
         tab_words = keep.tile([P, T], I32, name="tab_words", align_bytes=64)
         nc.sync.dma_start(tab_words[:], tab[0, 0 : PASS * T].rearrange("(p x) -> p x", p=P).bitcast(I32))
-        wi_first = keep.tile([P, 4 * PASS], U8, name="wi_first", tag="wi_words", align_bytes=64)
+        wi_first = keep.tile([P, 4 * PASS], U8, name="wi_first", align_bytes=64)
         load_wi(0, wi_first[:])
 
         nc.vector.memset(warm[:], 0.0)
@@ -281,7 +281,7 @@ def tile_list_saccade_divisive_inhibition_kernel(
                         start=(b == 0),
                         stop=(b == 1),
                     )
-                if last and c == 1:
+                if c == 1:
                     nc.vector.tensor_scalar_add(result[:, c, :], bank[:], wo["bias"][:, c : c + 1])
                 else:
                     nc.scalar.activation(result[:, c, :], bank[:], ACT.Identity, bias=wo["bias"][:, c : c + 1])
@@ -289,15 +289,16 @@ def tile_list_saccade_divisive_inhibition_kernel(
             nc.sync.dma_start(out[:, first : first + n].rearrange("(c p) j -> p c j", p=P), result[:])
 
         order_wi_scales()
-        we_early = stage.tile([P, QUARTER // 2], U8, name="we_early", offset=0, align_bytes=64)
+        we_early = stage.tile([P, QUARTER // 2], U8, name="we_early", offset=4 * PASS, align_bytes=64)
         load_we(0, 0, we_early[:], 0, PASS // 2)
+        wi_second = stage.tile([P, 4 * PASS], U8, name="wi_second", offset=0, align_bytes=64)
+        load_wi(1, wi_second[:])
         gather_scales()
-        we_first = stage.tile([P, 3 * QUARTER // 2], U8, name="we_first", offset=QUARTER // 2, align_bytes=64)
-        we_bf[0, 0] = stage.tile([P, 4 * PASS], BF16, name="we_bf_first", offset=2 * QUARTER, align_bytes=64)
+        we_first = stage.tile([P, 3 * QUARTER // 2], U8, name="we_first", offset=4 * PASS + QUARTER // 2, align_bytes=64)
+        we_bf[0, 0] = stage.tile([P, 4 * PASS], BF16, name="we_bf_first", offset=4 * PASS + 2 * QUARTER, align_bytes=64)
         round_we(0, 0, 0, nc.scalar.copy)
         load_we(0, 0, we_first[:, 0 : QUARTER // 2], PASS // 2, PASS // 2)
-        load_we(0, 1, we_first[:, QUARTER // 2 : QUARTER], 0, PASS // 2)
-        load_we(0, 1, we_first[:, QUARTER : 3 * QUARTER // 2], PASS // 2, PASS // 2)
+        load_we(0, 1, we_first[:, QUARTER // 2 : 3 * QUARTER // 2])
         warm_bank = psum_e.tile([P, PASS], F32, name="warm_bank", tag="bank_e")
         for step in range(WARM_PASSES):
             nc.tensor.matmul_mx(
@@ -310,8 +311,6 @@ def tile_list_saccade_divisive_inhibition_kernel(
                 stop=True,
             )
         order_wi_words(0)
-        wi_second = keep.tile([P, 4 * PASS], U8, name="wi_second", tag="wi_words", align_bytes=64)
-        load_wi(1, wi_second[:])
         we_second = keep.tile([P, 2 * QUARTER], U8, name="we_second", tag="we_second", align_bytes=64)
         for a in range(2):
             load_we(1, a, we_second[:, QUARTER * a : QUARTER * (a + 1)])
@@ -324,10 +323,9 @@ def tile_list_saccade_divisive_inhibition_kernel(
         for u in range(1, LEAD):
             inhibit(u)
         round_we(0, 0, 1)
-        round_we(0, 1, 0)
-        quantize_we(0, 0)
-        round_we(0, 1, 1)
         order_wi_words(1)
+        quantize_we(0, 0)
+        round_we(0, 1)
         quantize_we(0, 1)
         inhibit(LEAD)
         make_root(1, 0, BLOCK)
@@ -337,14 +335,14 @@ def tile_list_saccade_divisive_inhibition_kernel(
         inhibit(LEAD + 1)
         round_we(1, 0)
         quantize_h(0, 0, BLOCK)
-        round_we(1, 1)
         quantize_we(1, 0)
         make_root(2, 0, BLOCK)
         excite(1)
+        round_we(1, 1)
+        quantize_h(1, 0, BLOCK)
         quantize_we(1, 1)
         load_read_out()
         make_gain(2, 0, BLOCK)
-        quantize_h(1, 0, BLOCK)
 
         for u in range(2, PIECES):
             if u + LEAD < PIECES:

@@ -161,8 +161,8 @@ def tile_list_saccade_divisive_inhibition_kernel(
                 we_bf[b, a] = work.tile([P, 4 * PASS], BF16, name="we_bf", tag="we_bf", bufs=4, align_bytes=64)
             m0, count, raw = we_raw[b, a][part]
             copy(
-                we_bf[b, a][:].rearrange("p (t m q) -> p m t q", t=4, q=4)[:, m0 : m0 + count, :, :],
-                raw.rearrange("p q (m t) -> p m t q", t=4),
+                we_bf[b, a][:].rearrange("p (tp s m q) -> p m tp q s", tp=2, s=2, q=4)[:, m0 : m0 + count],
+                raw.rearrange("p q (m tp s) -> p m tp q s", tp=2, s=2),
             )
 
         def quantize_we(b, a):
@@ -291,13 +291,13 @@ def tile_list_saccade_divisive_inhibition_kernel(
         order_wi_scales()
         we_early = stage.tile([P, QUARTER // 2], U8, name="we_early", offset=4 * PASS, align_bytes=64)
         load_we(0, 0, we_early[:], 0, PASS // 2)
-        wi_second = stage.tile([P, 4 * PASS], U8, name="wi_second", offset=0, align_bytes=64)
-        load_wi(1, wi_second[:])
         gather_scales()
         we_first = stage.tile([P, 3 * QUARTER // 2], U8, name="we_first", offset=4 * PASS + QUARTER // 2, align_bytes=64)
-        we_bf[0, 0] = stage.tile([P, 4 * PASS], BF16, name="we_bf_first", offset=4 * PASS + 2 * QUARTER, align_bytes=64)
+        we_bf[0, 0] = keep.tile([P, 4 * PASS], BF16, name="we_bf_first", align_bytes=64)
         round_we(0, 0, 0, nc.scalar.copy)
         load_we(0, 0, we_first[:, 0 : QUARTER // 2], PASS // 2, PASS // 2)
+        wi_second = stage.tile([P, 4 * PASS], U8, name="wi_second", offset=4 * PASS + 2 * QUARTER, align_bytes=64)
+        load_wi(1, wi_second[:])
         load_we(0, 1, we_first[:, QUARTER // 2 : 3 * QUARTER // 2])
         warm_bank = psum_e.tile([P, PASS], F32, name="warm_bank", tag="bank_e")
         for step in range(WARM_PASSES):

@@ -121,6 +121,7 @@ def tile_list_saccade_divisive_inhibition_kernel(
             gathered = keep.tile([P, S], U8, name="v_rows", tag="we_second", align_bytes=64)
             nc.vector.tensor_copy(gathered[:], tab_rows[:].indirect(offsets[:]))
             move_rows(v_planes, gathered, 2, (nc.sync,))
+            return gathered
 
         def gather_words(run):
             j0, n = RUNS[run]
@@ -225,8 +226,8 @@ def tile_list_saccade_divisive_inhibition_kernel(
                 nc.scalar.activation(gains[u][:, cols], roots[u][:, cols], ACT.Square)
 
         h_bf = {}
-        h_codes = {}
-        h_planes = {}
+        h_codes = [keep.tile([P, S], U32, name="h_codes%d" % b, align_bytes=64) for b in range(2)]
+        h_planes = [keep.tile([P, S], U8, name="h_planes%d" % b, align_bytes=64) for b in range(2)]
 
         def excite(u):
             b, block = divmod(u, BLOCKS)
@@ -255,43 +256,44 @@ def tile_list_saccade_divisive_inhibition_kernel(
             h_bf[u] = h
 
         def quantize_h(u, j0, n):
-            codes = keep.tile([P, n], U32, name="h_codes%d_%d" % (u, j0), align_bytes=64)
-            plane = keep.tile([P, n], U8, name="h_plane%d_%d" % (u, j0), align_bytes=64)
-            nc.vector.quantize_mx(codes[:].bitcast(FP8X4), plane[:], h_bf[u][:, 4 * j0 : 4 * (j0 + n)])
-            h_codes[u, j0] = codes
-            h_planes[u, j0] = plane
+            b, block = divmod(u, BLOCKS)
+            cols = slice(BLOCK * block + j0, BLOCK * block + j0 + n)
+            nc.vector.quantize_mx(
+                h_codes[b][:, cols].bitcast(FP8X4), h_planes[b][:, cols], h_bf[u][:, 4 * j0 : 4 * (j0 + n)]
+            )
 
-        def read_out(block, j0, n):
-            last = block == BLOCKS - 1
-            result = work.tile([P, 2, n], F32, name="result", bufs=BLOCKS + 1)
+        def read_out(first, n):
+            last = first >= S - BLOCK
+            cols = slice(first, first + n)
+            result = keep.tile([P, 2, n], F32, name="result%d" % first)
             for c in range(2):
                 if last:
                     bank = psum_e.tile([P, n], F32, name="bank_last", tag="bank_e")
                 else:
                     bank = psum_i.tile([P, n], F32, name="bank_y", tag="bank_i")
                 for b in range(2):
-                    o = j0 if b == 0 else 0
-                    key = (BLOCKS * b + block, j0 - o)
                     nc.tensor.matmul_mx(
                         out=bank[:],
                         lhsT=wo["codes"][:, b, P * c : P * (c + 1)].bitcast(FP8X4),
                         lhsT_scale=wo["planes"][:, N * b + P * c : N * b + P * (c + 1)],
-                        rhs=h_codes[key][:, o : o + n].bitcast(FP8X4),
-                        rhs_scale=h_planes[key][:, o : o + n],
+                        rhs=h_codes[b][:, cols].bitcast(FP8X4),
+                        rhs_scale=h_planes[b][:, cols],
                         start=(b == 0),
                         stop=(b == 1),
                     )
-                if c == 1:
+                if c == 1 and last:
                     nc.vector.tensor_scalar_add(result[:, c, :], bank[:], wo["bias"][:, c : c + 1])
                 else:
                     nc.scalar.activation(result[:, c, :], bank[:], ACT.Identity, bias=wo["bias"][:, c : c + 1])
-            first = BLOCK * block + j0
-            nc.sync.dma_start(out[:, first : first + n].rearrange("(c p) j -> p c j", p=P), result[:])
+                if n > BLOCK:
+                    nc.sync.dma_start(out[P * c : P * (c + 1), cols], result[:, c, :])
+            if n <= BLOCK:
+                nc.sync.dma_start(out[:, cols].rearrange("(c p) j -> p c j", p=P), result[:])
 
         order_wi_scales()
         we_early = stage.tile([P, QUARTER // 2], U8, name="we_early", offset=4 * PASS, align_bytes=64)
         load_we(0, 0, we_early[:], 0, PASS // 2)
-        gather_scales()
+        v_rows = gather_scales()
         we_first = stage.tile([P, 3 * QUARTER // 2], U8, name="we_first", offset=4 * PASS + QUARTER // 2, align_bytes=64)
         we_bf[0, 0] = keep.tile([P, 4 * PASS], BF16, name="we_bf_first", align_bytes=64)
         round_we(0, 0, 0, nc.scalar.copy)
@@ -303,10 +305,10 @@ def tile_list_saccade_divisive_inhibition_kernel(
         for step in range(WARM_PASSES):
             nc.tensor.matmul_mx(
                 out=warm_bank[:],
-                lhsT=wi_first[:, 0 : 2 * P].bitcast(FP4X4),
-                lhsT_scale=wi_planes[:, 0:P],
-                rhs=wi_first[:, 0 : 2 * PASS].bitcast(FP4X4),
-                rhs_scale=wi_planes[:, 0:PASS],
+                lhsT=tab_words[:, 0 : P // 2].bitcast(FP4X4),
+                lhsT_scale=v_rows[:, 0:P],
+                rhs=tab_words[:, 0 : PASS // 2].bitcast(FP4X4),
+                rhs_scale=v_rows[:, 0:PASS],
                 start=True,
                 stop=True,
             )
@@ -348,12 +350,15 @@ def tile_list_saccade_divisive_inhibition_kernel(
             if u + LEAD < PIECES:
                 inhibit(u + LEAD)
             excite(u)
-            if u + 1 < PIECES:
-                for j0, n in parts(u + 1):
-                    make_root(u + 1, j0, n)
-                    make_gain(u + 1, j0, n)
+            if u <= BLOCKS:
+                for ahead in range(u + 1, u + 2 if u < BLOCKS else PIECES):
+                    for j0, n in parts(ahead):
+                        make_root(ahead, j0, n)
+                        make_gain(ahead, j0, n)
             for j0, n in parts(u):
                 quantize_h(u, j0, n)
-            if u >= BLOCKS:
+            if u == BLOCKS + 1:
+                read_out(0, 2 * BLOCK)
+            if u > BLOCKS + 1:
                 for j0, n in parts(u):
-                    read_out(u - BLOCKS, j0, n)
+                    read_out(BLOCK * (u - BLOCKS) + j0, n)

@@ -21,11 +21,18 @@ PASS = 512
 BLOCK = 256
 BLOCKS = S // BLOCK
 PIECES = 2 * BLOCKS
-RUNS = ((0, BLOCK), (BLOCK, S - BLOCK))
-VECTOR_SQUARES = (2, 3, 4)
+RUNS = ((0, BLOCK), (BLOCK, BLOCK), (2 * BLOCK, 2 * BLOCK))
+VECTOR_SQUARES = {1: BLOCK // 2, 2: BLOCK, 3: BLOCK, 4: BLOCK}
 LEAD = 3
 WARM_PASSES = 4
 QUARTER = 4 * 4 * PASS
+EARLY = 4 * PASS
+EIGHTH = EARLY + QUARTER // 2
+SECOND = EIGHTH + QUARTER // 2
+WI_SECOND = SECOND + QUARTER
+LATE = WI_SECOND + 4 * PASS
+WI_FIRST = LATE + 2 * QUARTER
+PAIRS = WI_FIRST + 4 * PASS + 4 * BLOCK
 
 
 def tile_list_saccade_divisive_inhibition_kernel(
@@ -40,7 +47,7 @@ def tile_list_saccade_divisive_inhibition_kernel(
         psum_e = ctx.enter_context(tc.psum_pool(name="psum_e", bufs=4))
 
         offsets = keep.tile([P, S // 16], U16, name="offsets")
-        tab_rows = stage.tile([P, T], U8, name="tab_rows", offset=4 * PASS + 2 * QUARTER - T // 2, align_bytes=64)
+        tab_rows = stage.tile([P, T], U8, name="tab_rows", offset=SECOND - T // 2, align_bytes=64)
         wi_rows = stage.tile([P, PASS], U8, name="wi_rows", offset=4 * PASS - PASS // 2, align_bytes=64)
         v_planes = keep.tile([P, 2 * S], U8, name="v_planes", align_bytes=64)
         wi_planes = keep.tile([P, 4 * PASS], U8, name="wi_planes", align_bytes=64)
@@ -82,7 +89,7 @@ def tile_list_saccade_divisive_inhibition_kernel(
         nc.sync.dma_start(offsets[:], offs)
         tab_words = keep.tile([P, T], I32, name="tab_words", align_bytes=64)
         nc.sync.dma_start(tab_words[:], tab[0, 0 : PASS * T].rearrange("(p x) -> p x", p=P).bitcast(I32))
-        wi_first = keep.tile([P, 4 * PASS], U8, name="wi_first", align_bytes=64)
+        wi_first = stage.tile([P, 4 * PASS], U8, name="wi_first", offset=WI_FIRST, align_bytes=64)
         load_wi(0, wi_first[:])
 
         nc.vector.memset(warm[:], 0.0)
@@ -104,11 +111,10 @@ def tile_list_saccade_divisive_inhibition_kernel(
 
         def load_read_out():
             codes = work.tile([P, 2, N], I32, name="wo_codes", tag="we_bf", bufs=4, align_bytes=64)
-            planes = work.tile([P, 2 * N], U8, name="wo_planes", tag="we_bf", bufs=4, align_bytes=64)
-            bias = keep.tile([P, 2], F32, name="bias", tag="v_pairs", align_bytes=64)
+            planes = wi_planes[:, 0 : 2 * N]
+            bias = stage.tile([P, 2], F32, name="bias", offset=PAIRS, align_bytes=64)
             nc.sync.dma_start(codes[:], wo_words.rearrange("a p c q -> p a (c q)").bitcast(I32))
-            nc.vector.memset(planes[:].bitcast(I32), 0)
-            load_planes(planes[:], wo_scales)
+            load_planes(planes, wo_scales)
             with nc.allow_non_contiguous_dma(reason="one bias value a partition"):
                 nc.sync.dma_start(bias[:], bo.rearrange("(c p) -> p c", p=P))
             wo["codes"] = codes
@@ -118,21 +124,35 @@ def tile_list_saccade_divisive_inhibition_kernel(
         v_codes = {}
 
         def gather_scales():
-            gathered = keep.tile([P, S], U8, name="v_rows", tag="we_second", align_bytes=64)
+            gathered = stage.tile([P, S], U8, name="v_rows", offset=LATE - S // 2, align_bytes=64)
             nc.vector.tensor_copy(gathered[:], tab_rows[:].indirect(offsets[:]))
             move_rows(v_planes, gathered, 2, (nc.sync,))
             return gathered
 
+        v_pairs = {}
+
         def gather_words(run):
             j0, n = RUNS[run]
-            pairs = keep.tile([P, n], U32, name="v_pairs%d" % run, tag="v_pairs", align_bytes=64)
+            where = PAIRS - (2 * n, 4 * n, 0)[run]
+            pairs = stage.tile([P, n], U32, name="v_pairs%d" % run, offset=where, align_bytes=64)
             nc.vector.tensor_copy(pairs[:], tab_words[:].bitcast(U32).indirect(offsets[:, j0 // 16 : (j0 + n) // 16]))
-            codes = keep.tile([P, 2, 2 * n], U8, name="v_codes%d" % run, align_bytes=64)
-            nc.vector.tensor_copy(codes[:].bitcast(U16), pairs[:].bitcast(U16).rearrange("p (j a) -> p a j", a=2))
+            v_pairs[run] = pairs
+
+        def part_words(run):
+            n = RUNS[run][1]
+            if run == 0:
+                codes = stage.tile([P, 2, 2 * n], U8, name="v_codes0", offset=WI_FIRST, align_bytes=64)
+            elif run == 2:
+                codes = stage.tile([P, 2, 2 * n], U8, name="v_codes2", offset=EIGHTH, align_bytes=64)
+            else:
+                codes = keep.tile([P, 2, 2 * n], U8, name="v_codes%d" % run, align_bytes=64)
+            nc.vector.tensor_copy(
+                codes[:].bitcast(U16), v_pairs[run][:].bitcast(U16).rearrange("p (j a) -> p a j", a=2)
+            )
             v_codes[run] = codes
 
         def v_operand(a, j0, n):
-            run = 0 if j0 < BLOCK else 1
+            run = min(j0 // BLOCK, 2)
             o = j0 - RUNS[run][0]
             return v_codes[run][:, a, 2 * o : 2 * (o + n)].bitcast(FP4X4), v_planes[:, S * a + j0 : S * a + j0 + n]
 
@@ -146,7 +166,10 @@ def tile_list_saccade_divisive_inhibition_kernel(
             move_rows(wi_planes, ordered, 4, (nc.sync,))
 
         def order_wi_words(b):
-            codes = keep.tile([P, 4 * PASS], U8, name="wi_codes%d" % b, align_bytes=64)
+            if b == 0:
+                codes = keep.tile([P, 4 * PASS], U8, name="wi_codes0", align_bytes=64)
+            else:
+                codes = stage.tile([P, 4 * PASS], U8, name="wi_codes1", offset=SECOND, align_bytes=64)
             nc.vector.tensor_copy(
                 codes[:].bitcast(U16).rearrange("p (a t m) -> p a t m", a=2, t=4),
                 wi_raw[b].bitcast(U16).rearrange("p (a m t) -> p a t m", a=2, t=4),
@@ -173,13 +196,14 @@ def tile_list_saccade_divisive_inhibition_kernel(
             we_codes[b, a] = codes
             we_planes[b, a] = plane
 
+        banks_i = {}
         mags = {}
         roots = {}
         gains = {}
 
         def inhibit(u):
             b, block = divmod(u, BLOCKS)
-            mag = keep.tile([P, 2, 2 * BLOCK], F32, name="mag%d" % u)
+            mags[u] = keep.tile([P, 2, 2 * BLOCK], F32, name="mag%d" % u)
             for tp in range(2):
                 bank = psum_i.tile([P, 2, BLOCK], F32, name="bank_i", tag="bank_i")
                 for s in range(2):
@@ -196,12 +220,14 @@ def tile_list_saccade_divisive_inhibition_kernel(
                             start=(a == 0),
                             stop=(a == 1),
                         )
-                nc.scalar.activation(
-                    mag[:, tp, :].rearrange("p (g s x) -> p g s x", s=2, x=2),
-                    bank[:].rearrange("p s (g x) -> p g s x", x=2),
-                    ACT.Abs,
-                )
-            mags[u] = mag
+                banks_i[u, tp] = bank
+
+        def take_abs(u, tp):
+            nc.scalar.activation(
+                mags[u][:, tp, :].rearrange("p (g s x) -> p g s x", s=2, x=2),
+                banks_i[u, tp][:].rearrange("p s (g x) -> p g s x", x=2),
+                ACT.Abs,
+            )
 
         def parts(u):
             return [(0, BLOCK)] if u + 1 < PIECES else [(0, BLOCK // 2), (BLOCK // 2, BLOCK // 2)]
@@ -219,41 +245,42 @@ def tile_list_saccade_divisive_inhibition_kernel(
         def make_gain(u, j0, n):
             if j0 == 0:
                 gains[u] = keep.tile([P, 4 * BLOCK], F32, name="gain%d" % u)
-            cols = slice(4 * j0, 4 * (j0 + n))
-            if u in VECTOR_SQUARES:
+            split = j0 + min(n, VECTOR_SQUARES.get(u, 0))
+            if split > j0:
+                cols = slice(4 * j0, 4 * split)
                 nc.vector.tensor_tensor(gains[u][:, cols], roots[u][:, cols], roots[u][:, cols], MULT)
-            else:
+            if split < j0 + n:
+                cols = slice(4 * split, 4 * (j0 + n))
                 nc.scalar.activation(gains[u][:, cols], roots[u][:, cols], ACT.Square)
 
         h_bf = {}
         h_codes = [keep.tile([P, S], U32, name="h_codes%d" % b, align_bytes=64) for b in range(2)]
         h_planes = [keep.tile([P, S], U8, name="h_planes%d" % b, align_bytes=64) for b in range(2)]
 
-        def excite(u):
+        def excite(u, j0):
             b, block = divmod(u, BLOCKS)
-            h = work.tile([P, 4 * BLOCK], BF16, name="h_bf", bufs=3, align_bytes=64)
-            for j0 in range(0, BLOCK, P):
-                bank = psum_e.tile([P, 4, P], F32, name="bank_e", tag="bank_e")
-                for t in range(4):
-                    for a in range(2):
-                        rhs, rhs_scale = v_operand(a, BLOCK * block + j0, P)
-                        nc.tensor.matmul_mx(
-                            out=bank[:, t, :],
-                            lhsT=we_codes[b, a][:, P * t : P * (t + 1)].bitcast(FP8X4),
-                            lhsT_scale=we_planes[b, a][:, P * t : P * (t + 1)],
-                            rhs=rhs,
-                            rhs_scale=rhs_scale,
-                            start=(a == 0),
-                            stop=(a == 1),
-                        )
-                cols = slice(4 * j0, 4 * (j0 + P))
-                nc.vector.tensor_tensor(
-                    h[:, cols].rearrange("p (g x t) -> p g t x", t=4, x=2),
-                    bank[:].rearrange("p t (g x) -> p g t x", x=2),
-                    gains[u][:, cols].rearrange("p (g t x) -> p g t x", t=4, x=2),
-                    MULT,
-                )
-            h_bf[u] = h
+            if j0 == 0:
+                h_bf[u] = work.tile([P, 4 * BLOCK], BF16, name="h_bf", bufs=3, align_bytes=64)
+            bank = psum_e.tile([P, 4, P], F32, name="bank_e", tag="bank_e")
+            for t in range(4):
+                for a in range(2):
+                    rhs, rhs_scale = v_operand(a, BLOCK * block + j0, P)
+                    nc.tensor.matmul_mx(
+                        out=bank[:, t, :],
+                        lhsT=we_codes[b, a][:, P * t : P * (t + 1)].bitcast(FP8X4),
+                        lhsT_scale=we_planes[b, a][:, P * t : P * (t + 1)],
+                        rhs=rhs,
+                        rhs_scale=rhs_scale,
+                        start=(a == 0),
+                        stop=(a == 1),
+                    )
+            cols = slice(4 * j0, 4 * (j0 + P))
+            nc.vector.tensor_tensor(
+                h_bf[u][:, cols].rearrange("p (g x t) -> p g t x", t=4, x=2),
+                bank[:].rearrange("p t (g x) -> p g t x", x=2),
+                gains[u][:, cols].rearrange("p (g t x) -> p g t x", t=4, x=2),
+                MULT,
+            )
 
         def quantize_h(u, j0, n):
             b, block = divmod(u, BLOCKS)
@@ -294,13 +321,14 @@ def tile_list_saccade_divisive_inhibition_kernel(
         we_early = stage.tile([P, QUARTER // 2], U8, name="we_early", offset=4 * PASS, align_bytes=64)
         load_we(0, 0, we_early[:], 0, PASS // 2)
         v_rows = gather_scales()
-        we_first = stage.tile([P, 3 * QUARTER // 2], U8, name="we_first", offset=4 * PASS + QUARTER // 2, align_bytes=64)
+        we_eighth = stage.tile([P, QUARTER // 2], U8, name="we_eighth", offset=EIGHTH, align_bytes=64)
+        we_quarter = stage.tile([P, QUARTER], U8, name="we_quarter", offset=SECOND, align_bytes=64)
         we_bf[0, 0] = keep.tile([P, 4 * PASS], BF16, name="we_bf_first", align_bytes=64)
         round_we(0, 0, 0, nc.scalar.copy)
-        load_we(0, 0, we_first[:, 0 : QUARTER // 2], PASS // 2, PASS // 2)
-        wi_second = stage.tile([P, 4 * PASS], U8, name="wi_second", offset=4 * PASS + 2 * QUARTER, align_bytes=64)
+        load_we(0, 0, we_eighth[:], PASS // 2, PASS // 2)
+        load_we(0, 1, we_quarter[:])
+        wi_second = stage.tile([P, 4 * PASS], U8, name="wi_second", offset=WI_SECOND, align_bytes=64)
         load_wi(1, wi_second[:])
-        load_we(0, 1, we_first[:, QUARTER // 2 : 3 * QUARTER // 2])
         warm_bank = psum_e.tile([P, PASS], F32, name="warm_bank", tag="bank_e")
         for step in range(WARM_PASSES):
             nc.tensor.matmul_mx(
@@ -312,53 +340,88 @@ def tile_list_saccade_divisive_inhibition_kernel(
                 start=True,
                 stop=True,
             )
+        gather_words(0)
         order_wi_words(0)
-        we_second = keep.tile([P, 2 * QUARTER], U8, name="we_second", tag="we_second", align_bytes=64)
+        part_words(0)
+        we_second = stage.tile([P, 2 * QUARTER], U8, name="we_second", offset=LATE, align_bytes=64)
         for a in range(2):
             load_we(1, a, we_second[:, QUARTER * a : QUARTER * (a + 1)])
 
-        gather_words(0)
         inhibit(0)
+        take_abs(0, 0)
+        take_abs(0, 1)
         gather_words(1)
-        make_root(0, 0, BLOCK)
-        make_gain(0, 0, BLOCK)
-        for u in range(1, LEAD):
-            inhibit(u)
+        gather_words(2)
+        part_words(1)
         round_we(0, 0, 1)
-        order_wi_words(1)
+        part_words(2)
+        inhibit(1)
+        take_abs(1, 0)
+        make_root(0, 0, BLOCK)
+        take_abs(1, 1)
+        make_gain(0, 0, BLOCK)
+        inhibit(2)
+        take_abs(2, 0)
+        take_abs(2, 1)
         quantize_we(0, 0)
         round_we(0, 1)
+        order_wi_words(1)
         quantize_we(0, 1)
-        inhibit(LEAD)
+        inhibit(3)
+        take_abs(3, 0)
         make_root(1, 0, BLOCK)
-        make_gain(1, 0, BLOCK)
+        take_abs(3, 1)
 
-        excite(0)
-        inhibit(LEAD + 1)
+        excite(0, 0)
+        excite(0, P)
+        inhibit(4)
         round_we(1, 0)
         quantize_h(0, 0, BLOCK)
+        make_gain(1, 0, BLOCK)
         quantize_we(1, 0)
+        take_abs(4, 0)
+        take_abs(4, 1)
         make_root(2, 0, BLOCK)
-        excite(1)
+        excite(1, 0)
+        excite(1, P)
         round_we(1, 1)
         quantize_h(1, 0, BLOCK)
+        make_gain(2, 0, BLOCK)
         quantize_we(1, 1)
         load_read_out()
-        make_gain(2, 0, BLOCK)
 
-        for u in range(2, PIECES):
-            if u + LEAD < PIECES:
-                inhibit(u + LEAD)
-            excite(u)
-            if u <= BLOCKS:
-                for ahead in range(u + 1, u + 2 if u < BLOCKS else PIECES):
-                    for j0, n in parts(ahead):
-                        make_root(ahead, j0, n)
-                        make_gain(ahead, j0, n)
-            for j0, n in parts(u):
-                quantize_h(u, j0, n)
-            if u == BLOCKS + 1:
+        for u in (2, 3):
+            inhibit(u + LEAD)
+            take_abs(u + LEAD, 0)
+            take_abs(u + LEAD, 1)
+            excite(u, 0)
+            excite(u, P)
+            make_root(u + 1, 0, BLOCK)
+            make_gain(u + 1, 0, BLOCK)
+            quantize_h(u, 0, BLOCK)
+
+        inhibit(7)
+        make_root(5, 0, BLOCK)
+        take_abs(7, 0)
+        make_gain(5, 0, BLOCK)
+        make_root(6, 0, BLOCK)
+        take_abs(7, 1)
+        make_gain(6, 0, BLOCK)
+        for j0, n in parts(7):
+            make_root(7, j0, n)
+        for j0, n in parts(7):
+            make_gain(7, j0, n)
+        excite(4, 0)
+        excite(4, P)
+        for u in range(5, PIECES):
+            excite(u, 0)
+            quantize_h(u - 1, 0, BLOCK)
+            excite(u, P)
+            if u == 6:
                 read_out(0, 2 * BLOCK)
-            if u > BLOCKS + 1:
-                for j0, n in parts(u):
-                    read_out(BLOCK * (u - BLOCKS) + j0, n)
+            if u == 7:
+                read_out(2 * BLOCK, BLOCK)
+        for j0, n in parts(7):
+            quantize_h(7, j0, n)
+        for j0, n in parts(7):
+            read_out(3 * BLOCK + j0, n)

@@ -19,20 +19,15 @@ MULT = mybir.AluOpType.mult
 P = 128
 PASS = 512
 BLOCK = 256
-BLOCKS = S // BLOCK
-PIECES = 2 * BLOCKS
 RUNS = ((0, BLOCK), (BLOCK, BLOCK), (2 * BLOCK, 2 * BLOCK))
-VECTOR_SQUARES = {1: BLOCK // 2, 2: BLOCK, 3: BLOCK, 4: BLOCK}
-LEAD = 3
 WARM_PASSES = 4
 QUARTER = 4 * 4 * PASS
-EARLY = 4 * PASS
-EIGHTH = EARLY + QUARTER // 2
-SECOND = EIGHTH + QUARTER // 2
-WI_SECOND = SECOND + QUARTER
-LATE = WI_SECOND + 4 * PASS
-WI_FIRST = LATE + 2 * QUARTER
-PAIRS = WI_FIRST + 4 * PASS + 4 * BLOCK
+HALF = S // 2
+FIRST = 0
+SECOND = FIRST + QUARTER + PASS
+PAIRS = SECOND + 3 * QUARTER
+LAST_BF = PAIRS + 9 * HALF
+EARLY_H = SECOND + 2 * QUARTER
 
 
 def tile_list_saccade_divisive_inhibition_kernel(
@@ -42,151 +37,109 @@ def tile_list_saccade_divisive_inhibition_kernel(
     with ExitStack() as ctx:
         keep = ctx.enter_context(tc.tile_pool(name="keep", bufs=1))
         stage = ctx.enter_context(tc.tile_pool(name="stage", bufs=1))
-        work = ctx.enter_context(tc.tile_pool(name="work", bufs=2))
         psum_i = ctx.enter_context(tc.psum_pool(name="psum_i", bufs=4))
         psum_e = ctx.enter_context(tc.psum_pool(name="psum_e", bufs=4))
 
         offsets = keep.tile([P, S // 16], U16, name="offsets")
-        tab_rows = stage.tile([P, T], U8, name="tab_rows", offset=SECOND - T // 2, align_bytes=64)
-        wi_rows = stage.tile([P, PASS], U8, name="wi_rows", offset=4 * PASS - PASS // 2, align_bytes=64)
-        v_planes = keep.tile([P, 2 * S], U8, name="v_planes", align_bytes=64)
-        wi_planes = keep.tile([P, 4 * PASS], U8, name="wi_planes", align_bytes=64)
+        wi_rows = stage.tile([P, PASS], U8, name="wi_rows", offset=FIRST + QUARTER - BLOCK, align_bytes=64)
+        tab_rows = stage.tile([P, T], U8, name="tab_rows", offset=SECOND + QUARTER - T // 2, align_bytes=64)
+        rows = keep.tile([P, PASS + HALF], U8, name="rows", align_bytes=64)
+        planes = [keep.tile([P, 2, PASS + HALF], U8, name="planes%d" % b, align_bytes=64) for b in range(2)]
+        wi_raw = [
+            stage.tile([P, 2, 2 * PASS], U8, name="wi_raw%d" % b, offset=SECOND + 2 * QUARTER + 4 * PASS * b, align_bytes=64)
+            for b in range(2)
+        ]
+        wi_codes = [keep.tile([P, 2, 2 * PASS], U8, name="wi_codes%d" % b, align_bytes=64) for b in range(2)]
+        tab_words = keep.tile([P, T], I32, name="tab_words", align_bytes=64)
         warm = keep.tile([P, 1], F32, name="warm")
         warm_out = keep.tile([P, 1], F32, name="warm_out")
-        wi_raw = {}
-        we_raw = {}
 
-        def load_wi(b, area):
+        tab_scales = tab[0, PASS * T : (PASS + 32) * T].rearrange("(a n x) -> n a x", a=2, n=16).bitcast(I32)
+        for b in range(2):
+            nc.sync.dma_start(tab_rows[32 * b : 32 * (b + 1), :].bitcast(I32), tab_scales)
+        nc.sync.dma_start(offsets[:], offs)
+        for b in range(2):
             nc.sync.dma_start(
-                area.bitcast(I32).rearrange("p (a x) -> p a x", a=2),
+                wi_rows[32 * b : 32 * (b + 1), :].bitcast(I32),
+                wi_scales[:, :, PASS * b : PASS * (b + 1)].rearrange("a n c -> n a c").bitcast(I32),
+            )
+        nc.sync.dma_start(tab_words[:], tab[0, 0 : PASS * T].rearrange("(p x) -> p x", p=P).bitcast(I32))
+        for b in range(2):
+            nc.sync.dma_start(
+                wi_raw[b][:].bitcast(I32),
                 wi_words[:, :, 2 * PASS * b : 2 * PASS * (b + 1)].rearrange("a p x -> p a x").bitcast(I32),
             )
-            wi_raw[b] = area
-
-        def load_planes(planes, scales):
-            rows = scales.rearrange("a s c -> s a c").bitcast(I32)
-            for quad in range(4):
-                nc.sync.dma_start(
-                    planes[32 * quad : 32 * quad + 4, :].bitcast(I32).rearrange("p (a x) -> p a x", a=2),
-                    rows[4 * quad : 4 * quad + 4, :, :],
-                )
-
-        def load_we(b, a, area, c0=0, width=PASS):
-            raw = area.bitcast(F32).rearrange("p (q c) -> p q c", q=4)
-            first = PASS * b + c0
-            nc.sync.dma_start(
-                raw, we[PASS * a : PASS * (a + 1), first : first + width].rearrange("(p q) c -> p q c", q=4)
-            )
-            we_raw.setdefault((b, a), []).append((c0 // 4, width // 4, raw))
-
-        nc.sync.dma_start(
-            wi_rows[0:64, :].bitcast(I32), wi_scales.rearrange("a n (b c) -> (n b) a c", b=2).bitcast(I32)
-        )
-        nc.sync.dma_start(
-            tab_rows[0:32, :].bitcast(I32),
-            tab[0, PASS * T : (PASS + 32) * T].rearrange("(a n x) -> n a x", a=2, n=16).bitcast(I32),
-        )
-        nc.sync.dma_start(offsets[:], offs)
-        tab_words = keep.tile([P, T], I32, name="tab_words", align_bytes=64)
-        nc.sync.dma_start(tab_words[:], tab[0, 0 : PASS * T].rearrange("(p x) -> p x", p=P).bitcast(I32))
-        wi_first = stage.tile([P, 4 * PASS], U8, name="wi_first", offset=WI_FIRST, align_bytes=64)
-        load_wi(0, wi_first[:])
 
         nc.vector.memset(warm[:], 0.0)
-        nc.vector.memset(wi_rows[64:P, :].bitcast(I32), 0)
-        nc.vector.memset(tab_rows[32:64, :].bitcast(I32), 0)
         nc.vector.memset(tab_rows[64:P, :].bitcast(I32), 0)
-        nc.gpsimd.memset(wi_planes[:].bitcast(I32), 0)
-        nc.gpsimd.memset(v_planes[:].bitcast(I32), 0)
+        nc.vector.memset(wi_rows[64:P, :].bitcast(I32), 0)
+        for b in range(2):
+            nc.gpsimd.memset(planes[b][:].bitcast(I32), 0)
         nc.scalar.activation(warm_out[:], warm[:], ACT.Abs_reciprocal_sqrt, bias=1.0)
 
-        def move_rows(planes, rows, count, engines):
+        def move_rows(b):
             for quad in range(4):
-                engines[quad % len(engines)].dma_start(
-                    planes[32 * quad : 32 * quad + 4, :].bitcast(I32).rearrange("p (a x) -> p a x", a=count),
-                    rows[4 * count * quad : 4 * count * (quad + 1), :].bitcast(I32),
-                )
+                first = 32 * b + 8 * quad
+                nc.sync.dma_start(planes[b][32 * quad : 32 * quad + 4].bitcast(I32), rows[first : first + 8, :].bitcast(I32))
 
-        wo = {}
+        def order_wi_words(b):
+            nc.scalar.copy(
+                wi_codes[b][:].bitcast(U16).rearrange("p a (t m) -> p a t m", t=4),
+                wi_raw[b][:].bitcast(U16).rearrange("p a (m t) -> p a t m", t=4),
+            )
 
-        def load_read_out():
-            codes = work.tile([P, 2, N], I32, name="wo_codes", tag="we_bf", bufs=4, align_bytes=64)
-            planes = wi_planes[:, 0 : 2 * N]
-            bias = stage.tile([P, 2], F32, name="bias", offset=PAIRS, align_bytes=64)
-            nc.sync.dma_start(codes[:], wo_words.rearrange("a p c q -> p a (c q)").bitcast(I32))
-            load_planes(planes, wo_scales)
-            with nc.allow_non_contiguous_dma(reason="one bias value a partition"):
-                nc.sync.dma_start(bias[:], bo.rearrange("(c p) -> p c", p=P))
-            wo["codes"] = codes
-            wo["planes"] = planes
-            wo["bias"] = bias
+        we_raw = {}
 
-        v_codes = {}
-
-        def gather_scales():
-            gathered = stage.tile([P, S], U8, name="v_rows", offset=LATE - S // 2, align_bytes=64)
-            nc.vector.tensor_copy(gathered[:], tab_rows[:].indirect(offsets[:]))
-            move_rows(v_planes, gathered, 2, (nc.sync,))
-            return gathered
+        def load_we(b, a, offset, c0=0, width=PASS):
+            area = stage.tile([P, 4, width], F32, name="we_raw%d%d_%d" % (b, a, c0), offset=offset, align_bytes=64)
+            first = PASS * b + c0
+            nc.sync.dma_start(
+                area[:], we[PASS * a : PASS * (a + 1), first : first + width].rearrange("(p q) c -> p q c", q=4)
+            )
+            we_raw.setdefault((b, a), []).append((c0 // 4, width // 4, area))
 
         v_pairs = {}
+        v_codes = {}
 
         def gather_words(run):
             j0, n = RUNS[run]
-            where = PAIRS - (2 * n, 4 * n, 0)[run]
-            pairs = stage.tile([P, n], U32, name="v_pairs%d" % run, offset=where, align_bytes=64)
-            nc.vector.tensor_copy(pairs[:], tab_words[:].bitcast(U32).indirect(offsets[:, j0 // 16 : (j0 + n) // 16]))
-            v_pairs[run] = pairs
+            where = PAIRS + (5 * HALF, 7 * HALF, HALF - P)[run]
+            v_pairs[run] = stage.tile([P, n], U32, name="v_pairs%d" % run, offset=where, align_bytes=64)
+            nc.vector.tensor_copy(
+                v_pairs[run][:], tab_words[:].bitcast(U32).indirect(offsets[:, j0 // 16 : (j0 + n) // 16])
+            )
 
         def part_words(run):
             n = RUNS[run][1]
-            if run == 0:
-                codes = stage.tile([P, 2, 2 * n], U8, name="v_codes0", offset=WI_FIRST, align_bytes=64)
-            elif run == 2:
-                codes = stage.tile([P, 2, 2 * n], U8, name="v_codes2", offset=EIGHTH, align_bytes=64)
+            if run == 2:
+                v_codes[run] = stage.tile([P, 2, 2 * n], U8, name="v_codes2", offset=FIRST, align_bytes=64)
             else:
-                codes = keep.tile([P, 2, 2 * n], U8, name="v_codes%d" % run, align_bytes=64)
+                v_codes[run] = keep.tile([P, 2, 2 * n], U8, name="v_codes%d" % run, align_bytes=64)
             nc.vector.tensor_copy(
-                codes[:].bitcast(U16), v_pairs[run][:].bitcast(U16).rearrange("p (j a) -> p a j", a=2)
+                v_codes[run][:].bitcast(U16), v_pairs[run][:].bitcast(U16).rearrange("p (j a) -> p a j", a=2)
             )
-            v_codes[run] = codes
 
         def v_operand(a, j0, n):
             run = min(j0 // BLOCK, 2)
             o = j0 - RUNS[run][0]
-            return v_codes[run][:, a, 2 * o : 2 * (o + n)].bitcast(FP4X4), v_planes[:, S * a + j0 : S * a + j0 + n]
-
-        wi_codes = {}
-
-        def order_wi_scales():
-            ordered = keep.tile([P, PASS], U8, name="wi_ordered", align_bytes=64)
-            nc.vector.tensor_copy(
-                ordered[:].rearrange("p (t m) -> p t m", t=4), wi_rows[:].rearrange("p (m t) -> p t m", t=4)
-            )
-            move_rows(wi_planes, ordered, 4, (nc.sync,))
-
-        def order_wi_words(b):
-            if b == 0:
-                codes = keep.tile([P, 4 * PASS], U8, name="wi_codes0", align_bytes=64)
-            else:
-                codes = stage.tile([P, 4 * PASS], U8, name="wi_codes1", offset=SECOND, align_bytes=64)
-            nc.vector.tensor_copy(
-                codes[:].bitcast(U16).rearrange("p (a t m) -> p a t m", a=2, t=4),
-                wi_raw[b].bitcast(U16).rearrange("p (a m t) -> p a t m", a=2, t=4),
-            )
-            wi_codes[b] = codes
+            words = v_codes[run][:, a, 2 * o : 2 * (o + n)].bitcast(FP4X4)
+            half, o = divmod(j0, HALF)
+            return words, planes[half][:, a, PASS + o : PASS + o + n]
 
         we_bf = {}
         we_codes = {}
         we_planes = {}
 
-        def round_we(b, a, part=0, copy=nc.vector.tensor_copy):
-            if (b, a) not in we_bf:
-                we_bf[b, a] = work.tile([P, 4 * PASS], BF16, name="we_bf", tag="we_bf", bufs=4, align_bytes=64)
+        def round_we(b, a, part=0):
+            if part == 0:
+                if (b, a) == (1, 1):
+                    we_bf[b, a] = stage.tile([P, 4 * PASS], BF16, name="we_bf11", offset=LAST_BF, align_bytes=64)
+                else:
+                    we_bf[b, a] = keep.tile([P, 4 * PASS], BF16, name="we_bf%d%d" % (b, a), align_bytes=64)
             m0, count, raw = we_raw[b, a][part]
-            copy(
+            nc.vector.tensor_copy(
                 we_bf[b, a][:].rearrange("p (tp s m q) -> p m tp q s", tp=2, s=2, q=4)[:, m0 : m0 + count],
-                raw.rearrange("p q (m tp s) -> p m tp q s", tp=2, s=2),
+                raw[:].rearrange("p q (m tp s) -> p m tp q s", tp=2, s=2),
             )
 
         def quantize_we(b, a):
@@ -196,75 +149,65 @@ def tile_list_saccade_divisive_inhibition_kernel(
             we_codes[b, a] = codes
             we_planes[b, a] = plane
 
-        banks_i = {}
         mags = {}
-        roots = {}
-        gains = {}
 
-        def inhibit(u):
-            b, block = divmod(u, BLOCKS)
-            mags[u] = keep.tile([P, 2, 2 * BLOCK], F32, name="mag%d" % u)
-            for tp in range(2):
-                bank = psum_i.tile([P, 2, BLOCK], F32, name="bank_i", tag="bank_i")
-                for s in range(2):
-                    t = 2 * tp + s
+        def inhibit(b, run):
+            j0, n = RUNS[run]
+            mags[b, run] = keep.tile([P, 4, n], F32, name="mag%d%d" % (b, run))
+            per_bank = PASS // n
+            for t0 in range(0, 4, per_bank):
+                bank = psum_i.tile([P, per_bank, n], F32, name="bank_i", tag="bank_i")
+                for s in range(per_bank):
+                    t = t0 + s
                     for a in range(2):
-                        rhs, rhs_scale = v_operand(a, BLOCK * block, BLOCK)
-                        first = 2 * (PASS * a + P * t)
+                        rhs, rhs_scale = v_operand(a, j0, n)
                         nc.tensor.matmul_mx(
                             out=bank[:, s, :],
-                            lhsT=wi_codes[b][:, first : first + 2 * P].bitcast(FP4X4),
-                            lhsT_scale=wi_planes[:, PASS * (2 * b + a) + P * t : PASS * (2 * b + a) + P * (t + 1)],
+                            lhsT=wi_codes[b][:, a, 2 * P * t : 2 * P * (t + 1)].bitcast(FP4X4),
+                            lhsT_scale=planes[b][:, a, P * t : P * (t + 1)],
                             rhs=rhs,
                             rhs_scale=rhs_scale,
                             start=(a == 0),
                             stop=(a == 1),
                         )
-                banks_i[u, tp] = bank
+                nc.scalar.activation(mags[b, run][:, t0 : t0 + per_bank, :], bank[:], ACT.Abs)
 
-        def take_abs(u, tp):
+        roots = {}
+        gains = {}
+
+        def make_root(b, block):
+            run = min(block, 2)
+            o = BLOCK * block - RUNS[run][0]
+            roots[b, block] = keep.tile([P, 4 * BLOCK], F32, name="root%d%d" % (b, block))
             nc.scalar.activation(
-                mags[u][:, tp, :].rearrange("p (g s x) -> p g s x", s=2, x=2),
-                banks_i[u, tp][:].rearrange("p s (g x) -> p g s x", x=2),
-                ACT.Abs,
-            )
-
-        def parts(u):
-            return [(0, BLOCK)] if u + 1 < PIECES else [(0, BLOCK // 2), (BLOCK // 2, BLOCK // 2)]
-
-        def make_root(u, j0, n):
-            if j0 == 0:
-                roots[u] = work.tile([P, 4 * BLOCK], F32, name="root", bufs=3)
-            nc.scalar.activation(
-                roots[u][:, 4 * j0 : 4 * (j0 + n)].rearrange("p (g tp y) -> p g tp y", tp=2, y=4),
-                mags[u][:].rearrange("p tp (g y) -> p g tp y", y=4)[:, j0 // 2 : (j0 + n) // 2, :, :],
+                roots[b, block][:].rearrange("p (g t x) -> p g t x", t=4, x=4),
+                mags[b, run][:, :, o : o + BLOCK].rearrange("p t (g x) -> p g t x", x=4),
                 ACT.Abs_reciprocal_sqrt,
                 bias=1.0,
             )
 
-        def make_gain(u, j0, n):
-            if j0 == 0:
-                gains[u] = keep.tile([P, 4 * BLOCK], F32, name="gain%d" % u)
-            split = j0 + min(n, VECTOR_SQUARES.get(u, 0))
-            if split > j0:
-                cols = slice(4 * j0, 4 * split)
-                nc.vector.tensor_tensor(gains[u][:, cols], roots[u][:, cols], roots[u][:, cols], MULT)
-            if split < j0 + n:
-                cols = slice(4 * split, 4 * (j0 + n))
-                nc.scalar.activation(gains[u][:, cols], roots[u][:, cols], ACT.Square)
+        def make_gain(b, block, engine=None, offset=None):
+            root = roots[b, block]
+            name = "gain%d%d" % (b, block)
+            if engine is None:
+                gains[b, block] = keep.tile([P, 4 * BLOCK], F32, name=name)
+                nc.scalar.activation(gains[b, block][:], root[:], ACT.Square)
+            else:
+                gains[b, block] = stage.tile([P, 4 * BLOCK], F32, name=name, offset=offset, align_bytes=64)
+                engine.tensor_tensor(gains[b, block][:], root[:], root[:], MULT)
 
         h_bf = {}
+        for b in range(2):
+            h_bf[b, 0] = stage.tile([P, 4 * HALF], BF16, name="h_bf%d0" % b, offset=EARLY_H + 8 * HALF * b, align_bytes=64)
+            h_bf[b, 1] = keep.tile([P, 4 * HALF], BF16, name="h_bf%d1" % b, align_bytes=64)
         h_codes = [keep.tile([P, S], U32, name="h_codes%d" % b, align_bytes=64) for b in range(2)]
         h_planes = [keep.tile([P, S], U8, name="h_planes%d" % b, align_bytes=64) for b in range(2)]
 
-        def excite(u, j0):
-            b, block = divmod(u, BLOCKS)
-            if j0 == 0:
-                h_bf[u] = work.tile([P, 4 * BLOCK], BF16, name="h_bf", bufs=3, align_bytes=64)
+        def excite(b, j0):
             bank = psum_e.tile([P, 4, P], F32, name="bank_e", tag="bank_e")
             for t in range(4):
                 for a in range(2):
-                    rhs, rhs_scale = v_operand(a, BLOCK * block + j0, P)
+                    rhs, rhs_scale = v_operand(a, j0, P)
                     nc.tensor.matmul_mx(
                         out=bank[:, t, :],
                         lhsT=we_codes[b, a][:, P * t : P * (t + 1)].bitcast(FP8X4),
@@ -274,41 +217,54 @@ def tile_list_saccade_divisive_inhibition_kernel(
                         start=(a == 0),
                         stop=(a == 1),
                     )
-            cols = slice(4 * j0, 4 * (j0 + P))
+            block, o = divmod(j0, BLOCK)
             nc.vector.tensor_tensor(
-                h_bf[u][:, cols].rearrange("p (g x t) -> p g t x", t=4, x=2),
-                bank[:].rearrange("p t (g x) -> p g t x", x=2),
-                gains[u][:, cols].rearrange("p (g t x) -> p g t x", t=4, x=2),
+                h_bf[b, j0 // HALF][:, 4 * (j0 % HALF) : 4 * (j0 % HALF + P)].rearrange("p (g x t) -> p g t x", t=4, x=4),
+                bank[:].rearrange("p t (g x) -> p g t x", x=4),
+                gains[b, block][:, 4 * o : 4 * (o + P)].rearrange("p (g t x) -> p g t x", t=4, x=4),
                 MULT,
             )
 
-        def quantize_h(u, j0, n):
-            b, block = divmod(u, BLOCKS)
-            cols = slice(BLOCK * block + j0, BLOCK * block + j0 + n)
+        def quantize_h(b, j0, n):
+            cols = slice(j0, j0 + n)
             nc.vector.quantize_mx(
-                h_codes[b][:, cols].bitcast(FP8X4), h_planes[b][:, cols], h_bf[u][:, 4 * j0 : 4 * (j0 + n)]
+                h_codes[b][:, cols].bitcast(FP8X4),
+                h_planes[b][:, cols],
+                h_bf[b, j0 // HALF][:, 4 * (j0 % HALF) : 4 * (j0 % HALF + n)],
             )
 
-        def read_out(first, n):
-            last = first >= S - BLOCK
+        wo = {}
+
+        def load_read_out():
+            codes = stage.tile([P, 2, N], I32, name="wo_codes", offset=FIRST + QUARTER // 4, align_bytes=64)
+            bias = stage.tile([P, 2], F32, name="bias", offset=FIRST + QUARTER // 2, align_bytes=64)
+            wo_planes = planes[0][:, :, 0:N]
+            nc.sync.dma_start(codes[:], wo_words.rearrange("a p c q -> p a (c q)").bitcast(I32))
+            wo_rows = wo_scales.rearrange("a s c -> s a c").bitcast(I32)
+            for quad in range(4):
+                nc.sync.dma_start(wo_planes[32 * quad : 32 * quad + 4].bitcast(I32), wo_rows[4 * quad : 4 * quad + 4])
+            with nc.allow_non_contiguous_dma(reason="one bias value a partition"):
+                nc.sync.dma_start(bias[:], bo.rearrange("(c p) -> p c", p=P))
+            wo["codes"] = codes
+            wo["planes"] = wo_planes
+            wo["bias"] = bias
+
+        def read_out(first, n, pool, tag, share=False):
             cols = slice(first, first + n)
             result = keep.tile([P, 2, n], F32, name="result%d" % first)
             for c in range(2):
-                if last:
-                    bank = psum_e.tile([P, n], F32, name="bank_last", tag="bank_e")
-                else:
-                    bank = psum_i.tile([P, n], F32, name="bank_y", tag="bank_i")
+                bank = pool.tile([P, n], F32, name="bank_y", tag=tag)
                 for b in range(2):
                     nc.tensor.matmul_mx(
                         out=bank[:],
                         lhsT=wo["codes"][:, b, P * c : P * (c + 1)].bitcast(FP8X4),
-                        lhsT_scale=wo["planes"][:, N * b + P * c : N * b + P * (c + 1)],
+                        lhsT_scale=wo["planes"][:, b, P * c : P * (c + 1)],
                         rhs=h_codes[b][:, cols].bitcast(FP8X4),
                         rhs_scale=h_planes[b][:, cols],
                         start=(b == 0),
                         stop=(b == 1),
                     )
-                if c == 1 and last:
+                if c == 1 and share:
                     nc.vector.tensor_scalar_add(result[:, c, :], bank[:], wo["bias"][:, c : c + 1])
                 else:
                     nc.scalar.activation(result[:, c, :], bank[:], ACT.Identity, bias=wo["bias"][:, c : c + 1])
@@ -317,111 +273,101 @@ def tile_list_saccade_divisive_inhibition_kernel(
             if n <= BLOCK:
                 nc.sync.dma_start(out[:, cols].rearrange("(c p) j -> p c j", p=P), result[:])
 
-        order_wi_scales()
-        we_early = stage.tile([P, QUARTER // 2], U8, name="we_early", offset=4 * PASS, align_bytes=64)
-        load_we(0, 0, we_early[:], 0, PASS // 2)
-        v_rows = gather_scales()
-        we_eighth = stage.tile([P, QUARTER // 2], U8, name="we_eighth", offset=EIGHTH, align_bytes=64)
-        we_quarter = stage.tile([P, QUARTER], U8, name="we_quarter", offset=SECOND, align_bytes=64)
-        we_bf[0, 0] = keep.tile([P, 4 * PASS], BF16, name="we_bf_first", align_bytes=64)
-        round_we(0, 0, 0, nc.scalar.copy)
-        load_we(0, 0, we_eighth[:], PASS // 2, PASS // 2)
-        load_we(0, 1, we_quarter[:])
-        wi_second = stage.tile([P, 4 * PASS], U8, name="wi_second", offset=WI_SECOND, align_bytes=64)
-        load_wi(1, wi_second[:])
+        first_rows = stage.tile([P, HALF], U8, name="first_rows", offset=FIRST, align_bytes=64)
+        nc.vector.tensor_copy(first_rows[:], tab_rows[:].indirect(offsets[:, 0 : HALF // 16]))
+        nc.vector.tensor_copy(
+            rows[:, 0:PASS].rearrange("p (t m) -> p t m", t=4), wi_rows[:].rearrange("p (m t) -> p t m", t=4)
+        )
+        nc.vector.tensor_copy(rows[:, PASS:], first_rows[:])
+        move_rows(0)
+        load_we(0, 0, FIRST)
+        order_wi_words(0)
         warm_bank = psum_e.tile([P, PASS], F32, name="warm_bank", tag="bank_e")
         for step in range(WARM_PASSES):
             nc.tensor.matmul_mx(
+                out=warm_bank[:, 0:BLOCK],
+                lhsT=rows[:, 0 : 2 * P].bitcast(FP4X4),
+                lhsT_scale=rows[:, 0:P],
+                rhs=rows[:, 0 : 2 * BLOCK].bitcast(FP4X4),
+                rhs_scale=rows[:, 0:BLOCK],
+                start=True,
+                stop=True,
+            )
+        for step in range(WARM_PASSES // 2):
+            nc.tensor.matmul_mx(
                 out=warm_bank[:],
-                lhsT=tab_words[:, 0 : P // 2].bitcast(FP4X4),
-                lhsT_scale=v_rows[:, 0:P],
-                rhs=tab_words[:, 0 : PASS // 2].bitcast(FP4X4),
-                rhs_scale=v_rows[:, 0:PASS],
+                lhsT=wi_raw[0][:, 0, 0 : 2 * P].bitcast(FP4X4),
+                lhsT_scale=rows[:, 0:P],
+                rhs=wi_raw[0][:, 0, :].bitcast(FP4X4),
+                rhs_scale=rows[:, 0:PASS],
                 start=True,
                 stop=True,
             )
         gather_words(0)
-        order_wi_words(0)
-        part_words(0)
-        we_second = stage.tile([P, 2 * QUARTER], U8, name="we_second", offset=LATE, align_bytes=64)
-        for a in range(2):
-            load_we(1, a, we_second[:, QUARTER * a : QUARTER * (a + 1)])
-
-        inhibit(0)
-        take_abs(0, 0)
-        take_abs(0, 1)
         gather_words(1)
-        gather_words(2)
+        part_words(0)
         part_words(1)
-        round_we(0, 0, 1)
-        part_words(2)
-        inhibit(1)
-        take_abs(1, 0)
-        make_root(0, 0, BLOCK)
-        take_abs(1, 1)
-        make_gain(0, 0, BLOCK)
-        inhibit(2)
-        take_abs(2, 0)
-        take_abs(2, 1)
-        quantize_we(0, 0)
-        round_we(0, 1)
+        late_rows = stage.tile([P, HALF], U8, name="late_rows", offset=PAIRS + 4 * HALF + HALF // 2, align_bytes=64)
+        nc.vector.tensor_copy(late_rows[:], tab_rows[:].indirect(offsets[:, HALF // 16 : S // 16]))
+        nc.vector.tensor_copy(rows[32:64, PASS:].bitcast(I32), late_rows[32:64, :].bitcast(I32))
+        move_rows(1)
+        load_we(0, 1, SECOND)
+        load_we(1, 0, SECOND + QUARTER)
+        inhibit(0, 0)
         order_wi_words(1)
+        load_we(1, 1, SECOND + 2 * QUARTER)
+        inhibit(0, 1)
+        gather_words(2)
+        make_root(0, 0)
+        make_root(0, 1)
+        inhibit(1, 0)
+        inhibit(1, 1)
+        round_we(0, 0)
+        part_words(2)
+        quantize_we(0, 0)
+        make_gain(0, 0, nc.vector, FIRST + QUARTER // 2 + 64)
+        round_we(0, 1)
+        make_gain(0, 1, nc.vector, SECOND)
         quantize_we(0, 1)
-        inhibit(3)
-        take_abs(3, 0)
-        make_root(1, 0, BLOCK)
-        take_abs(3, 1)
-
-        excite(0, 0)
-        excite(0, P)
-        inhibit(4)
+        inhibit(0, 2)
+        make_root(1, 0)
+        make_root(1, 1)
+        make_gain(1, 0)
         round_we(1, 0)
-        quantize_h(0, 0, BLOCK)
-        make_gain(1, 0, BLOCK)
-        quantize_we(1, 0)
-        take_abs(4, 0)
-        take_abs(4, 1)
-        make_root(2, 0, BLOCK)
-        excite(1, 0)
-        excite(1, P)
         round_we(1, 1)
-        quantize_h(1, 0, BLOCK)
-        make_gain(2, 0, BLOCK)
+        quantize_we(1, 0)
         quantize_we(1, 1)
+        make_gain(1, 1, nc.gpsimd, LAST_BF)
+        for j0 in range(0, HALF, P):
+            excite(0, j0)
+        inhibit(1, 2)
         load_read_out()
-
-        for u in (2, 3):
-            inhibit(u + LEAD)
-            take_abs(u + LEAD, 0)
-            take_abs(u + LEAD, 1)
-            excite(u, 0)
-            excite(u, P)
-            make_root(u + 1, 0, BLOCK)
-            make_gain(u + 1, 0, BLOCK)
-            quantize_h(u, 0, BLOCK)
-
-        inhibit(7)
-        make_root(5, 0, BLOCK)
-        take_abs(7, 0)
-        make_gain(5, 0, BLOCK)
-        make_root(6, 0, BLOCK)
-        take_abs(7, 1)
-        make_gain(6, 0, BLOCK)
-        for j0, n in parts(7):
-            make_root(7, j0, n)
-        for j0, n in parts(7):
-            make_gain(7, j0, n)
-        excite(4, 0)
-        excite(4, P)
-        for u in range(5, PIECES):
-            excite(u, 0)
-            quantize_h(u - 1, 0, BLOCK)
-            excite(u, P)
-            if u == 6:
-                read_out(0, 2 * BLOCK)
-            if u == 7:
-                read_out(2 * BLOCK, BLOCK)
-        for j0, n in parts(7):
-            quantize_h(7, j0, n)
-        for j0, n in parts(7):
-            read_out(3 * BLOCK + j0, n)
+        make_root(0, 2)
+        make_root(1, 2)
+        make_gain(0, 2)
+        make_root(0, 3)
+        make_root(1, 3)
+        make_gain(0, 3)
+        excite(1, 0)
+        quantize_h(0, 0, HALF)
+        make_gain(1, 2, nc.gpsimd, EARLY_H)
+        for j0 in range(P, HALF, P):
+            excite(1, j0)
+        excite(0, 4 * P)
+        excite(0, 5 * P)
+        quantize_h(1, 0, HALF)
+        make_gain(1, 3, nc.gpsimd, EARLY_H + 8 * HALF)
+        excite(1, 4 * P)
+        excite(1, 5 * P)
+        excite(0, 6 * P)
+        excite(0, 7 * P)
+        read_out(0, HALF, psum_i, "bank_i", True)
+        quantize_h(1, HALF, BLOCK)
+        quantize_h(0, HALF, HALF)
+        read_out(HALF, BLOCK, psum_i, "bank_i")
+        excite(1, 6 * P)
+        excite(1, 7 * P)
+        quantize_h(1, 6 * P, P)
+        quantize_h(1, 7 * P, P)
+        read_out(6 * P, P, psum_e, "bank_e", True)
+        read_out(7 * P, P, psum_e, "bank_e", True)

@@ -175,23 +175,27 @@ def tile_list_saccade_divisive_inhibition_kernel(
         roots = {}
         gains = {}
 
-        def make_root(b, block):
+        def make_root(b, block, parts=1):
             run = min(block, 2)
-            o = BLOCK * block - RUNS[run][0]
+            first = BLOCK * block - RUNS[run][0]
             roots[b, block] = keep.tile([P, 4 * BLOCK], F32, name="root%d%d" % (b, block))
-            nc.scalar.activation(
-                roots[b, block][:].rearrange("p (g t x) -> p g t x", t=4, x=4),
-                mags[b, run][:, :, o : o + BLOCK].rearrange("p t (g x) -> p g t x", x=4),
-                ACT.Abs_reciprocal_sqrt,
-                bias=1.0,
-            )
+            n = BLOCK // parts
+            for o in range(0, BLOCK, n):
+                nc.scalar.activation(
+                    roots[b, block][:, 4 * o : 4 * (o + n)].rearrange("p (g t x) -> p g t x", t=4, x=4),
+                    mags[b, run][:, :, first + o : first + o + n].rearrange("p t (g x) -> p g t x", x=4),
+                    ACT.Abs_reciprocal_sqrt,
+                    bias=1.0,
+                )
 
-        def make_gain(b, block, engine=None, offset=None):
+        def make_gain(b, block, engine=None, offset=None, parts=1):
             root = roots[b, block]
             name = "gain%d%d" % (b, block)
             if engine is None:
                 gains[b, block] = keep.tile([P, 4 * BLOCK], F32, name=name)
-                nc.scalar.activation(gains[b, block][:], root[:], ACT.Square)
+                n = 4 * BLOCK // parts
+                for o in range(0, 4 * BLOCK, n):
+                    nc.scalar.activation(gains[b, block][:, o : o + n], root[:, o : o + n], ACT.Square)
             else:
                 gains[b, block] = stage.tile([P, 4 * BLOCK], F32, name=name, offset=offset, align_bytes=64)
                 engine.tensor_tensor(gains[b, block][:], root[:], root[:], MULT)
@@ -340,30 +344,30 @@ def tile_list_saccade_divisive_inhibition_kernel(
         make_gain(1, 1, nc.gpsimd, LAST_BF)
         for j0 in range(0, HALF, P):
             excite(0, j0)
+        make_root(0, 2)
+        make_root(0, 3)
+        make_gain(0, 2)
         inhibit(1, 2)
         load_read_out()
-        make_root(0, 2)
-        make_root(1, 2)
-        make_gain(0, 2)
-        make_root(0, 3)
         make_root(1, 3)
-        make_gain(0, 3)
+        make_root(1, 2, 2)
+        make_gain(1, 2, parts=2)
         excite(1, 0)
         quantize_h(0, 0, HALF)
-        make_gain(1, 2, nc.gpsimd, EARLY_H)
+        make_gain(0, 3, nc.gpsimd, EARLY_H)
         for j0 in range(P, HALF, P):
             excite(1, j0)
         excite(0, 4 * P)
         excite(0, 5 * P)
         quantize_h(1, 0, HALF)
         make_gain(1, 3, nc.gpsimd, EARLY_H + 8 * HALF)
-        excite(1, 4 * P)
-        excite(1, 5 * P)
         excite(0, 6 * P)
         excite(0, 7 * P)
         read_out(0, HALF, psum_i, "bank_i", True)
-        quantize_h(1, HALF, BLOCK)
+        excite(1, 4 * P)
+        excite(1, 5 * P)
         quantize_h(0, HALF, HALF)
+        quantize_h(1, HALF, BLOCK)
         read_out(HALF, BLOCK, psum_i, "bank_i")
         excite(1, 6 * P)
         excite(1, 7 * P)

@@ -130,22 +130,26 @@ def tile_list_saccade_divisive_inhibition_kernel(
         we_codes = {}
         we_planes = {}
 
-        def round_we(b, a, part=0):
-            if part == 0:
+        def round_we(b, a, pairs=slice(0, 2)):
+            if pairs.start == 0:
                 if (b, a) == (1, 1):
                     we_bf[b, a] = stage.tile([P, 4 * PASS], BF16, name="we_bf11", offset=LAST_BF, align_bytes=64)
                 else:
                     we_bf[b, a] = keep.tile([P, 4 * PASS], BF16, name="we_bf%d%d" % (b, a), align_bytes=64)
-            m0, count, raw = we_raw[b, a][part]
+            m0, count, raw = we_raw[b, a][0]
             nc.vector.tensor_copy(
-                we_bf[b, a][:].rearrange("p (tp s m q) -> p m tp q s", tp=2, s=2, q=4)[:, m0 : m0 + count],
-                raw[:].rearrange("p q (m tp s) -> p m tp q s", tp=2, s=2),
+                we_bf[b, a][:].rearrange("p (tp s m q) -> p m tp q s", tp=2, s=2, q=4)[:, m0 : m0 + count, pairs],
+                raw[:].rearrange("p q (m tp s) -> p m tp q s", tp=2, s=2)[:, :, pairs],
             )
 
-        def quantize_we(b, a):
+        def quantize_we(b, a, parts=1):
             codes = keep.tile([P, PASS], U32, name="we_codes%d%d" % (b, a), align_bytes=64)
             plane = keep.tile([P, PASS], U8, name="we_plane%d%d" % (b, a), align_bytes=64)
-            nc.vector.quantize_mx(codes[:].bitcast(FP8X4), plane[:], we_bf[b, a][:])
+            n = PASS // parts
+            for o in range(0, PASS, n):
+                nc.vector.quantize_mx(
+                    codes[:, o : o + n].bitcast(FP8X4), plane[:, o : o + n], we_bf[b, a][:, 4 * o : 4 * (o + n)]
+                )
             we_codes[b, a] = codes
             we_planes[b, a] = plane
 
@@ -182,8 +186,8 @@ def tile_list_saccade_divisive_inhibition_kernel(
             n = BLOCK // parts
             for o in range(0, BLOCK, n):
                 nc.scalar.activation(
-                    roots[b, block][:, 4 * o : 4 * (o + n)].rearrange("p (g t x) -> p g t x", t=4, x=4),
-                    mags[b, run][:, :, first + o : first + o + n].rearrange("p t (g x) -> p g t x", x=4),
+                    roots[b, block][:, 4 * o : 4 * (o + n)].rearrange("p (g t x) -> p g t x", t=4, x=2),
+                    mags[b, run][:, :, first + o : first + o + n].rearrange("p t (g x) -> p g t x", x=2),
                     ACT.Abs_reciprocal_sqrt,
                     bias=1.0,
                 )
@@ -223,9 +227,9 @@ def tile_list_saccade_divisive_inhibition_kernel(
                     )
             block, o = divmod(j0, BLOCK)
             nc.vector.tensor_tensor(
-                h_bf[b, j0 // HALF][:, 4 * (j0 % HALF) : 4 * (j0 % HALF + P)].rearrange("p (g x t) -> p g t x", t=4, x=4),
-                bank[:].rearrange("p t (g x) -> p g t x", x=4),
-                gains[b, block][:, 4 * o : 4 * (o + P)].rearrange("p (g t x) -> p g t x", t=4, x=4),
+                h_bf[b, j0 // HALF][:, 4 * (j0 % HALF) : 4 * (j0 % HALF + P)].rearrange("p (g x t) -> p g t x", t=4, x=2),
+                bank[:].rearrange("p t (g x) -> p g t x", x=2),
+                gains[b, block][:, 4 * o : 4 * (o + P)].rearrange("p (g t x) -> p g t x", t=4, x=2),
                 MULT,
             )
 
@@ -338,9 +342,10 @@ def tile_list_saccade_divisive_inhibition_kernel(
         make_root(1, 1)
         make_gain(1, 0)
         round_we(1, 0)
-        round_we(1, 1)
         quantize_we(1, 0)
-        quantize_we(1, 1)
+        round_we(1, 1, slice(0, 1))
+        round_we(1, 1, slice(1, 2))
+        quantize_we(1, 1, 2)
         make_gain(1, 1, nc.gpsimd, LAST_BF)
         for j0 in range(0, HALF, P):
             excite(0, j0)

@@ -192,7 +192,7 @@ def tile_list_saccade_divisive_inhibition_kernel(
                     bias=1.0,
                 )
 
-        def make_gain(b, block, engine=None, offset=None, parts=1):
+        def make_gain(b, block, engine=None, offset=None, parts=1, last=4 * BLOCK):
             root = roots[b, block]
             name = "gain%d%d" % (b, block)
             if engine is None:
@@ -202,7 +202,7 @@ def tile_list_saccade_divisive_inhibition_kernel(
                     nc.scalar.activation(gains[b, block][:, o : o + n], root[:, o : o + n], ACT.Square)
             else:
                 gains[b, block] = stage.tile([P, 4 * BLOCK], F32, name=name, offset=offset, align_bytes=64)
-                engine.tensor_tensor(gains[b, block][:], root[:], root[:], MULT)
+                engine.tensor_tensor(gains[b, block][:, 0:last], root[:, 0:last], root[:, 0:last], MULT)
 
         h_bf = {}
         for b in range(2):
@@ -257,7 +257,7 @@ def tile_list_saccade_divisive_inhibition_kernel(
             wo["planes"] = wo_planes
             wo["bias"] = bias
 
-        def read_out(first, n, pool, tag, share=False):
+        def read_out(first, n, pool, tag, on_vector=None):
             cols = slice(first, first + n)
             result = keep.tile([P, 2, n], F32, name="result%d" % first)
             for c in range(2):
@@ -272,7 +272,7 @@ def tile_list_saccade_divisive_inhibition_kernel(
                         start=(b == 0),
                         stop=(b == 1),
                     )
-                if c == 1 and share:
+                if c == on_vector:
                     nc.vector.tensor_scalar_add(result[:, c, :], bank[:], wo["bias"][:, c : c + 1])
                 else:
                     nc.scalar.activation(result[:, c, :], bank[:], ACT.Identity, bias=wo["bias"][:, c : c + 1])
@@ -335,12 +335,13 @@ def tile_list_saccade_divisive_inhibition_kernel(
         quantize_we(0, 0)
         make_gain(0, 0, nc.vector, FIRST + QUARTER // 2 + 64)
         round_we(0, 1)
-        make_gain(0, 1, nc.vector, SECOND)
+        make_gain(0, 1, nc.vector, SECOND, last=HALF)
         quantize_we(0, 1)
         inhibit(0, 2)
-        make_root(1, 0)
+        nc.scalar.activation(gains[0, 1][:, HALF:], roots[0, 1][:, HALF:], ACT.Square)
         make_root(1, 1)
-        make_gain(1, 0)
+        make_root(1, 0)
+        make_gain(1, 0, parts=2)
         round_we(1, 0)
         quantize_we(1, 0)
         round_we(1, 1, slice(0, 1))
@@ -368,7 +369,7 @@ def tile_list_saccade_divisive_inhibition_kernel(
         make_gain(1, 3, nc.gpsimd, EARLY_H + 8 * HALF)
         excite(0, 6 * P)
         excite(0, 7 * P)
-        read_out(0, HALF, psum_i, "bank_i", True)
+        read_out(0, HALF, psum_i, "bank_i", 0)
         excite(1, 4 * P)
         excite(1, 5 * P)
         quantize_h(0, HALF, HALF)
@@ -378,5 +379,5 @@ def tile_list_saccade_divisive_inhibition_kernel(
         excite(1, 7 * P)
         quantize_h(1, 6 * P, P)
         quantize_h(1, 7 * P, P)
-        read_out(6 * P, P, psum_e, "bank_e", True)
-        read_out(7 * P, P, psum_e, "bank_e", True)
+        read_out(6 * P, P, psum_e, "bank_e", 1)
+        read_out(7 * P, P, psum_e, "bank_e", 1)

@@ -157,7 +157,8 @@ def tile_list_saccade_divisive_inhibition_kernel(
 
         def inhibit(b, run):
             j0, n = RUNS[run]
-            mags[b, run] = keep.tile([P, 4, n], F32, name="mag%d%d" % (b, run))
+            mags[b, run] = keep.tile([P, 4 * n], F32, name="mag%d%d" % (b, run))
+            grouped = mags[b, run][:].rearrange("p (g t x) -> p t g x", t=4, x=4)
             per_bank = PASS // n
             for t0 in range(0, 4, per_bank):
                 bank = psum_i.tile([P, per_bank, n], F32, name="bank_i", tag="bank_i")
@@ -174,7 +175,9 @@ def tile_list_saccade_divisive_inhibition_kernel(
                             start=(a == 0),
                             stop=(a == 1),
                         )
-                nc.scalar.activation(mags[b, run][:, t0 : t0 + per_bank, :], bank[:], ACT.Abs)
+                nc.scalar.activation(
+                    grouped[:, t0 : t0 + per_bank], bank[:].rearrange("p t (g x) -> p t g x", x=4), ACT.Abs
+                )
 
         roots = {}
         gains = {}
@@ -186,8 +189,8 @@ def tile_list_saccade_divisive_inhibition_kernel(
             n = BLOCK // parts
             for o in range(0, BLOCK, n):
                 nc.scalar.activation(
-                    roots[b, block][:, 4 * o : 4 * (o + n)].rearrange("p (g t x) -> p g t x", t=4, x=2),
-                    mags[b, run][:, :, first + o : first + o + n].rearrange("p t (g x) -> p g t x", x=2),
+                    roots[b, block][:, 4 * o : 4 * (o + n)],
+                    mags[b, run][:, 4 * (first + o) : 4 * (first + o + n)],
                     ACT.Abs_reciprocal_sqrt,
                     bias=1.0,
                 )
@@ -227,9 +230,9 @@ def tile_list_saccade_divisive_inhibition_kernel(
                     )
             block, o = divmod(j0, BLOCK)
             nc.vector.tensor_tensor(
-                h_bf[b, j0 // HALF][:, 4 * (j0 % HALF) : 4 * (j0 % HALF + P)].rearrange("p (g x t) -> p g t x", t=4, x=2),
-                bank[:].rearrange("p t (g x) -> p g t x", x=2),
-                gains[b, block][:, 4 * o : 4 * (o + P)].rearrange("p (g t x) -> p g t x", t=4, x=2),
+                h_bf[b, j0 // HALF][:, 4 * (j0 % HALF) : 4 * (j0 % HALF + P)].rearrange("p (g x t) -> p g t x", t=4, x=4),
+                bank[:].rearrange("p t (g x) -> p g t x", x=4),
+                gains[b, block][:, 4 * o : 4 * (o + P)].rearrange("p (g t x) -> p g t x", t=4, x=4),
                 MULT,
             )
 

from contextlib import ExitStack

import concourse.mybir as mybir

K, T, S, H, N = 1024, 2048, 1024, 1024, 256
FLOPS = 2 * K * H * S * 2 + 2 * H * N * S

F32 = mybir.dt.float32
BF16 = mybir.dt.bfloat16
I32 = mybir.dt.int32
U32 = mybir.dt.uint32
U16 = mybir.dt.uint16
U8 = mybir.dt.uint8
FP8X4 = mybir.dt.float8_e4m3fn_x4
FP4X4 = mybir.dt.float4_e2m1fn_x4
ACT = mybir.ActivationFunctionType
MULT = mybir.AluOpType.mult

P = 128
PASS = 512
BLOCK = 256
RUNS = ((0, BLOCK), (BLOCK, BLOCK), (2 * BLOCK, 2 * BLOCK))
WARM_PASSES = 4
QUARTER = 4 * 4 * PASS
HALF = S // 2
FIRST = 0
SECOND = FIRST + QUARTER + PASS
PAIRS = SECOND + 3 * QUARTER
LAST_BF = PAIRS + 9 * HALF
EARLY_H = SECOND + 2 * QUARTER


def tile_list_saccade_divisive_inhibition_kernel(
    tc, tab, offs, we, wi_words, wi_scales, wo_words, wo_scales, bo, out
):
    nc = tc.nc
    with ExitStack() as ctx:
        keep = ctx.enter_context(tc.tile_pool(name="keep", bufs=1))
        stage = ctx.enter_context(tc.tile_pool(name="stage", bufs=1))
        psum_i = ctx.enter_context(tc.psum_pool(name="psum_i", bufs=4))
        psum_e = ctx.enter_context(tc.psum_pool(name="psum_e", bufs=4))

        offsets = keep.tile([P, S // 16], U16, name="offsets")
        wi_rows = stage.tile([P, PASS], U8, name="wi_rows", offset=FIRST + QUARTER - BLOCK, align_bytes=64)
        tab_rows = stage.tile([P, T], U8, name="tab_rows", offset=SECOND + QUARTER - T // 2, align_bytes=64)
        rows = keep.tile([P, PASS + HALF], U8, name="rows", align_bytes=64)
        planes = [keep.tile([P, 2, PASS + HALF], U8, name="planes%d" % b, align_bytes=64) for b in range(2)]
        wi_raw = [
            stage.tile([P, 2, 2 * PASS], U8, name="wi_raw%d" % b, offset=SECOND + 2 * QUARTER + 4 * PASS * b, align_bytes=64)
            for b in range(2)
        ]
        wi_codes = [keep.tile([P, 2, 2 * PASS], U8, name="wi_codes%d" % b, align_bytes=64) for b in range(2)]
        tab_words = keep.tile([P, T], I32, name="tab_words", align_bytes=64)
        warm = keep.tile([P, 1], F32, name="warm")
        warm_out = keep.tile([P, 1], F32, name="warm_out")

        tab_scales = tab[0, PASS * T : (PASS + 32) * T].rearrange("(a n x) -> n a x", a=2, n=16).bitcast(I32)
        for b in range(2):
            nc.sync.dma_start(tab_rows[32 * b : 32 * (b + 1), :].bitcast(I32), tab_scales)
        nc.sync.dma_start(offsets[:], offs)
        for b in range(2):
            nc.sync.dma_start(
                wi_rows[32 * b : 32 * (b + 1), :].bitcast(I32),
                wi_scales[:, :, PASS * b : PASS * (b + 1)].rearrange("a n c -> n a c").bitcast(I32),
            )
        nc.sync.dma_start(tab_words[:], tab[0, 0 : PASS * T].rearrange("(p x) -> p x", p=P).bitcast(I32))
        for b in range(2):
            nc.sync.dma_start(
                wi_raw[b][:].bitcast(I32),
                wi_words[:, :, 2 * PASS * b : 2 * PASS * (b + 1)].rearrange("a p x -> p a x").bitcast(I32),
            )

        nc.vector.memset(warm[:], 0.0)
        nc.vector.memset(tab_rows[64:P, :].bitcast(I32), 0)
        nc.vector.memset(wi_rows[64:P, :].bitcast(I32), 0)
        for b in range(2):
            nc.gpsimd.memset(planes[b][:].bitcast(I32), 0)
        nc.scalar.activation(warm_out[:], warm[:], ACT.Abs_reciprocal_sqrt, bias=1.0)

        def move_rows(b):
            for quad in range(4):
                first = 32 * b + 8 * quad
                nc.sync.dma_start(planes[b][32 * quad : 32 * quad + 4].bitcast(I32), rows[first : first + 8, :].bitcast(I32))

        def order_wi_words(b):
            nc.scalar.copy(
                wi_codes[b][:].bitcast(U16).rearrange("p a (t m) -> p a t m", t=4),
                wi_raw[b][:].bitcast(U16).rearrange("p a (m t) -> p a t m", t=4),
            )

        we_raw = {}

        def load_we(b, a, offset, c0=0, width=PASS):
            area = stage.tile([P, 4, width], F32, name="we_raw%d%d_%d" % (b, a, c0), offset=offset, align_bytes=64)
            first = PASS * b + c0
            nc.sync.dma_start(
                area[:], we[PASS * a : PASS * (a + 1), first : first + width].rearrange("(p q) c -> p q c", q=4)
            )
            we_raw.setdefault((b, a), []).append((c0 // 4, width // 4, area))

        v_pairs = {}
        v_codes = {}

        def gather_words(run):
            j0, n = RUNS[run]
            where = PAIRS + (5 * HALF, 7 * HALF, HALF - P)[run]
            v_pairs[run] = stage.tile([P, n], U32, name="v_pairs%d" % run, offset=where, align_bytes=64)
            nc.vector.tensor_copy(
                v_pairs[run][:], tab_words[:].bitcast(U32).indirect(offsets[:, j0 // 16 : (j0 + n) // 16])
            )

        def part_words(run):
            n = RUNS[run][1]
            if run == 2:
                v_codes[run] = stage.tile([P, 2, 2 * n], U8, name="v_codes2", offset=FIRST, align_bytes=64)
            else:
                v_codes[run] = keep.tile([P, 2, 2 * n], U8, name="v_codes%d" % run, align_bytes=64)
            nc.vector.tensor_copy(
                v_codes[run][:].bitcast(U16), v_pairs[run][:].bitcast(U16).rearrange("p (j a) -> p a j", a=2)
            )

        def v_operand(a, j0, n):
            run = min(j0 // BLOCK, 2)
            o = j0 - RUNS[run][0]
            words = v_codes[run][:, a, 2 * o : 2 * (o + n)].bitcast(FP4X4)
            half, o = divmod(j0, HALF)
            return words, planes[half][:, a, PASS + o : PASS + o + n]

        we_bf = {}
        we_codes = {}
        we_planes = {}

        def round_we(b, a, pairs=slice(0, 2)):
            if pairs.start == 0:
                if (b, a) == (1, 1):
                    we_bf[b, a] = stage.tile([P, 4 * PASS], BF16, name="we_bf11", offset=LAST_BF, align_bytes=64)
                else:
                    we_bf[b, a] = keep.tile([P, 4 * PASS], BF16, name="we_bf%d%d" % (b, a), align_bytes=64)
            m0, count, raw = we_raw[b, a][0]
            nc.vector.tensor_copy(
                we_bf[b, a][:].rearrange("p (tp s m q) -> p m tp q s", tp=2, s=2, q=4)[:, m0 : m0 + count, pairs],
                raw[:].rearrange("p q (m tp s) -> p m tp q s", tp=2, s=2)[:, :, pairs],
            )

        def quantize_we(b, a, parts=1):
            codes = keep.tile([P, PASS], U32, name="we_codes%d%d" % (b, a), align_bytes=64)
            plane = keep.tile([P, PASS], U8, name="we_plane%d%d" % (b, a), align_bytes=64)
            n = PASS // parts
            for o in range(0, PASS, n):
                nc.vector.quantize_mx(
                    codes[:, o : o + n].bitcast(FP8X4), plane[:, o : o + n], we_bf[b, a][:, 4 * o : 4 * (o + n)]
                )
            we_codes[b, a] = codes
            we_planes[b, a] = plane

        mags = {}

        def inhibit(b, run):
            j0, n = RUNS[run]
            mags[b, run] = keep.tile([P, 4 * n], F32, name="mag%d%d" % (b, run))
            grouped = mags[b, run][:].rearrange("p (g t x) -> p t g x", t=4, x=4)
            per_bank = PASS // n
            for t0 in range(0, 4, per_bank):
                bank = psum_i.tile([P, per_bank, n], F32, name="bank_i", tag="bank_i")
                for s in range(per_bank):
                    t = t0 + s
                    for a in range(2):
                        rhs, rhs_scale = v_operand(a, j0, n)
                        nc.tensor.matmul_mx(
                            out=bank[:, s, :],
                            lhsT=wi_codes[b][:, a, 2 * P * t : 2 * P * (t + 1)].bitcast(FP4X4),
                            lhsT_scale=planes[b][:, a, P * t : P * (t + 1)],
                            rhs=rhs,
                            rhs_scale=rhs_scale,
                            start=(a == 0),
                            stop=(a == 1),
                        )
                nc.scalar.activation(
                    grouped[:, t0 : t0 + per_bank], bank[:].rearrange("p t (g x) -> p t g x", x=4), ACT.Abs
                )

        roots = {}
        gains = {}

        def make_root(b, block, parts=1):
            run = min(block, 2)
            first = BLOCK * block - RUNS[run][0]
            roots[b, block] = keep.tile([P, 4 * BLOCK], F32, name="root%d%d" % (b, block))
            n = BLOCK // parts
            for o in range(0, BLOCK, n):
                nc.scalar.activation(
                    roots[b, block][:, 4 * o : 4 * (o + n)],
                    mags[b, run][:, 4 * (first + o) : 4 * (first + o + n)],
                    ACT.Abs_reciprocal_sqrt,
                    bias=1.0,
                )

        def make_gain(b, block, engine=None, offset=None, parts=1, last=4 * BLOCK):
            root = roots[b, block]
            name = "gain%d%d" % (b, block)
            if engine is None:
                gains[b, block] = keep.tile([P, 4 * BLOCK], F32, name=name)
                n = 4 * BLOCK // parts
                for o in range(0, 4 * BLOCK, n):
                    nc.scalar.activation(gains[b, block][:, o : o + n], root[:, o : o + n], ACT.Square)
            else:
                gains[b, block] = stage.tile([P, 4 * BLOCK], F32, name=name, offset=offset, align_bytes=64)
                engine.tensor_tensor(gains[b, block][:, 0:last], root[:, 0:last], root[:, 0:last], MULT)

        h_bf = {}
        for b in range(2):
            h_bf[b, 0] = stage.tile([P, 4 * HALF], BF16, name="h_bf%d0" % b, offset=EARLY_H + 8 * HALF * b, align_bytes=64)
            h_bf[b, 1] = keep.tile([P, 4 * HALF], BF16, name="h_bf%d1" % b, align_bytes=64)
        h_codes = [keep.tile([P, S], U32, name="h_codes%d" % b, align_bytes=64) for b in range(2)]
        h_planes = [keep.tile([P, S], U8, name="h_planes%d" % b, align_bytes=64) for b in range(2)]

        def excite(b, j0):
            bank = psum_e.tile([P, 4, P], F32, name="bank_e", tag="bank_e")
            for t in range(4):
                for a in range(2):
                    rhs, rhs_scale = v_operand(a, j0, P)
                    nc.tensor.matmul_mx(
                        out=bank[:, t, :],
                        lhsT=we_codes[b, a][:, P * t : P * (t + 1)].bitcast(FP8X4),
                        lhsT_scale=we_planes[b, a][:, P * t : P * (t + 1)],
                        rhs=rhs,
                        rhs_scale=rhs_scale,
                        start=(a == 0),
                        stop=(a == 1),
                    )
            block, o = divmod(j0, BLOCK)
            nc.vector.tensor_tensor(
                h_bf[b, j0 // HALF][:, 4 * (j0 % HALF) : 4 * (j0 % HALF + P)].rearrange("p (g x t) -> p g t x", t=4, x=4),
                bank[:].rearrange("p t (g x) -> p g t x", x=4),
                gains[b, block][:, 4 * o : 4 * (o + P)].rearrange("p (g t x) -> p g t x", t=4, x=4),
                MULT,
            )

        def quantize_h(b, j0, n):
            cols = slice(j0, j0 + n)
            nc.vector.quantize_mx(
                h_codes[b][:, cols].bitcast(FP8X4),
                h_planes[b][:, cols],
                h_bf[b, j0 // HALF][:, 4 * (j0 % HALF) : 4 * (j0 % HALF + n)],
            )

        wo = {}

        def load_read_out():
            codes = stage.tile([P, 2, N], I32, name="wo_codes", offset=FIRST + QUARTER // 4, align_bytes=64)
            bias = stage.tile([P, 2], F32, name="bias", offset=FIRST + QUARTER // 2, align_bytes=64)
            wo_planes = planes[0][:, :, 0:N]
            nc.sync.dma_start(codes[:], wo_words.rearrange("a p c q -> p a (c q)").bitcast(I32))
            wo_rows = wo_scales.rearrange("a s c -> s a c").bitcast(I32)
            for quad in range(4):
                nc.sync.dma_start(wo_planes[32 * quad : 32 * quad + 4].bitcast(I32), wo_rows[4 * quad : 4 * quad + 4])
            with nc.allow_non_contiguous_dma(reason="one bias value a partition"):
                nc.sync.dma_start(bias[:], bo.rearrange("(c p) -> p c", p=P))
            wo["codes"] = codes
            wo["planes"] = wo_planes
            wo["bias"] = bias

        def read_out(first, n, pool, tag, on_vector=None):
            cols = slice(first, first + n)
            result = keep.tile([P, 2, n], F32, name="result%d" % first)
            for c in range(2):
                bank = pool.tile([P, n], F32, name="bank_y", tag=tag)
                for b in range(2):
                    nc.tensor.matmul_mx(
                        out=bank[:],
                        lhsT=wo["codes"][:, b, P * c : P * (c + 1)].bitcast(FP8X4),
                        lhsT_scale=wo["planes"][:, b, P * c : P * (c + 1)],
                        rhs=h_codes[b][:, cols].bitcast(FP8X4),
                        rhs_scale=h_planes[b][:, cols],
                        start=(b == 0),
                        stop=(b == 1),
                    )
                if c == on_vector:
                    nc.vector.tensor_scalar_add(result[:, c, :], bank[:], wo["bias"][:, c : c + 1])
                else:
                    nc.scalar.activation(result[:, c, :], bank[:], ACT.Identity, bias=wo["bias"][:, c : c + 1])
                if n > BLOCK:
                    nc.sync.dma_start(out[P * c : P * (c + 1), cols], result[:, c, :])
            if n <= BLOCK:
                nc.sync.dma_start(out[:, cols].rearrange("(c p) j -> p c j", p=P), result[:])

        first_rows = stage.tile([P, HALF], U8, name="first_rows", offset=FIRST, align_bytes=64)
        nc.vector.tensor_copy(first_rows[:], tab_rows[:].indirect(offsets[:, 0 : HALF // 16]))
        nc.vector.tensor_copy(
            rows[:, 0:PASS].rearrange("p (t m) -> p t m", t=4), wi_rows[:].rearrange("p (m t) -> p t m", t=4)
        )
        nc.vector.tensor_copy(rows[:, PASS:], first_rows[:])
        move_rows(0)
        load_we(0, 0, FIRST)
        order_wi_words(0)
        warm_bank = psum_e.tile([P, PASS], F32, name="warm_bank", tag="bank_e")
        for step in range(WARM_PASSES):
            nc.tensor.matmul_mx(
                out=warm_bank[:, 0:BLOCK],
                lhsT=rows[:, 0 : 2 * P].bitcast(FP4X4),
                lhsT_scale=rows[:, 0:P],
                rhs=rows[:, 0 : 2 * BLOCK].bitcast(FP4X4),
                rhs_scale=rows[:, 0:BLOCK],
                start=True,
                stop=True,
            )
        for step in range(WARM_PASSES // 2):
            nc.tensor.matmul_mx(
                out=warm_bank[:],
                lhsT=wi_raw[0][:, 0, 0 : 2 * P].bitcast(FP4X4),
                lhsT_scale=rows[:, 0:P],
                rhs=wi_raw[0][:, 0, :].bitcast(FP4X4),
                rhs_scale=rows[:, 0:PASS],
                start=True,
                stop=True,
            )
        gather_words(0)
        gather_words(1)
        part_words(0)
        part_words(1)
        late_rows = stage.tile([P, HALF], U8, name="late_rows", offset=PAIRS + 4 * HALF + HALF // 2, align_bytes=64)
        nc.vector.tensor_copy(late_rows[:], tab_rows[:].indirect(offsets[:, HALF // 16 : S // 16]))
        nc.vector.tensor_copy(rows[32:64, PASS:].bitcast(I32), late_rows[32:64, :].bitcast(I32))
        move_rows(1)
        load_we(0, 1, SECOND)
        load_we(1, 0, SECOND + QUARTER)
        inhibit(0, 0)
        order_wi_words(1)
        load_we(1, 1, SECOND + 2 * QUARTER)
        inhibit(0, 1)
        gather_words(2)
        make_root(0, 0)
        make_root(0, 1)
        inhibit(1, 0)
        inhibit(1, 1)
        round_we(0, 0)
        part_words(2)
        quantize_we(0, 0)
        make_gain(0, 0, nc.vector, FIRST + QUARTER // 2 + 64)
        round_we(0, 1)
        make_gain(0, 1, nc.vector, SECOND, last=HALF)
        quantize_we(0, 1)
        inhibit(0, 2)
        nc.scalar.activation(gains[0, 1][:, HALF:], roots[0, 1][:, HALF:], ACT.Square)
        make_root(1, 1)
        make_root(1, 0)
        make_gain(1, 0, parts=2)
        round_we(1, 0)
        quantize_we(1, 0)
        round_we(1, 1, slice(0, 1))
        round_we(1, 1, slice(1, 2))
        quantize_we(1, 1, 2)
        make_gain(1, 1, nc.gpsimd, LAST_BF)
        for j0 in range(0, HALF, P):
            excite(0, j0)
        make_root(0, 2)
        make_root(0, 3)
        make_gain(0, 2)
        inhibit(1, 2)
        load_read_out()
        make_root(1, 3)
        make_root(1, 2, 2)
        make_gain(1, 2, parts=2)
        excite(1, 0)
        quantize_h(0, 0, HALF)
        make_gain(0, 3, nc.gpsimd, EARLY_H)
        for j0 in range(P, HALF, P):
            excite(1, j0)
        excite(0, 4 * P)
        excite(0, 5 * P)
        quantize_h(1, 0, HALF)
        make_gain(1, 3, nc.gpsimd, EARLY_H + 8 * HALF)
        excite(0, 6 * P)
        excite(0, 7 * P)
        read_out(0, HALF, psum_i, "bank_i", 0)
        excite(1, 4 * P)
        excite(1, 5 * P)
        quantize_h(0, HALF, HALF)
        quantize_h(1, HALF, BLOCK)
        read_out(HALF, BLOCK, psum_i, "bank_i")
        excite(1, 6 * P)
        excite(1, 7 * P)
        quantize_h(1, 6 * P, P)
        quantize_h(1, 7 * P, P)
        read_out(6 * P, P, psum_e, "bank_e", 1)
        read_out(7 * P, P, psum_e, "bank_e", 1)
